import numpy as np, ml_dtypes
CORES = [2,3,42,43,82,83,122,123]
N = 8
BF = ml_dtypes.bfloat16
S, U, NP, CAP, FO, RO = 2048, 4096, 256, 64, 2, 4
G = NP + FO * CAP
def parts(rng):
    x = rng.integers(0, 256, (N, 8, 16, S)); kd = rng.integers(0, 4096, (N, 16, U)); wt = rng.integers(0, 256, (N, 8, 16, 1))
    th = rng.integers(64, 208, (N, 8, 16, 1)); th = np.where(rng.random(th.shape) < 0.06, 256 * rng.integers(0, 2, th.shape), th)
    tau = rng.integers(900, 1700, (N, 8, 1, 1)) + rng.integers(-150, 151, (N, 8, 16, 1))
    return x, kd, wt, th, tau
def pack(x, kd, wt, th, tau):
    col = lambda a: np.ascontiguousarray(a.reshape(N, 128, 1)).astype(np.int32)
    return {"x0": np.ascontiguousarray(x.reshape(N, 128, S)).astype(np.float32).astype(BF), "kd": kd.astype(np.int32), "wt": col(wt), "th": col(th), "tau": col(tau)}
def draw_of(a):
    return (a * 4096 + S - 1) // S
def apart(rng, n):
    got = []; used = {0}
    for d in rng.permutation(np.arange(64, 4096 * S // (S + (RO - 1) * G))):
        v = {int(d) * (S + t * G) >> 12 for t in range(RO)}
        if len(v) == RO and not v & used:
            got.append(int(d)); used |= v
        if len(got) == n: break
    return np.array(got)
def columns_of(rng, h):
    z = h[:, None, :] // 16 + (np.arange(16)[None, :, None] < h[:, None, :] % 16)
    a, b = z[:, ::2], z[:, 1::2]; s = rng.integers(0, np.minimum(a, 255 - b) + 1); z = np.concatenate([a - s, b + s], axis=1)
    return np.take_along_axis(z, np.argsort(rng.random(z.shape), axis=1), 1)
def setup_inputs(rng):
    return pack(*parts(rng))
def setup_inputs_corners(rng):
    x, kd, wt, th, tau = parts(rng)
    kd = np.where(rng.random(kd.shape) < 0.3, 4095 * rng.integers(0, 2, kd.shape), kd); ui = (613 * np.arange(NP)) & (U - 1)
    for a in range(N):
        o = 2 + rng.permutation(S - 2); o = np.concatenate([[0], o[:NP - 1], [1], o[NP - 1:]]); p, q = o[:NP], o[NP:2 * NP]
        first = rng.random((16, NP)) < 0.5; first[0] = True; first[15] = False
        kd[a][:, ui] = draw_of(np.where(first, p[None, :], q[None, :]))
        cnt = rng.permutation(np.array([0, 1, CAP - 1, CAP, CAP + 1, NP]))
        for g in range(6):
            m = rng.permutation(NP)[:int(cnt[g])]
            wt[a, g] = 0; th[a, g] = 256 * rng.integers(0, 2, (16, 1)); th[a, g, 0] = 0
            tau[a, g] = rng.choice(np.array([0, 1, 1000, 1500, 4079, 4080]), (16, 1)); tau[a, g, 0] = 4079
            x[a, g][:, q] = x[a, g][:, p]; x[a, g][:, p[m]] = 0; x[a, g][:, q[m]] = 255
        wt[a, 6] = 255; th[a, 6] = rng.choice(np.array([0, 1, 128, 255, 256]), (16, 1)); tau[a, 6] = rng.choice(np.array([0, 1300, 4080]), (16, 1))
        th[a, 7] = 256
    return pack(x, kd, wt, th, tau)
def setup_inputs_deep(rng):
    x, kd, wt, th, tau = parts(rng)
    near = 4095 - np.floor(300 * rng.random(kd.shape) ** 2).astype(np.int64)
    kd = np.where(rng.random(kd.shape) < 0.7, near, kd); th = rng.integers(90, 140, th.shape)
    tau = np.minimum(rng.choice(np.array([0, 300, 600, 900, 1200, 4080]), (N, 8, 1, 1)) + rng.integers(0, 200, (N, 8, 16, 1)), 4080)
    tau[:, 2] = 4080; tau[:, 5] = 0
    return pack(x, kd, wt, th, tau)
def setup_inputs_ends(rng):
    x = 255 * rng.integers(0, 2, (N, 8, 16, S)); x = np.where(rng.random((N, 8, 1, S)) < 0.4, 255 * rng.integers(0, 2, (N, 8, 1, S)), x)
    wt = 255 * rng.integers(0, 2, (N, 8, 16, 1)); sh = wt.shape
    th = np.where(rng.random(sh) < 0.75, 256 * rng.integers(0, 2, sh), rng.choice(np.array([1, 128, 255]), sh))
    tau = np.where(rng.random(sh) < 0.7, 4080 * rng.integers(0, 2, sh), 255 * rng.integers(0, 17, sh))
    end = (rng.random((N, 1, U)) < 0.5) | (rng.random((N, 16, U)) < 0.5)
    kd = np.where(end, 4095 * rng.integers(0, 2, (N, 16, U)), rng.integers(0, 4096, (N, 16, U)))
    bits = rng.integers(0, 2, (N, 1, S)); bits[..., 0] = 0; bits[..., S - 1] = 1; bits[..., S - G] = 1; bits[..., S - G + 1] = 0; bits[..., S - G + NP - 1] = 1
    x[:, 7] = 255 * bits; wt[:, 7] = 255
    th[:, 7] = 256 * rng.integers(0, 2, (N, 16, 1)); th[:, 7, 0] = 0; th[:, 7, 1] = 256; th[:, 7, 14] = 0; th[:, 7, 15] = 0
    tau[:, 7] = 4080 * rng.integers(0, 2, (N, 16, 1)); tau[:, 7, 0] = 4080; tau[:, 7, 14] = 4080; tau[:, 7, 15] = 0
    i = 613 * np.arange(NP); both = np.unique(np.concatenate([i & (U - 1), (i + 16 * 255 * 255) & (U - 1)]))
    kd[:, :, both] = 4095 * rng.integers(0, 2, (N, 16, len(both))); kd[:, 1, both] = 4095; kd[:, 15, both] = 0; kd[:, 0, 0] = 0
    e = np.array([613 * (CAP - 1), 613 * (NP - 1)]); e = np.concatenate([e, e + 16 * 255 * 255]) & (U - 1)
    kd[:, :, e] = 4095; kd[:, 15, e] = 0; kd[:, 0, (e + 1) & (U - 1)] = 4095
    return pack(x, kd, wt, th, tau)
def setup_inputs_spread(rng):
    x, kd, wt, th, tau = parts(rng); sh = wt.shape
    x = np.minimum(np.floor(np.exp2(8 * rng.random((N, 8, 1, S))) * rng.random((N, 8, 16, S))), 255).astype(np.int64)
    kd = np.minimum(np.floor(4096 * rng.random((N, 16, U)) ** np.exp2(rng.integers(-2, 3, (N, 1, U)))), 4095).astype(np.int64)
    wt = np.minimum(np.floor(np.exp2(8 * rng.random(sh))) - 1, 255).astype(np.int64); wt[:, :, 3] = 255
    th = np.where(rng.random(sh) < 0.7, np.minimum(np.floor(np.exp2(8.01 * rng.random(sh))) - 1, 256), rng.integers(0, 257, sh)).astype(np.int64)
    tau = np.where(rng.random(sh) < 0.5, np.minimum(np.floor(np.exp2(12 * rng.random(sh))) - 1, 4080), rng.integers(200, 2200, sh)).astype(np.int64)
    return pack(x, kd, wt, th, tau)
def setup_inputs_turns(rng):
    x, kd, wt, th, tau = parts(rng); wt[...] = 0; ui = (613 * np.arange(NP)) & (U - 1); n = 20; tight = np.arange(n) % 2 == 0
    own = np.concatenate([np.arange(4), np.full(CAP - 2, 4), 5 + np.arange(NP - CAP - 2) % (n - 5)])
    pat = np.zeros((6, n), bool); pat[1, 0] = True; pat[2, [0, 4]] = True; pat[3, [0, 1, 4]] = True; pat[4, [0, 1, 2, 4]] = True; pat[5] = True
    q = rng.permutation(N)
    for a in range(N):
        d = apart(rng, n); c = rng.permutation(own); size = np.bincount(c, minlength=n)
        first = rng.random((16, NP)) < 0.5; first[0] = True; first[15] = False
        kd[a][:, ui] = np.where(first, d[c][None, :], 0)
        opt = rng.integers(0, 7, (RO, 8))
        if a == q[0]:
            opt[0] = rng.permutation(np.array([0, 1, 1, 1, 2, 3, 4, 5])); opt[1] = 0; opt[2] = rng.integers(1, 6, 8)
        if a == q[1]:
            opt[1] = 5; opt[2] = rng.integers(1, 6, 8)
        go = np.where((opt == 6)[..., None], rng.random((RO, 8, n)) < 0.5, pat[np.minimum(opt, 5)])
        least = rng.permutation(np.concatenate([np.array([0, 64, 2047, 2048, 4064]), rng.integers(100, 4065, 3)])); row = rng.integers(0, 16, 8)
        th[a, :, :, 0] = rng.choice(np.array([0, 0, 1, 128, 255, 256]), (8, 16))
        tau[a, :, :, 0] = np.minimum(least[:, None] + rng.choice(np.array([0, 0, 1, 15, 500, 4080]), (8, 16)), 4080)
        th[a, np.arange(8), row, 0] = 0; tau[a, np.arange(8), row, 0] = least
        count = 0
        for t in range(RO):
            lim = (least + (count & 15))[:, None]; v = (d * (S + t * G)) >> 12
            over = np.where(tight, 1, 1 + np.floor((4080 - lim) * rng.random((8, n))).astype(np.int64))
            under = np.where(tight, 0, np.floor((lim + 1) * rng.random((8, n))).astype(np.int64))
            x[a][:, :, v] = columns_of(rng, np.where(go[t], lim + over, lim - under))
            count = int(np.sum(size * go[t]))
        x[a][:, :, 0] = 0
    return pack(x, kd, wt, th, tau)
def check_inputs(d):
    bad = []
    for k, lo, hi in (("x0", 0, 255), ("kd", 0, 4095), ("wt", 0, 255), ("th", 0, 256), ("tau", 0, 4080)):
        a = np.asarray(d[k]).astype(np.float64)
        if not (np.all(a >= lo) and np.all(a <= hi) and np.all(a == np.floor(a))): bad.append("range of " + k)
    return bad
def reference(x0, kd, wt, th, tau):
    tot = S + RO * G
    X = np.zeros((N, 8, 16, tot), np.int64); X[..., :S] = x0.astype(np.float32).astype(np.int64).reshape(N, 8, 16, S)
    A = np.zeros((N, 8, 16, tot), np.int64); A[...] = np.arange(tot)
    tb = kd.astype(np.int64); w = wt.astype(np.int64).reshape(N, 8, 16, 1); lim = tau.astype(np.int64).reshape(N, 8, 16, 1); thr = th.astype(np.int64).reshape(N, 8, 16, 1, 1)
    C = [0] * N
    for t in range(RO):
        B = S + t * G
        u = (np.sum(w * X[..., B - G:B - G + NP], axis=2) + 613 * np.arange(NP)) & (U - 1)
        mail = []
        for a in range(N):
            e = (tb[a][:, u[a]] * B) >> 12
            ix = np.ascontiguousarray(e.transpose(1, 2, 0)).reshape(8, 1, NP * 16)
            xe = np.take_along_axis(X[a], ix, 2).reshape(8, 16, NP, 16); ne = np.take_along_axis(A[a], ix, 2).reshape(8, 16, NP, 16)
            m = xe >= thr[a]
            lo = np.min(np.where(m, ne, tot), axis=3); hi = np.max(np.where(m, ne, -1), axis=3); none = hi < 0
            lo = np.where(none, ne[..., 0], lo); hi = np.where(none, ne[..., 0], hi)
            xl = np.take_along_axis(X[a], lo.reshape(8, 1, 16 * NP), 2).reshape(8, 16, 16, NP)
            xh = np.take_along_axis(X[a], hi.reshape(8, 1, 16 * NP), 2).reshape(8, 16, 16, NP)
            D = np.sum(np.abs(xl - xh), axis=1)
            far = D > lim[a] + (C[a] & 15)
            A[a, :, :, B:B + NP] = np.where(far, np.arange(B, B + NP), lo)
            nx = (np.max(xl, axis=2) + np.min(xh, axis=2)) >> 1
            X[a, :, :, B:B + NP] = nx
            c = np.any(far, axis=1)
            C[a] = int(np.sum(c))
            o = np.argsort(np.where(c, 0, 1), axis=1, kind="stable")[:, :CAP]
            mail.append(np.where(np.take_along_axis(c, o, 1)[:, None, :], np.take_along_axis(nx, o[:, None, :], 2), 0))
        for a in range(N):
            for f in range(FO):
                q = (a - 1 - (FO * t + f) % (N - 1)) % N; b = B + NP + f * CAP
                X[a, :, :, b:b + CAP] = mail[q]
    return {"ya": A[..., S:].reshape(N, 128, RO * G).astype(np.float32), "yx": X[..., S:].reshape(N, 128, RO * G).astype(np.float32).astype(BF)}

@@ -1,0 +1,502 @@
+from concourse.bass import DstId, RemoteDMATransfer
+from concourse.mybir import AluOpType, ActivationFunctionType, AxisListType
+
+N, S, U, NP, CAP, FO, RO = 8, 2048, 4096, 256, 64, 2, 4
+G = NP + FO * CAP
+TOT = S + RO * G
+CH = [(0, 64), (64, 128), (128, 192), (192, 256)]
+UH = [(0, 256)]
+XHV, XLV = ((2, 0), (3, 0)), ()
+FUS = ((3, 1),)
+SUB = {3: [(0, 32), (32, 64)]}
+P = max(b - a for a, b in CH)
+E = 16 * P
+DEP = 4
+AHEAD = 4
+WAKE = 0.1
+GCY, TCY, MLAT = 1.6, 0.001, 3.0
+DELTA = 0.3
+BK = {'-:9': 5.2, 'ab:0': -6.2, 'ab:1': 3.1, 'ab:2': -7.5, 'ab:3': -5.7, 'ad:0': 8.1, 'ad:1': 5.0, 'ad:2': -6.5, 'ad:3': -6.8,
+      'ci:9': -1.5, 'cj:9': -7.0, 'df:3': -2.8, 'e:3': -8.2, 'fb:0': -4.8, 'fb:1': -4.7, 'fb:2': -4.3, 'fb:3': 6.5, 'fc:9': 6.6,
+      'hk:0': 13.4, 'hk:1': 5.9, 'hk:2': -9.1, 'hk:3': -9.8, 'hl:0': -5.7, 'hl:1': 3.6, 'hl:2': 1.2, 'hl:3': 3.7, 'hs:0': 5.6,
+      'hs:1': -9.0, 'hs:2': -2.7, 'hs:3': 2.3, 'kw:0': -7.4, 'kw:1': -3.7, 'kw:2': 4.7, 'kw:3': -4.6, 'kw:9': -1.7, 'lk:0': 7.2,
+      'lk:1': -7.2, 'lk:2': -3.5, 'lk:3': 2.4, 'lof:0': 2.1, 'lof:1': 8.7, 'lof:2': 2.0, 'lof:3': 10.4, 'ls:0': -2.6, 'ls:1': 10.8,
+      'ls:2': -8.2, 'ls:3': -8.5, 'mn:0': -6.4, 'mn:1': -4.8, 'mn:2': -7.1, 'mn:3': -3.1, 'ms:0': -5.5, 'ms:1': -3.6, 'ms:2': -3.8,
+      'ms:3': 7.7, 'mw:9': -4.1, 'nc:9': 4.0, 'no:0': -4.2, 'no:1': 2.4, 'no:2': 5.8, 'no:3': -0.4, 'nq:9': -2.0, 'off:9': -5.0,
+      'pd:0': 12.2, 'pd:1': 5.8, 'pd:2': -2.8, 'pd:3': -8.5, 'pl:0': 6.8, 'pl:1': 5.8, 'pl:2': 3.1, 'pl:3': -5.5, 'pm:9': 9.1, 'pq:0': 1.3,
+      'pq:1': 7.3, 'pq:2': -5.3, 'pq:3': -6.8, 'pw:0': -1.7, 'pw:1': -7.7, 'pw:2': -2.2, 'pw:3': -7.0, 'pw:7': -5.7, 'pw:9': -4.0,
+      'r:0': 10.9, 'r:1': 7.0, 'r:2': -5.4, 'r:3': -5.5, 'ui:3': -10.1, 'uj:3': -6.7, 'uo:3': -1.9, 'w:0': 0.4, 'w:1': 8.0, 'w:2': -2.9,
+      'w:3': 1.0, 'xb:0': 3.9, 'xb:1': 2.2, 'xb:2': -3.3, 'xb:3': -2.5, 'xb:9': -0.7, 'xh:0': -5.3, 'xh:1': -4.6, 'xh:2': -6.7,
+      'xh:3': -8.1, 'xl:0': 7.1, 'xl:1': 5.8, 'xl:2': -1.1, 'xl:3': -2.3, 'yf:3': 6.4}
+STATS = {}
+MAGIC = 12582912.0
+F16 = "float16"
+
+COLS = ["wtf", "thf", "ntau", "prf", "pixf", "cs", "iz0", "iz1", "nb0", "nb1", "nb2", "nb3"]
+
+SCRATCH = {
+    "xb": ("sbuf", [128, TOT], "bfloat16"),
+    "kw": ("sbuf", [128, TOT], "float32"),
+    "kdw": ("sbuf", [128, U], "int32"),
+    "ab": ("sbuf", [128, RO * G], "float32"),
+    "onesb": ("sbuf", [128, 512], "bfloat16"),
+    "io16": ("sbuf", [128, 512], F16),
+    "n8h": ("sbuf", [128, S], F16),
+    "rneg": ("sbuf", [128, E], "bfloat16"),
+    "rpos": ("sbuf", [128, E], "bfloat16"),
+    "g2a": ("sbuf", [128, 144], "bfloat16"),
+    "g2": ("sbuf", [128, 144], "bfloat16"),
+    "l1": ("sbuf", [128, 144], "bfloat16"),
+    "lw": ("sbuf", [128, 144], "bfloat16"),
+    "ib": ("sbuf", [128, 128], "bfloat16"),
+    "nib": ("sbuf", [128, 128], "bfloat16"),
+    "hib": ("sbuf", [128, 128], "bfloat16"),
+    "nif": ("sbuf", [128, 128], "float32"),
+    "ih": ("sbuf", [128, 128], F16),
+    "nih": ("sbuf", [128, 128], F16),
+    "i84h": ("sbuf", [128, 128], F16),
+    "c17": ("sbuf", [128, P], F16),
+    "cq": ("sbuf", [128, P], "bfloat16"),
+    "wti": ("sbuf", [128, 1], "int32"), "thi": ("sbuf", [128, 1], "int32"), "taui": ("sbuf", [128, 1], "int32"),
+    "fc": ("sbuf", [128, len(COLS)], "float32"),
+    "pix": ("sbuf", [128, 1], "int32"), "pr": ("sbuf", [128, 1], "int32"),
+    "c16": ("sbuf", [128, 16], "float32"), "icf": ("sbuf", [128, 16], "float32"),
+    "uc": ("sbuf", [128, 16], "float32"),
+    "ui": ("sbuf", [128, 16], "int32"), "uj": ("sbuf", [128, 16], "int32"), "uo": ("sbuf", [128, 16], "uint16"),
+    "am": ("sbuf", [128, 128], "bfloat16"), "qm": ("sbuf", [128, 128], "bfloat16"), "leq": ("sbuf", [128, 128], F16),
+    "bef": ("sbuf", [128, 8], "bfloat16"), "befh": ("sbuf", [128, 8], F16), "ich": ("sbuf", [128, 16], F16),
+    "onh": ("sbuf", [128, 128], F16), "nonh": ("sbuf", [128, 8], F16), "selh": ("sbuf", [128, 8], F16),
+    "pm": ("psum", [128, 512], "float32"),
+    "off": ("sbuf", [128, 16], "uint16"),
+    "ci": ("sbuf", [128, 1], "int32"), "cj": ("sbuf", [128, 1], "int32"),
+    "pl0": ("psum", [128, 512], "float32"), "pl1": ("psum", [128, 512], "float32"),
+    "pq": ("psum", [128, 512], "float32"), "pw": ("psum", [128, 512], "float32"),
+}
+for _b in range(2):
+    for _n in ("nc", "nq", "qz", "mz"):
+        SCRATCH["%s%d" % (_n, _b)] = ("sbuf", [128, 128], F16)
+    SCRATCH["df%d" % _b] = ("sbuf", [128, E], "bfloat16")
+    SCRATCH["yf%d" % _b] = ("sbuf", [128, NP], "float32")
+    SCRATCH["e16%d" % _b] = ("sbuf", [128, NP], "uint16")
+    SCRATCH["r%d" % _b] = ("sbuf", [128, NP], "bfloat16")
+    SCRATCH["lof%d" % _b] = ("sbuf", [128, NP], "float32")
+    SCRATCH["fb%d" % _b] = ("sbuf", [128, NP], "float32")
+for _b in range(DEP):
+    SCRATCH["hk%d" % _b] = ("sbuf", [128, E], F16)
+    SCRATCH["hs%d" % _b] = ("sbuf", [128, E], F16)
+    SCRATCH["lk%d" % _b] = ("sbuf", [128, E], "float32")
+    SCRATCH["ls%d" % _b] = ("sbuf", [128, E], "float32")
+    for _n in ("xl", "xh", "ms", "mn", "ad"):
+        SCRATCH["%s%d" % (_n, _b)] = ("sbuf", [128, E], "bfloat16")
+    SCRATCH["no%d" % _b] = ("sbuf", [128, P], F16)
+    SCRATCH["w%d" % _b] = ("sbuf", [128, P], "float32")
+    SCRATCH["hl%d" % _b] = ("sbuf", [128, 2 * P], "uint16")
+for _t in range(RO):
+    if _t < 3:
+        SCRATCH["pd%d" % _t] = ("psum", [128, 512], "float32")
+    SCRATCH["mw%d" % _t] = ("sbuf", [128, 768], "bfloat16")
+
+SEMAPHORES = (["sv", "ss", "st", "sg", "rl"] + ["ma%d" % t for t in range(RO)] + ["lx%d" % b for b in range(4)]
+              + ["lk"] + ["lc%d" % b for b in range(3)] + ["out%d" % b for b in range(24)])
+
+
+def rank_program(g, core, T, topo):
+    rank = T.rank_of(core)
+    if rank is None:
+        return
+    A, AF = AluOpType, ActivationFunctionType
+    queues = {"V": g.vector, "S": g.scalar, "T": g.tensor, "G": g, "Y": g.sync}
+    own = {"V": "sv", "S": "ss", "T": "st", "G": "sg"}
+    CY = 0.001
+    ch, parts = [8], {}
+
+    nodes, acc = [], {}
+
+    def R(name, c0, c1, step=1):
+        if name in COLS:
+            k = COLS.index(name)
+            return (T.fc[:, k:k + 1], [("fc", k, k + 1)])
+        return (T[name][:, c0:c1:step] if step > 1 else T[name][:, c0:c1], [(name, c0, c1)])
+
+    def IND(win, off):
+        return (win[0].indirect(off[0]), win[1] + off[1])
+
+    def clash(a, q, name, c0, c1, w):
+        if a[0] < c1 and c0 < a[1] and (w or a[2]):
+            return True
+        return name[:2] in ("pd", "pl", "pq", "pw", "pm") and a[3] != q
+
+    def node(q, fns, ins, outs, cost, sem=None, inc=1, preds=(), lat=0.0):
+        k, ps = len(nodes), set(preds)
+        early = []
+        for regs in parts.get(k, ()):
+            early.append({a[4] for name, c0, c1 in regs for a in acc.get(name, ()) if clash(a, q, name, c0, c1, False)})
+        before = {a[4] for name, c0, c1 in outs for a in acc.get(name, ()) if clash(a, q, name, c0, c1, True)}
+        kind = outs[0][0].strip("0123456789") if outs else "-"
+        for regs, w in ((ins, False), (outs, True)):
+            for name, c0, c1 in regs:
+                for a in acc.get(name, ()):
+                    if a[4] != k and clash(a, q, name, c0, c1, w):
+                        ps.add(a[4])
+        for regs, w in ((ins, False), (outs, True)):
+            for name, c0, c1 in regs:
+                lst = acc.setdefault(name, [])
+                if w:
+                    lst[:] = [a for a in lst if not (c0 <= a[0] and a[1] <= c1)]
+                lst.append((c0, c1, w, q, k))
+        nodes.append({"q": q, "fns": fns, "cost": cost, "sem": sem or own[q], "inc": inc, "ps": sorted(ps), "early": early, "before": before, "lat": lat, "kind": kind + ":%d" % ch[0]})
+        return k
+
+    def cat(*rs):
+        return [x for r_ in rs for x in r_[1]]
+
+    def col(c):
+        return R(c, 0, 1)[1]
+
+    def gat(n):
+        return 0.06 + n * GCY * CY
+
+    def size(r_, j=0):
+        return max(64, r_[1][j][2] - r_[1][j][1])
+
+    def copy(out, in_, n=None):
+        node("V", [lambda: g.vector.tensor_copy(out[0], in_[0])], in_[1], out[1], gat(n) if n else size(out) * CY)
+
+    def ts(out, in0, s1, s2, op0, op1=None, n=None, half=False):
+        ins = list(in0[1])
+        if isinstance(s1, str):
+            ins += col(s1)
+            s1 = R(s1, 0, 1)[0]
+        if isinstance(s2, str):
+            ins += col(s2)
+            s2 = R(s2, 0, 1)[0]
+        cost = gat(n) if n else (max(64, size(out) / 2) if half else size(out)) * CY
+        if op1 is None:
+            node("V", [lambda: g.vector.tensor_scalar(out[0], in0[0], s1, None, op0)], ins, out[1], cost)
+        else:
+            node("V", [lambda: g.vector.tensor_scalar(out[0], in0[0], s1, s2, op0, op1)], ins, out[1], cost)
+
+    def tt(out, in0, in1, op, n=None):
+        ps = any(x[1][0][0][:2] in ("pl", "pw", "pm") for x in (in0, in1))
+        node("V", [lambda: g.vector.tensor_tensor(out[0], in0[0], in1[0], op)], cat(in0, in1), out[1],
+             gat(n) if n else size(out) * (1 if ps else 2) * CY)
+
+    def scan(out, d0, d1, init, op0, op1, half=True):
+        first, ins = init, cat(d0, d1)
+        if isinstance(init, tuple):
+            first, ins = init[0], ins + init[1]
+        node("V", [lambda: g.vector.tensor_tensor_scan(out[0], d0[0], d1[0], first, op0, op1)], ins, out[1],
+             max(64, size(out) * (0.5 if half else 1)) * CY)
+
+    def fill(out, c):
+        node("V", [lambda: g.vector.memset(out[0], c)], [], out[1], size(out) * 0.5 * CY)
+
+    def act(out, in_, func, bias=None, scale=None, n=None):
+        kw, ins = {}, list(in_[1])
+        if isinstance(bias, str):
+            ins += col(bias)
+            kw["bias"] = R(bias, 0, 1)[0]
+        elif bias is not None:
+            kw["bias"] = bias
+        if isinstance(scale, str):
+            ins += col(scale)
+            kw["scale"] = R(scale, 0, 1)[0]
+        elif scale is not None:
+            kw["scale"] = scale
+        node("S", [lambda: g.scalar.activation(out[0], in_[0], func, **kw)], ins, out[1], gat(n) if n else 0.04 + size(out) * CY)
+
+    def group(out, pairs):
+        fns, ins, cost = [], [], 0.0
+        for j, (l, r_) in enumerate(pairs):
+            parts.setdefault(len(nodes), []).append(l[1] + r_[1])
+            fns.append(lambda l=l, r_=r_, j=j: g.tensor.matmul(out[0], l[0], r_[0], j == 0, j == len(pairs) - 1))
+            ins += [x for x in l[1] + r_[1] if x not in ins]
+            cost += max(64, out[1][0][2] - out[1][0][1]) * TCY * (4 if l[1][0][0] == "nif" else 1)
+        node("T", fns, ins, out[1], cost)
+
+    def wrap(out, mat, rname, c0, c1):
+        group(out, [(R(mat, 15 - r_, 143 - r_), R(rname, c0 + r_, c1, 16)) for r_ in range(16)])
+
+    def load(q, pairs, sem, outs, lat):
+        node(q, [lambda o=o, i=i: queues[q].dma_start(o, i) for o, i in pairs], [], outs, 0.06 * len(pairs), sem=sem, inc=16, lat=lat)
+
+    load("Y", [(T.wti[:, 0:1], T.wt[:, 0:1])], "lc0", col("wti"), 2.0)
+    load("Y", [(T.thi[:, 0:1], T.th[:, 0:1])], "lc1", col("thi"), 2.0)
+    for j, (c0, c1) in enumerate(((1536, 2048), (0, 768), (768, 1536))):
+        load("Y", [(T.xb[:, c0:c1], T.x0[:, c0:c1])], "lx%d" % j, [("xb", c0, c1)], 2.5 + 0.8 * j)
+    load("Y", [(T.kdw[16 * k:16 * k + 16, :], T.kd[:, :]) for k in range(8)], "lk", [("kdw", 0, U)], 9.5)
+    load("Y", [(T.taui[:, 0:1], T.tau[:, 0:1])], "lc2", col("taui"), 9.5)
+
+    fill(R("onesb", 0, 512), 1.0)
+
+    def asel(out, in_, pattern, op, base, cm):
+        node("G", [lambda: g.affine_select(out[0], in_[0], pattern, op, 0.0, base, cm)], in_[1], out[1], 0.5)
+
+    def iota(name, c0, c1, pattern, base, cm):
+        node("G", [lambda: g.iota(T[name][:, c0:c1], pattern, base, cm, allow_small_or_imprecise_dtypes=True)], [], [(name, c0, c1)],
+             0.15 + 2 * (c1 - c0) * CY)
+    asel(R("ib", 0, 128), R("onesb", 0, 128), [[-1, 128]], A.is_equal, 0, 1)
+    asel(R("g2a", 0, 144), R("onesb", 0, 144), [[-16, 9], [0, 16]], A.is_ge, 0, 1)
+    asel(R("g2", 0, 144), R("g2a", 0, 144), [[16, 9], [0, 16]], A.is_ge, 15, -1)
+    asel(R("l1", 0, 144), R("g2", 0, 144), [[0, 9], [1, 16]], A.is_equal, -15, 0)
+    node("G", [lambda: g.iota(T.pix[:, 0:1], [[0, 1]], 0, 1)], [], col("pix"), 0.15)
+    iota("c16", 0, 16, [[16, 16]], 0, 0)
+    asel(R("am", 0, 128), R("onesb", 0, 128), [[0, 8], [-1, 16]], A.is_ge, 0, 1)
+    asel(R("bef", 0, 8), R("onesb", 0, 8), [[16, 8]], A.is_gt, 0, -1)
+    asel(R("qm", 0, 128), R("onesb", 0, 128), [[0, 8], [-1, 16]], A.is_equal, 0, 1)
+    for b in range(3):
+        iota("ab", 512 * b, 512 * b + 512, [[1, 512]], S + 512 * b, 0)
+    scan(R("io16", 0, 512), R("onesb", 0, 512), R("onesb", 0, 512), -1.0, A.mult, A.add)
+    copy(R("ih", 0, 128), R("ib", 0, 128))
+    ts(R("nih", 0, 128), R("ib", 0, 128), -1.0, None, A.mult)
+    copy(R("thf", 0, 1), R("thi", 0, 1))
+    copy(R("wtf", 0, 1), R("wti", 0, 1))
+    act(R("lw", 0, 144), R("l1", 0, 144), AF.Copy, scale="wtf")
+    ts(R("pr", 0, 1), R("pix", 0, 1), 15, None, A.bitwise_and)
+    copy(R("prf", 0, 1), R("pr", 0, 1))
+    ts(R("icf", 0, 16), R("c16", 0, 16), "prf", None, A.add)
+    ts(R("uc", 0, 16), R("icf", 0, 16), 613.0, None, A.mult)
+
+    def next_u(t, i0, i1):
+        B = S + G * t
+        c0, c1 = i0 // 16, i1 // 16
+        n = str(t % 2)
+        wrap(R("pq", 304 + c0, 304 + c1), "lw", "xb", B - G + i0, B - G + i1)
+        tt(R("ui", c0, c1), R("pq", 304 + c0, 304 + c1), R("uc", c0, c1), A.add)
+        ts(R("uj", c0, c1), R("ui", c0, c1), 4095, None, A.bitwise_and)
+        copy(R("uo", c0, c1), R("uj", c0, c1))
+        ts(R("yf" + n, i0, i1), IND(R("kdw", 0, U), R("uo", c0, c1)), B / 4096.0, -0.484375, A.mult, A.add, n=i1 - i0)
+        ts(R("e16" + n, i0, i1), R("yf" + n, i0, i1), MAGIC, -MAGIC, A.add, A.add)
+
+    for b in (3, 0, 1, 2):
+        c0 = 512 * b
+        ts(R("n8h", c0, c0 + 512), R("xb", c0, c0 + 512), "thf", 8192.0, A.is_lt, A.mult, half=True)
+        group(R("pd%d" % (b % 3), 0, 512), [(R("ih", 0, 128), R("io16", 0, 512)), (R("nih", 0, 128), R("n8h", c0, c0 + 512))])
+        act(R("kw", c0, c0 + 512), R("pd%d" % (b % 3), 0, 512), AF.Copy, bias=float(c0))
+    for i0, i1 in UH:
+        next_u(0, i0, i1)
+    fill(R("rneg", 0, E), 0.0)
+    fill(R("rpos", 0, E), 0.0)
+    fill(R("rneg", 0, E, 16), -32768.0)
+    fill(R("rpos", 0, E, 16), 32768.0)
+    ts(R("i84h", 0, 128), R("ib", 0, 128), 8448.0, None, A.mult)
+    ts(R("c17", 0, P), R("onesb", 0, P), 1792.0, None, A.mult)
+    act(R("nif", 0, 128), R("ib", 0, 128), AF.Copy, scale=-1.0)
+    act(R("nib", 0, 128), R("ib", 0, 128), AF.Copy, scale=-1.0)
+    act(R("hib", 0, 128), R("ib", 0, 128), AF.Copy, scale=0.5)
+    fill(R("cq", 0, P), -0.25)
+    ts(R("ntau", 0, 1), R("taui", 0, 1), -8192.0, None, A.mult)
+    copy(R("nb0", 0, 1), R("ntau", 0, 1))
+    copy(R("pixf", 0, 1), R("pix", 0, 1))
+    copy(R("onh", 0, 128), R("onesb", 0, 128))
+    ts(R("nonh", 0, 8), R("onesb", 0, 8), -1.0, None, A.mult)
+    ts(R("befh", 0, 8), R("bef", 0, 8), -1.0, None, A.mult)
+    copy(R("ich", 0, 16), R("icf", 0, 16))
+    group(R("pm", 0, 128), [(R("qm", 0, 128), R("qm", 0, 128))])
+    group(R("pm", 128, 256), [(R("am", 0, 128), R("qm", 0, 128))])
+    copy(R("selh", 0, 8), R("g2", 0, 128, 16))
+    copy(R("leq", 0, 128), R("pm", 128, 256))
+    for j in range(2):
+        n = str(j)
+        ts(R("iz" + n, 0, 1), R("pixf", 0, 1), 256.0 + 128.0 * j, None, A.add)
+        ts(R("mz" + n, 0, 128), R("pm", 0, 128), "iz" + n, None, A.mult)
+        tt(R("qz" + n, 0, 128), R("mz" + n, 0, 128), R("leq", 0, 128), A.subtract)
+    for t in range(RO):
+        fill(R("mw%d" % t, 0, CAP), 0.0)
+
+    outs_used, pieces, uses = [0], [0], [0]
+
+    def store(out, in_):
+        node("Y", [lambda: g.sync.dma_start(out, in_[0])], in_[1], [], 0.06, sem="out%d" % outs_used[0], inc=16, lat=2.0)
+        outs_used[0] += 1
+
+    def send(t, B):
+        trs = []
+        for f in range(FO):
+            to = T.cores[(rank + 1 + (FO * t + f) % (N - 1)) % N]
+            rid, pid, _ = topo.addr(to)
+            b = B + NP + CAP * f
+            m = 0
+            for e in topo.engines(core, to)[4 * f:4 * f + 4]:
+                m |= 1 << e
+            trs.append(RemoteDMATransfer(dst_ids=[DstId(rid=rid, pnc=pid)], dma_engine_mask=m, remote_sem=T.sem["ma%d" % t],
+                                         srcs=[T["mw%d" % t][:, 0:CAP]], dsts=[T.xb[:, b:b + CAP]]))
+        g.remote_dma_fused(trs, local_sem=T.sem.rl)
+
+    for t in range(RO):
+        B, Y = S + G * t, G * t
+        gp = str(t % 2)
+        last = t == RO - 1
+        st = []
+        for c, (i0, i1) in enumerate(CH):
+            n, e = i1 - i0, 16 * (i1 - i0)
+            st.append((c, i0, i1, n, e, str(uses[0] % DEP), str(uses[0] % 2)))
+            uses[0] += 1
+
+        def names(c, i0, i1, n, e, b, l):
+            ch[0] = c
+            kids = IND(R("kw", 0, B), R("e16" + gp, i0, i1))
+            act(R("lk" + b, 0, e), kids, AF.Abs, n=e)
+            ts(R("hk" + b, 0, e), kids, -1792.0, -2048.0, A.add, A.max, n=e)
+            scan(R("hs" + b, 0, e), R("rneg", 0, e), R("hk" + b, 0, e), 0.0, A.add, A.max)
+            ts(R("no" + b, 0, n), R("hs" + b, 15, e, 16), -2000.0, None, A.is_lt)
+            tt(R("w" + b, 0, n), R("lk" + b, 0, e, 16), R("no" + b, 0, n), A.mult)
+            group(R("pl" + l, 0, n), [(R("ih", 0, 128), R("c17", 0, n)), (R("ih", 0, 128), R("hs" + b, 15, e, 16)),
+                                      (R("i84h", 0, 128), R("no" + b, 0, n)), (R("nif", 0, 128), R("w" + b, 0, n))])
+            scan(R("ls" + b, 0, e), R("rpos", 0, e), R("lk" + b, 0, e), 0.0, A.add, A.min, half=False)
+            copy(R("hl" + b, 0, n), R("pl" + l, 0, n))
+            tt(R("lof" + gp, i0, i1), R("pl" + l, 0, n), R("ls" + b, 15, e, 16), A.min)
+            copy(R("hl" + b, P, P + n), R("lof" + gp, i0, i1))
+
+        def values(c, i0, i1, n, e, b, l):
+            ch[0] = c
+            for j, (s0, s1) in enumerate(SUB.get(c, [(0, n)])):
+                f0, f1 = 16 * s0, 16 * s1
+                for name, h0, by in (("xl" + b, P, XLV), ("xh" + b, 0, XHV)):
+                    src = IND(R("xb", 0, B), R("hl" + b, h0 + s0, h0 + s1))
+                    if (c, j) in by:
+                        copy(R(name, f0, f1), src, n=f1 - f0)
+                    else:
+                        act(R(name, f0, f1), src, AF.Copy, n=f1 - f0)
+                if (c, j) in FUS:
+                    tt(R("df" + l, f0, f1), IND(R("xb", 0, B), R("hl" + b, s0, s1)), R("xl" + b, f0, f1), A.subtract, n=f1 - f0)
+                    act(R("ad" + b, f0, f1), R("df" + l, f0, f1), AF.Abs)
+                    continue
+                for c0 in range(f0, f1, 512):
+                    d = "pd%d" % (pieces[0] % 3)
+                    pieces[0] += 1
+                    c1 = min(f1, c0 + 512)
+                    assert c1 > c0
+                    group(R(d, 0, c1 - c0), [(R("nib", 0, 128), R("xh" + b, c0, c1)), (R("ib", 0, 128), R("xl" + b, c0, c1))])
+                    act(R("ad" + b, c0, c1), R(d, 0, c1 - c0), AF.Abs)
+            group(R("pq", 0, n), [(R("l1", 15 - r_, 143 - r_), R("ad" + b, r_, e, 16)) for r_ in range(16)])
+            act(R("r" + gp, i0, i1), R("pq", 0, n), AF.Relu, bias="nb%d" % t, scale=8192.0)
+            scan(R("mn" + b, 0, e), R("rpos", 0, e), R("xh" + b, 0, e), 0.0, A.add, A.min)
+            scan(R("ms" + b, 0, e), R("rneg", 0, e), R("xl" + b, 0, e), 0.0, A.add, A.max)
+            group(R("pl" + l, P, P + n), [(R("ib", 0, 128), R("cq", 0, n)), (R("hib", 0, 128), R("mn" + b, 15, e, 16)),
+                                          (R("hib", 0, 128), R("ms" + b, 15, e, 16))])
+            ts(R("xb", B + i0, B + i1), R("pl" + l, P, P + n), MAGIC, -MAGIC, A.add, A.add)
+            if not last:
+                ts(R("pw", i0, i1), R("xb", B + i0, B + i1), "thf", 8192.0, A.is_lt, A.mult)
+            tt(R("fb" + gp, i0, i1), R("r" + gp, i0, i1), R("pw", NP + i0, NP + i1), A.min)
+            tt(R("ab", Y + i0, Y + i1), R("fb" + gp, i0, i1), R("lof" + gp, i0, i1), A.max)
+            if not last:
+                tt(R("kw", B + i0, B + i1), R("ab", Y + i0, Y + i1), R("pw", i0, i1), A.subtract)
+                for u0, u1 in UH:
+                    if u1 == i1:
+                        next_u(t + 1, u0, u1)
+
+        ch[0] = 7
+        act(R("pw", NP, 2 * NP), R("ab", Y, Y + NP), AF.Copy)
+        for c in range(AHEAD):
+            names(*st[c])
+        for c in range(len(CH)):
+            values(*st[c])
+            if c + AHEAD < len(CH):
+                names(*st[c + AHEAD])
+        mw = "mw%d" % t
+        ch[0] = 9
+        for j in range(2):
+            m0, m1, c0, c1 = 128 * j, 128 * j + 128, 8 * j, 8 * j + 8
+            ncj = R("nc%d" % j, 0, 128)
+            group(R("pm", 0, 128), [(R("r" + gp, m0, m1), R("g2", 0, 128))])
+            ts(ncj, R("pm", 0, 128), 0.0, None, A.is_le)
+            tt(R("nq%d" % j, 0, 128), ncj, R("qz%d" % j, 0, 128), A.mult)
+            group(R("pm", 256 + c0, 256 + c1), [(R("ih", 0, 128), R("ich", c0, c1))]
+                  + ([(R("nc0", 0, 128), R("nonh", 0, 8))] if j else [])
+                  + [(ncj, R("befh", 0, 8)), (R("nq%d" % j, 0, 128), R("selh", 0, 8))])
+            copy(R("off", c0, c1), R("pm", 256 + c0, 256 + c1))
+            src, dst = R("xb", B + m0, B + m1), IND(R(mw, 0, 768), R("off", c0, c1))
+            node("V", [lambda src=src, dst=dst: g.vector.tensor_copy(dst[0], src[0])], src[1] + [("off", c0, c1)], [(mw, 0, 768)],
+                 0.06 + 0.003 * (m1 - m0))
+        k = node("G", [lambda t=t, B=B: send(t, B)], [(mw, 0, CAP)], [], 0.3, sem="rl", inc=8)
+        node("R", [None], [], [("xb", B + NP, B + G)], MLAT, sem="ma%d" % t, inc=8, preds=[k])
+        store(T.ya[:, Y:Y + G], R("ab", Y, Y + G))
+        store(T.yx[:, Y:Y + NP], R("xb", B, B + NP))
+        if not last:
+            nt = "nb%d" % (t + 1)
+            ts(R("pw", 0, 128), R("xb", B + NP, B + G), "thf", 8192.0, A.is_lt, A.mult)
+            tt(R("kw", B + NP, B + G), R("ab", Y + NP, Y + G), R("pw", 0, 128), A.subtract)
+            group(R("pm", 288, 296), [(R("onh", 0, 128), R("nc%d" % j, 0, 128, 16)) for j in range(2)])
+            node("V", [lambda: g.vector.tensor_reduce(R("cs", 0, 1)[0], T.pm[:, 288:296], AxisListType.X, A.add)],
+                 [("pm", 288, 296)], col("cs"), 0.064)
+            ts(R("ci", 0, 1), R("cs", 0, 1), -1.0, 2048.0, A.mult, A.add)
+            ts(R("cj", 0, 1), R("ci", 0, 1), 15, None, A.bitwise_and)
+            ts(R(nt, 0, 1), R("cj", 0, 1), -8192.0, "ntau", A.mult, A.add)
+        store(T.yx[:, Y + NP:Y + G], R("xb", B + NP, B + G))
+
+    rest = [0.0] * len(nodes)
+    users = [[] for _ in nodes]
+    for k in range(len(nodes) - 1, -1, -1):
+        nd = nodes[k]
+        rest[k] += nd["cost"] + nd["lat"]
+        for p in nd["ps"]:
+            rest[p] = max(rest[p], rest[k] + WAKE)
+            users[p].append(k)
+    left = [len(nd["ps"]) for nd in nodes]
+    ready_at = [0.0] * len(nodes)
+    ready = {q: [] for q in list(queues) + ["R"]}
+    free = {q: 0.0 for q in ready}
+    for k, nd in enumerate(nodes):
+        if not left[k]:
+            ready[nd["q"]].append(k)
+    order = []
+    for k, nd in enumerate(nodes):
+        rest[k] += BK.get(nd["kind"], 0.0)
+        if nd["q"] == "Y" and nd["kind"][-1] == "8":
+            rest[k] = 1e6 - k
+    while len(order) < len(nodes):
+        best = None
+        for q, lst in ready.items():
+            if lst:
+                at = max(free[q], min(ready_at[k] for k in lst))
+                if best is None or at < best[0]:
+                    best = (at, q)
+        at, q = best
+        k = max((k for k in ready[q] if ready_at[k] <= at + DELTA), key=lambda k: (rest[k], -k))
+        at = max(at, ready_at[k])
+        ready[q].remove(k)
+        order.append(k)
+        free[q] = at + nodes[k]["cost"]
+        for u in users[k]:
+            ready_at[u] = max(ready_at[u], free[q] + nodes[k]["lat"] + WAKE)
+            left[u] -= 1
+            if not left[u]:
+                ready[nodes[u]["q"]].append(u)
+
+    STATS["end"] = max(free.values())
+
+    count, waited, snap, token = {}, {}, {}, {}
+    known = {q: {} for q in ready}
+    for k in order:
+        nd = nodes[k]
+        q, sem = nd["q"], nd["sem"]
+        kn = known[q]
+        for j, fn in enumerate(nd["fns"]):
+            need, ps = {}, set() if j else set(nd["ps"])
+            if nd["early"]:
+                ps = nd["early"][j] if j else nd["before"] | nd["early"][0]
+            for p in ps:
+                s, n = token[p]
+                if q != "R" and kn.get(s, 0) < n:
+                    need[s] = max(need.get(s, 0), n)
+            for s, n in list(need.items()):
+                if any(o != s and snap[(o, m)].get(s, 0) >= n for o, m in need.items()):
+                    del need[s]
+            for s, n in need.items():
+                queues[q].wait_ge(T.sem[s], n)
+                waited[s] = max(waited.get(s, 0), n)
+                for o, m in snap[(s, n)].items():
+                    kn[o] = max(kn.get(o, 0), m)
+            count[sem] = count.get(sem, 0) + nd["inc"]
+            if fn is not None:
+                call = fn()
+                if sem != "rl":
+                    call.then_inc(T.sem[sem], nd["inc"])
+        n = count[sem]
+        token[k] = (sem, n)
+        snap[(sem, n)] = dict(kn) if q != "R" else {}
+        snap[(sem, n)][sem] = n
+    for s, n in count.items():
+        if waited.get(s, 0) < n:
+            (g if s == "rl" else g.sync).wait_ge(T.sem[s], n)

@@ -4,100 +4,184 @@ from concourse.mybir import AluOpType, ActivationFunctionType, AxisListType
 N, S, U, NP, CAP, FO, RO = 8, 2048, 4096, 256, 64, 2, 4
 G = NP + FO * CAP
 TOT = S + RO * G
-CH = [(0, 64), (64, 128), (128, 192), (192, 256)]
-UH = [(0, 256)]
-XHV, XLV = ((2, 0), (3, 0)), ()
-FUS = ((3, 1),)
-SUB = {3: [(0, 32), (32, 64)]}
-P = max(b - a for a, b in CH)
-E = 16 * P
-DEP = 4
-AHEAD = 4
-WAKE = 0.1
-GCY, TCY, MLAT = 1.6, 0.001, 3.0
-DELTA = 0.3
-BK = {'-:9': 5.2, 'ab:0': -6.2, 'ab:1': 3.1, 'ab:2': -7.5, 'ab:3': -5.7, 'ad:0': 8.1, 'ad:1': 5.0, 'ad:2': -6.5, 'ad:3': -6.8,
-      'ci:9': -1.5, 'cj:9': -7.0, 'df:3': -2.8, 'e:3': -8.2, 'fb:0': -4.8, 'fb:1': -4.7, 'fb:2': -4.3, 'fb:3': 6.5, 'fc:9': 6.6,
-      'hk:0': 13.4, 'hk:1': 5.9, 'hk:2': -9.1, 'hk:3': -9.8, 'hl:0': -5.7, 'hl:1': 3.6, 'hl:2': 1.2, 'hl:3': 3.7, 'hs:0': 5.6,
-      'hs:1': -9.0, 'hs:2': -2.7, 'hs:3': 2.3, 'kw:0': -7.4, 'kw:1': -3.7, 'kw:2': 4.7, 'kw:3': -4.6, 'kw:9': -1.7, 'lk:0': 7.2,
-      'lk:1': -7.2, 'lk:2': -3.5, 'lk:3': 2.4, 'lof:0': 2.1, 'lof:1': 8.7, 'lof:2': 2.0, 'lof:3': 10.4, 'ls:0': -2.6, 'ls:1': 10.8,
-      'ls:2': -8.2, 'ls:3': -8.5, 'mn:0': -6.4, 'mn:1': -4.8, 'mn:2': -7.1, 'mn:3': -3.1, 'ms:0': -5.5, 'ms:1': -3.6, 'ms:2': -3.8,
-      'ms:3': 7.7, 'mw:9': -4.1, 'nc:9': 4.0, 'no:0': -4.2, 'no:1': 2.4, 'no:2': 5.8, 'no:3': -0.4, 'nq:9': -2.0, 'off:9': -5.0,
-      'pd:0': 12.2, 'pd:1': 5.8, 'pd:2': -2.8, 'pd:3': -8.5, 'pl:0': 6.8, 'pl:1': 5.8, 'pl:2': 3.1, 'pl:3': -5.5, 'pm:9': 9.1, 'pq:0': 1.3,
-      'pq:1': 7.3, 'pq:2': -5.3, 'pq:3': -6.8, 'pw:0': -1.7, 'pw:1': -7.7, 'pw:2': -2.2, 'pw:3': -7.0, 'pw:7': -5.7, 'pw:9': -4.0,
-      'r:0': 10.9, 'r:1': 7.0, 'r:2': -5.4, 'r:3': -5.5, 'ui:3': -10.1, 'uj:3': -6.7, 'uo:3': -1.9, 'w:0': 0.4, 'w:1': 8.0, 'w:2': -2.9,
-      'w:3': 1.0, 'xb:0': 3.9, 'xb:1': 2.2, 'xb:2': -3.3, 'xb:3': -2.5, 'xb:9': -0.7, 'xh:0': -5.3, 'xh:1': -4.6, 'xh:2': -6.7,
-      'xh:3': -8.1, 'xl:0': 7.1, 'xl:1': 5.8, 'xl:2': -1.1, 'xl:3': -2.3, 'yf:3': 6.4}
+KT = TOT - G
+H = NP // 2
+NCH = [(0, 64), (64, 128)]
+VP = [(0, 32), (32, 64), (64, 96), (96, 128)]
+XH = ["SSSV"] + ["SSVV"] * 6 + ["SVVV"]
+DW = 512
+DP = [(0, 64), (64, 128)]
+KDE = "S"
+NQE = "S"
+CPE = "SSSSSSSS"
+CPB = "SVSVSVSV"
+REP = ""
+RW = 512
+Z16 = 1
+RE = "S"
+LIM = -8192.0 if RE == "S" else 1.0
+DLAT = 3.0
+TFIX = 0.0
+WAKE = 0.2
+GCY = 1.56
+SCY = 3.0
+CY = 0.00083
+TCY = 0.00083
+MLAT = 2.6
+DELTA = 0.2
+STEPB = 6.0
+SOFF = 7.0
+TRIES = 12000
+SEED = 1
+SLACK = 0.05
+PIECED = ("ha", "la", "hb", "lb", "hs", "ls", "xl", "xh", "ad", "mn", "ms", "pa", "pb", "r0", "r1", "no", "lo", "hl")
+ROUNDS = 8
 STATS = {}
 MAGIC = 12582912.0
-F16 = "float16"
+SH = 1792.0
+F16, BF, F32 = "float16", "bfloat16", "float32"
 
-COLS = ["wtf", "thf", "ntau", "prf", "pixf", "cs", "iz0", "iz1", "nb0", "nb1", "nb2", "nb3"]
+COLS = ["pixf", "prf", "pdf", "lom", "him", "zc", "etaf", "cs", "cm", "nb0", "nb1", "nt0", "nt1", "eb"]
+
+
+def _sb(n, dt):
+    return ("sbuf", [128, n], dt)
+
 
 SCRATCH = {
-    "xb": ("sbuf", [128, TOT], "bfloat16"),
-    "kw": ("sbuf", [128, TOT], "float32"),
-    "kdw": ("sbuf", [128, U], "int32"),
-    "ab": ("sbuf", [128, RO * G], "float32"),
-    "onesb": ("sbuf", [128, 512], "bfloat16"),
-    "io16": ("sbuf", [128, 512], F16),
-    "n8h": ("sbuf", [128, S], F16),
-    "rneg": ("sbuf", [128, E], "bfloat16"),
-    "rpos": ("sbuf", [128, E], "bfloat16"),
-    "g2a": ("sbuf", [128, 144], "bfloat16"),
-    "g2": ("sbuf", [128, 144], "bfloat16"),
-    "l1": ("sbuf", [128, 144], "bfloat16"),
-    "lw": ("sbuf", [128, 144], "bfloat16"),
-    "ib": ("sbuf", [128, 128], "bfloat16"),
-    "nib": ("sbuf", [128, 128], "bfloat16"),
-    "hib": ("sbuf", [128, 128], "bfloat16"),
-    "nif": ("sbuf", [128, 128], "float32"),
-    "ih": ("sbuf", [128, 128], F16),
-    "nih": ("sbuf", [128, 128], F16),
-    "i84h": ("sbuf", [128, 128], F16),
-    "c17": ("sbuf", [128, P], F16),
-    "cq": ("sbuf", [128, P], "bfloat16"),
-    "wti": ("sbuf", [128, 1], "int32"), "thi": ("sbuf", [128, 1], "int32"), "taui": ("sbuf", [128, 1], "int32"),
-    "fc": ("sbuf", [128, len(COLS)], "float32"),
-    "pix": ("sbuf", [128, 1], "int32"), "pr": ("sbuf", [128, 1], "int32"),
-    "c16": ("sbuf", [128, 16], "float32"), "icf": ("sbuf", [128, 16], "float32"),
-    "uc": ("sbuf", [128, 16], "float32"),
-    "ui": ("sbuf", [128, 16], "int32"), "uj": ("sbuf", [128, 16], "int32"), "uo": ("sbuf", [128, 16], "uint16"),
-    "am": ("sbuf", [128, 128], "bfloat16"), "qm": ("sbuf", [128, 128], "bfloat16"), "leq": ("sbuf", [128, 128], F16),
-    "bef": ("sbuf", [128, 8], "bfloat16"), "befh": ("sbuf", [128, 8], F16), "ich": ("sbuf", [128, 16], F16),
-    "onh": ("sbuf", [128, 128], F16), "nonh": ("sbuf", [128, 8], F16), "selh": ("sbuf", [128, 8], F16),
-    "pm": ("psum", [128, 512], "float32"),
-    "off": ("sbuf", [128, 16], "uint16"),
-    "ci": ("sbuf", [128, 1], "int32"), "cj": ("sbuf", [128, 1], "int32"),
-    "pl0": ("psum", [128, 512], "float32"), "pl1": ("psum", [128, 512], "float32"),
-    "pq": ("psum", [128, 512], "float32"), "pw": ("psum", [128, 512], "float32"),
+    "kdn": _sb(512, "int32"), "kdh": _sb(512, F16), "kdw": _sb(U, F32), "sel": _sb(1024, F16),
+    "onesb": _sb(512, BF),
+    "ab": _sb(2 * RO * H, F32), "xn": _sb(2 * (RO + 1) * H, BF), "mw": _sb(2 * RO * 768, BF), "mo": _sb(2 * RO * CAP, BF),
+    "mnm": _sb(RO * 128, F32),
+    "rn8": _sb(1024, BF), "rp8": _sb(1024, BF), "rn16": _sb(1024, BF), "rp16": _sb(1024, BF),
+    "ipad": _sb(144, BF), "nib": _sb(128, BF), "hib": _sb(128, F16), "ih": _sb(128, F16), "bigh": _sb(128, F16), "iff": _sb(128, F32),
+    "ilo": _sb(144, F16), "ihi": _sb(144, F16), "rpb": _sb(256, BF), "rpf": _sb(256, F32),
+    "jd": _sb(128, BF), "jm": _sb(128, BF), "g2": _sb(128, BF), "ng2": _sb(256, BF), "l1": _sb(144, BF), "ow": _sb(256, BF),
+    "wa": _sb(128, BF), "wb": _sb(128, BF), "nbef": _sb(8, BF), "none8": _sb(8, BF), "ich": _sb(8, BF), "c16": _sb(8, F32), "uc": _sb(8, F32),
+    "far": _sb(128, BF), "rz": _sb(128, BF), "csh": _sb(128, BF), "cns": _sb(128, BF),
+    "rowi": _sb(128, "int32"), "rowf": _sb(256, F32), "rep": _sb(8, F32),
+    "fc": _sb(len(COLS), F32), "pix": _sb(1, "int32"), "pr": _sb(1, "int32"), "pe_": _sb(1, "int32"), "pdi": _sb(1, "int32"),
+    "cia": _sb(1, "int32"), "cja": _sb(1, "int32"),
 }
-for _b in range(2):
-    for _n in ("nc", "nq", "qz", "mz"):
-        SCRATCH["%s%d" % (_n, _b)] = ("sbuf", [128, 128], F16)
-    SCRATCH["df%d" % _b] = ("sbuf", [128, E], "bfloat16")
-    SCRATCH["yf%d" % _b] = ("sbuf", [128, NP], "float32")
-    SCRATCH["e16%d" % _b] = ("sbuf", [128, NP], "uint16")
-    SCRATCH["r%d" % _b] = ("sbuf", [128, NP], "bfloat16")
-    SCRATCH["lof%d" % _b] = ("sbuf", [128, NP], "float32")
-    SCRATCH["fb%d" % _b] = ("sbuf", [128, NP], "float32")
-for _b in range(DEP):
-    SCRATCH["hk%d" % _b] = ("sbuf", [128, E], F16)
-    SCRATCH["hs%d" % _b] = ("sbuf", [128, E], F16)
-    SCRATCH["lk%d" % _b] = ("sbuf", [128, E], "float32")
-    SCRATCH["ls%d" % _b] = ("sbuf", [128, E], "float32")
-    for _n in ("xl", "xh", "ms", "mn", "ad"):
-        SCRATCH["%s%d" % (_n, _b)] = ("sbuf", [128, E], "bfloat16")
-    SCRATCH["no%d" % _b] = ("sbuf", [128, P], F16)
-    SCRATCH["w%d" % _b] = ("sbuf", [128, P], "float32")
-    SCRATCH["hl%d" % _b] = ("sbuf", [128, 2 * P], "uint16")
-for _t in range(RO):
-    if _t < 3:
-        SCRATCH["pd%d" % _t] = ("psum", [128, 512], "float32")
-    SCRATCH["mw%d" % _t] = ("sbuf", [128, 768], "bfloat16")
+for _n in ("pd0", "pd1", "pa0", "pa1", "pb0", "pb1", "pc", "pm"):
+    SCRATCH[_n] = ("psum", [128, 512], F32)
+for _s in "01":
+    SCRATCH.update({
+        "xb" + _s: _sb(TOT, BF), "kh" + _s: _sb(KT, F32), "kl" + _s: _sb(KT, F32), "lw" + _s: _sb(144, BF),
+        "ha" + _s: _sb(1024, F32), "la" + _s: _sb(1024, F32), "hb" + _s: _sb(1024, F16), "lb" + _s: _sb(1024, F16),
+        "hs" + _s: _sb(1024, F16), "ls" + _s: _sb(1024, F16), "no" + _s: _sb(H, F16), "lo" + _s: _sb(H, F16), "hl" + _s: _sb(2 * H, "uint16"),
+        "xl" + _s: _sb(2048, BF), "xh" + _s: _sb(2048, BF), "ad" + _s: _sb(2048, BF), "mn" + _s: _sb(2048, F16), "ms" + _s: _sb(2048, F16),
+        "z0" + _s: _sb(H, F16),
+        "r" + _s: _sb(H, BF), "fb" + _s: _sb(H, F32), "nq" + _s: _sb(320, BF), "off" + _s: _sb(8, "uint16"), "n8" + _s: _sb(G, BF),
+        "ui" + _s: _sb(8, "int32"), "uj" + _s: _sb(8, "int32"), "uo" + _s: _sb(8, "uint16"),
+        "kn" + _s: _sb(2 * H, F32), "yf" + _s: _sb(H, F32), "ek" + _s: _sb(H, F16), "el" + _s: _sb(H, "uint16"),
+    })
 
-SEMAPHORES = (["sv", "ss", "st", "sg", "rl"] + ["ma%d" % t for t in range(RO)] + ["lx%d" % b for b in range(4)]
-              + ["lk"] + ["lc%d" % b for b in range(3)] + ["out%d" % b for b in range(24)])
+SEMAPHORES = (["sv", "ss", "st", "sg", "rl", "out"] + ["ma%d" % k for k in range(2 * RO)] + ["l%d" % k for k in range(16)]
+              + [n + s for n in ("rx", "rkh", "rkl") for s in "01"])
+PSUM = [n for n, v in SCRATCH.items() if v[0] == "psum"]
+
+
+def place(nodes, seq, before, back):
+    at, busy = {}, {}
+    for k in seq:
+        nd = nodes[k]
+        t, d = (nd["lat"] if back else 0.0), nd["cost"]
+        for p in before[k]:
+            t = max(t, at[p] + nodes[p]["cost"] + (nd if back else nodes[p])["lat"] + WAKE)
+        if nd["q"] != "R":
+            lst = busy.setdefault(nd["q"], [])
+            j = len(lst)
+            while j and lst[j - 1][1] > t:
+                j -= 1
+            while j < len(lst) and lst[j][0] < t + d:
+                t = max(t, lst[j][1])
+                j += 1
+            lst.insert(j, (t, t + d))
+        at[k] = t
+    return at
+
+
+def tighten(nodes, users, order):
+    preds = [nd["ps"] for nd in nodes]
+    best = None
+    for _ in range(ROUNDS):
+        at = place(nodes, order, preds, False)
+        end = max(at[k] + nd["cost"] + nd["lat"] for k, nd in enumerate(nodes))
+        order = sorted(at, key=lambda k: (at[k], k))
+        if best is None or end < best[0]:
+            best = (end, order)
+        bk = place(nodes, sorted(at, key=lambda k: (-at[k] - nodes[k]["cost"], -k)), users, True)
+        order = sorted(bk, key=lambda k: (-bk[k] - nodes[k]["cost"], k))
+    STATS["end"] = best[0]
+    return best[1]
+
+
+def shift(nodes, users, order):
+    n = len(nodes)
+    npre = [len(nd["ps"]) for nd in nodes]
+    cost, tail, q = [nd["cost"] for nd in nodes], [nd["lat"] for nd in nodes], [nd["q"] for nd in nodes]
+    kind = [(nd["lab"][0].rstrip("01"), nd["lab"][1] if nd["step"] < 0 or nd["lab"][0][:2] in PIECED else 0, nd["q"], nd["step"] < 0)
+            for nd in nodes]
+    kinds = sorted(set(kind))
+    marks = [k for k in range(n) if q[k] == "R" or nodes[k]["lab"][0][:2] == "el"]
+    seed = [SEED]
+
+    def rnd():
+        seed[0] = (seed[0] * 6364136223846793005 + 1442695040888963407) % 2 ** 64
+        return (seed[0] >> 11) / 2.0 ** 53
+
+    def forward(key):
+        seq = sorted(range(n), key=lambda k: key[k])
+        left, ready, at, held = list(npre), [0.0] * n, [0.0] * n, [False] * n
+        busy, end = {x: [] for x in "VSTGY"}, 0.0
+        for k0 in seq:
+            if left[k0]:
+                held[k0] = True
+                continue
+            todo = [k0]
+            while todo:
+                k = todo.pop()
+                t, d = ready[k], cost[k]
+                if q[k] != "R":
+                    lst = busy[q[k]]
+                    j = len(lst)
+                    while j and lst[j - 1][1] > t:
+                        j -= 1
+                    while j < len(lst) and lst[j][0] < t + d:
+                        if lst[j][1] > t:
+                            t = lst[j][1]
+                        j += 1
+                    lst.insert(j, (t, t + d))
+                at[k] = t
+                e = t + d + tail[k]
+                if e > end:
+                    end = e
+                e += WAKE
+                for u in users[k]:
+                    if e > ready[u]:
+                        ready[u] = e
+                    left[u] -= 1
+                    if not left[u] and held[u]:
+                        todo.append(u)
+        return end + sum(at[k] for k in marks) / len(marks), at, end
+
+    key = [0.0] * n
+    for j, k in enumerate(order):
+        key[k] = j
+    best = cur = forward(key)
+    for it in range(TRIES):
+        by = {}
+        for _ in range((1, 2, 4)[int(3 * rnd())]):
+            by[kinds[int(len(kinds) * rnd())]] = (2 * rnd() - 1) * (0.5, 1.5, 3.0)[int(3 * rnd())]
+        st = int(9 * rnd()) - 1 if rnd() < 1 / 3 else None
+        c = forward([cur[1][k] + (by.get(kind[k], 0.0) if st is None or nodes[k]["step"] == st else 0.0) for k in range(n)])
+        if c[0] <= cur[0] + SLACK * (1 - it / TRIES):
+            cur = c
+        if c[0] < best[0]:
+            best = c
+    STATS["end"] = best[2]
+    return sorted(range(n), key=lambda k: (best[1][k], k))
 
 
 def rank_program(g, core, T, topo):
@@ -107,103 +191,109 @@ def rank_program(g, core, T, topo):
     A, AF = AluOpType, ActivationFunctionType
     queues = {"V": g.vector, "S": g.scalar, "T": g.tensor, "G": g, "Y": g.sync}
     own = {"V": "sv", "S": "ss", "T": "st", "G": "sg"}
-    CY = 0.001
-    ch, parts = [8], {}
+    parts, cur = {}, [-1]
 
     nodes, acc = [], {}
 
-    def R(name, c0, c1, step=1):
+    def R(name, c0, c1=None, step=1, p=(0, 128)):
         if name in COLS:
-            k = COLS.index(name)
-            return (T.fc[:, k:k + 1], [("fc", k, k + 1)])
-        return (T[name][:, c0:c1:step] if step > 1 else T[name][:, c0:c1], [(name, c0, c1)])
+            c0 = COLS.index(name)
+            name, c1 = "fc", c0 + 1
+        elif c1 is None:
+            c1 = c0 + 1
+        return (T[name][p[0]:p[1], c0:c1:step] if step > 1 else T[name][p[0]:p[1], c0:c1], [(name, c0, c1) + tuple(p)], -((c0 - c1) // step))
+
+    def C(name):
+        return R(name, 0)
 
     def IND(win, off):
-        return (win[0].indirect(off[0]), win[1] + off[1])
+        return (win[0].indirect(off[0]), win[1] + off[1], 16 * off[2])
 
-    def clash(a, q, name, c0, c1, w):
-        if a[0] < c1 and c0 < a[1] and (w or a[2]):
-            return True
-        return name[:2] in ("pd", "pl", "pq", "pw", "pm") and a[3] != q
+    def clash(a, q, reg, w):
+        return a[0] < reg[2] and reg[1] < a[1] and a[5] < reg[4] and reg[3] < a[6] and (w or a[2])
+
+    bank = {n: [None, [], []] for n in PSUM}
 
     def node(q, fns, ins, outs, cost, sem=None, inc=1, preds=(), lat=0.0):
         k, ps = len(nodes), set(preds)
         early = []
         for regs in parts.get(k, ()):
-            early.append({a[4] for name, c0, c1 in regs for a in acc.get(name, ()) if clash(a, q, name, c0, c1, False)})
-        before = {a[4] for name, c0, c1 in outs for a in acc.get(name, ()) if clash(a, q, name, c0, c1, True)}
-        kind = outs[0][0].strip("0123456789") if outs else "-"
+            early.append({a[4] for reg in regs for a in acc.get(reg[0], ()) if clash(a, q, reg, False)})
+        before = {a[4] for reg in outs for a in acc.get(reg[0], ()) if clash(a, q, reg, True)}
+        for name in {reg[0] for reg in ins + outs if reg[0] in bank}:
+            b = bank[name]
+            if b[0] != q:
+                b[:] = [q, [], b[1]]
+            b[1].append(k)
+            before |= set(b[2])
+        ps |= before
         for regs, w in ((ins, False), (outs, True)):
-            for name, c0, c1 in regs:
-                for a in acc.get(name, ()):
-                    if a[4] != k and clash(a, q, name, c0, c1, w):
+            for reg in regs:
+                for a in acc.get(reg[0], ()):
+                    if a[4] != k and clash(a, q, reg, w):
                         ps.add(a[4])
         for regs, w in ((ins, False), (outs, True)):
-            for name, c0, c1 in regs:
+            for name, c0, c1, p0, p1 in regs:
                 lst = acc.setdefault(name, [])
                 if w:
-                    lst[:] = [a for a in lst if not (c0 <= a[0] and a[1] <= c1)]
-                lst.append((c0, c1, w, q, k))
-        nodes.append({"q": q, "fns": fns, "cost": cost, "sem": sem or own[q], "inc": inc, "ps": sorted(ps), "early": early, "before": before, "lat": lat, "kind": kind + ":%d" % ch[0]})
+                    lst[:] = [a for a in lst if not (c0 <= a[0] and a[1] <= c1 and p0 <= a[5] and a[6] <= p1)]
+                lst.append((c0, c1, w, q, k, p0, p1))
+        nodes.append({"q": q, "fns": fns, "cost": cost, "sem": sem or own[q], "inc": inc, "ps": sorted(ps), "early": early,
+                      "before": before, "lat": lat, "step": cur[0], "lab": outs[0][:3] if outs else ("-", 0, 0)})
         return k
 
-    def cat(*rs):
-        return [x for r_ in rs for x in r_[1]]
+    def two(*rs):
+        return all(SCRATCH[x[1][0][0]][2] in (BF, F16, "uint16") for x in rs)
 
-    def col(c):
-        return R(c, 0, 1)[1]
+    def vcost(out, in_, *more):
+        if len(in_[1]) > 1:
+            return 0.05 + in_[2] * GCY * CY
+        return max(64, out[2] * (0.5 if two(out, in_, *more) else 1)) * CY
 
-    def gat(n):
-        return 0.06 + n * GCY * CY
+    def scal(x, ins):
+        if isinstance(x, tuple):
+            ins += x[1]
+            return x[0]
+        return x
 
-    def size(r_, j=0):
-        return max(64, r_[1][j][2] - r_[1][j][1])
+    def copy(out, in_):
+        node("V", [lambda: g.vector.tensor_copy(out[0], in_[0])], in_[1], out[1], vcost(out, in_))
 
-    def copy(out, in_, n=None):
-        node("V", [lambda: g.vector.tensor_copy(out[0], in_[0])], in_[1], out[1], gat(n) if n else size(out) * CY)
-
-    def ts(out, in0, s1, s2, op0, op1=None, n=None, half=False):
+    def ts(out, in0, s1, s2, op0, op1=None):
         ins = list(in0[1])
-        if isinstance(s1, str):
-            ins += col(s1)
-            s1 = R(s1, 0, 1)[0]
-        if isinstance(s2, str):
-            ins += col(s2)
-            s2 = R(s2, 0, 1)[0]
-        cost = gat(n) if n else (max(64, size(out) / 2) if half else size(out)) * CY
+        s1, s2 = scal(s1, ins), scal(s2, ins)
         if op1 is None:
-            node("V", [lambda: g.vector.tensor_scalar(out[0], in0[0], s1, None, op0)], ins, out[1], cost)
+            node("V", [lambda: g.vector.tensor_scalar(out[0], in0[0], s1, None, op0)], ins, out[1], vcost(out, in0))
         else:
-            node("V", [lambda: g.vector.tensor_scalar(out[0], in0[0], s1, s2, op0, op1)], ins, out[1], cost)
+            node("V", [lambda: g.vector.tensor_scalar(out[0], in0[0], s1, s2, op0, op1)], ins, out[1], vcost(out, in0))
 
-    def tt(out, in0, in1, op, n=None):
-        ps = any(x[1][0][0][:2] in ("pl", "pw", "pm") for x in (in0, in1))
-        node("V", [lambda: g.vector.tensor_tensor(out[0], in0[0], in1[0], op)], cat(in0, in1), out[1],
-             gat(n) if n else size(out) * (1 if ps else 2) * CY)
+    def tt(out, in0, in1, op):
+        ps = any(x[1][0][0] in PSUM for x in (in0, in1))
+        node("V", [lambda: g.vector.tensor_tensor(out[0], in0[0], in1[0], op)], in0[1] + in1[1], out[1],
+             vcost(out, in0) if len(in0[1]) > 1 else max(64, out[2] * (1 if ps else 2)) * CY)
 
-    def scan(out, d0, d1, init, op0, op1, half=True):
-        first, ins = init, cat(d0, d1)
-        if isinstance(init, tuple):
-            first, ins = init[0], ins + init[1]
-        node("V", [lambda: g.vector.tensor_tensor_scan(out[0], d0[0], d1[0], first, op0, op1)], ins, out[1],
-             max(64, size(out) * (0.5 if half else 1)) * CY)
+    def scan(out, d0, d1, init, op0, op1):
+        node("V", [lambda: g.vector.tensor_tensor_scan(out[0], d0[0], d1[0], init, op0, op1)], d0[1] + d1[1], out[1], vcost(out, d0, d1))
 
     def fill(out, c):
-        node("V", [lambda: g.vector.memset(out[0], c)], [], out[1], size(out) * 0.5 * CY)
+        node("V", [lambda: g.vector.memset(out[0], c)], [], out[1], vcost(out, out))
 
-    def act(out, in_, func, bias=None, scale=None, n=None):
+    def act(out, in_, func, bias=None, scale=None):
         kw, ins = {}, list(in_[1])
-        if isinstance(bias, str):
-            ins += col(bias)
-            kw["bias"] = R(bias, 0, 1)[0]
-        elif bias is not None:
-            kw["bias"] = bias
-        if isinstance(scale, str):
-            ins += col(scale)
-            kw["scale"] = R(scale, 0, 1)[0]
-        elif scale is not None:
-            kw["scale"] = scale
-        node("S", [lambda: g.scalar.activation(out[0], in_[0], func, **kw)], ins, out[1], gat(n) if n else 0.04 + size(out) * CY)
+        if bias is not None:
+            kw["bias"] = scal(bias, ins)
+        if scale is not None:
+            kw["scale"] = scal(scale, ins)
+        node("S", [lambda: g.scalar.activation(out[0], in_[0], func, **kw)], ins, out[1],
+             0.065 + in_[2] * GCY * CY if len(in_[1]) > 1 else 0.04 + max(64, out[2]) * CY)
+
+    def move(e, out, in_, add=0.0):
+        if e == "S":
+            act(out, in_, AF.Copy, bias=add if add else None)
+        elif add:
+            ts(out, in_, add, None, A.add)
+        else:
+            copy(out, in_)
 
     def group(out, pairs):
         fns, ins, cost = [], [], 0.0
@@ -211,107 +301,146 @@ def rank_program(g, core, T, topo):
             parts.setdefault(len(nodes), []).append(l[1] + r_[1])
             fns.append(lambda l=l, r_=r_, j=j: g.tensor.matmul(out[0], l[0], r_[0], j == 0, j == len(pairs) - 1))
             ins += [x for x in l[1] + r_[1] if x not in ins]
-            cost += max(64, out[1][0][2] - out[1][0][1]) * TCY * (4 if l[1][0][0] == "nif" else 1)
+            cost += TFIX + max(64, out[2]) * TCY * (4 if SCRATCH[l[1][0][0]][2] == F32 else 1)
         node("T", fns, ins, out[1], cost)
 
-    def wrap(out, mat, rname, c0, c1):
-        group(out, [(R(mat, 15 - r_, 143 - r_), R(rname, c0 + r_, c1, 16)) for r_ in range(16)])
+    loads = []
 
-    def load(q, pairs, sem, outs, lat):
-        node(q, [lambda o=o, i=i: queues[q].dma_start(o, i) for o, i in pairs], [], outs, 0.06 * len(pairs), sem=sem, inc=16, lat=lat)
-
-    load("Y", [(T.wti[:, 0:1], T.wt[:, 0:1])], "lc0", col("wti"), 2.0)
-    load("Y", [(T.thi[:, 0:1], T.th[:, 0:1])], "lc1", col("thi"), 2.0)
-    for j, (c0, c1) in enumerate(((1536, 2048), (0, 768), (768, 1536))):
-        load("Y", [(T.xb[:, c0:c1], T.x0[:, c0:c1])], "lx%d" % j, [("xb", c0, c1)], 2.5 + 0.8 * j)
-    load("Y", [(T.kdw[16 * k:16 * k + 16, :], T.kd[:, :]) for k in range(8)], "lk", [("kdw", 0, U)], 9.5)
-    load("Y", [(T.taui[:, 0:1], T.tau[:, 0:1])], "lc2", col("taui"), 9.5)
-
-    fill(R("onesb", 0, 512), 1.0)
-
-    def asel(out, in_, pattern, op, base, cm):
-        node("G", [lambda: g.affine_select(out[0], in_[0], pattern, op, 0.0, base, cm)], in_[1], out[1], 0.5)
-
-    def iota(name, c0, c1, pattern, base, cm):
-        node("G", [lambda: g.iota(T[name][:, c0:c1], pattern, base, cm, allow_small_or_imprecise_dtypes=True)], [], [(name, c0, c1)],
-             0.15 + 2 * (c1 - c0) * CY)
-    asel(R("ib", 0, 128), R("onesb", 0, 128), [[-1, 128]], A.is_equal, 0, 1)
-    asel(R("g2a", 0, 144), R("onesb", 0, 144), [[-16, 9], [0, 16]], A.is_ge, 0, 1)
-    asel(R("g2", 0, 144), R("g2a", 0, 144), [[16, 9], [0, 16]], A.is_ge, 15, -1)
-    asel(R("l1", 0, 144), R("g2", 0, 144), [[0, 9], [1, 16]], A.is_equal, -15, 0)
-    node("G", [lambda: g.iota(T.pix[:, 0:1], [[0, 1]], 0, 1)], [], col("pix"), 0.15)
-    iota("c16", 0, 16, [[16, 16]], 0, 0)
-    asel(R("am", 0, 128), R("onesb", 0, 128), [[0, 8], [-1, 16]], A.is_ge, 0, 1)
-    asel(R("bef", 0, 8), R("onesb", 0, 8), [[16, 8]], A.is_gt, 0, -1)
-    asel(R("qm", 0, 128), R("onesb", 0, 128), [[0, 8], [-1, 16]], A.is_equal, 0, 1)
-    for b in range(3):
-        iota("ab", 512 * b, 512 * b + 512, [[1, 512]], S + 512 * b, 0)
-    scan(R("io16", 0, 512), R("onesb", 0, 512), R("onesb", 0, 512), -1.0, A.mult, A.add)
-    copy(R("ih", 0, 128), R("ib", 0, 128))
-    ts(R("nih", 0, 128), R("ib", 0, 128), -1.0, None, A.mult)
-    copy(R("thf", 0, 1), R("thi", 0, 1))
-    copy(R("wtf", 0, 1), R("wti", 0, 1))
-    act(R("lw", 0, 144), R("l1", 0, 144), AF.Copy, scale="wtf")
-    ts(R("pr", 0, 1), R("pix", 0, 1), 15, None, A.bitwise_and)
-    copy(R("prf", 0, 1), R("pr", 0, 1))
-    ts(R("icf", 0, 16), R("c16", 0, 16), "prf", None, A.add)
-    ts(R("uc", 0, 16), R("icf", 0, 16), 613.0, None, A.mult)
-
-    def next_u(t, i0, i1):
-        B = S + G * t
-        c0, c1 = i0 // 16, i1 // 16
-        n = str(t % 2)
-        wrap(R("pq", 304 + c0, 304 + c1), "lw", "xb", B - G + i0, B - G + i1)
-        tt(R("ui", c0, c1), R("pq", 304 + c0, 304 + c1), R("uc", c0, c1), A.add)
-        ts(R("uj", c0, c1), R("ui", c0, c1), 4095, None, A.bitwise_and)
-        copy(R("uo", c0, c1), R("uj", c0, c1))
-        ts(R("yf" + n, i0, i1), IND(R("kdw", 0, U), R("uo", c0, c1)), B / 4096.0, -0.484375, A.mult, A.add, n=i1 - i0)
-        ts(R("e16" + n, i0, i1), R("yf" + n, i0, i1), MAGIC, -MAGIC, A.add, A.add)
-
-    for b in (3, 0, 1, 2):
-        c0 = 512 * b
-        ts(R("n8h", c0, c0 + 512), R("xb", c0, c0 + 512), "thf", 8192.0, A.is_lt, A.mult, half=True)
-        group(R("pd%d" % (b % 3), 0, 512), [(R("ih", 0, 128), R("io16", 0, 512)), (R("nih", 0, 128), R("n8h", c0, c0 + 512))])
-        act(R("kw", c0, c0 + 512), R("pd%d" % (b % 3), 0, 512), AF.Copy, bias=float(c0))
-    for i0, i1 in UH:
-        next_u(0, i0, i1)
-    fill(R("rneg", 0, E), 0.0)
-    fill(R("rpos", 0, E), 0.0)
-    fill(R("rneg", 0, E, 16), -32768.0)
-    fill(R("rpos", 0, E, 16), 32768.0)
-    ts(R("i84h", 0, 128), R("ib", 0, 128), 8448.0, None, A.mult)
-    ts(R("c17", 0, P), R("onesb", 0, P), 1792.0, None, A.mult)
-    act(R("nif", 0, 128), R("ib", 0, 128), AF.Copy, scale=-1.0)
-    act(R("nib", 0, 128), R("ib", 0, 128), AF.Copy, scale=-1.0)
-    act(R("hib", 0, 128), R("ib", 0, 128), AF.Copy, scale=0.5)
-    fill(R("cq", 0, P), -0.25)
-    ts(R("ntau", 0, 1), R("taui", 0, 1), -8192.0, None, A.mult)
-    copy(R("nb0", 0, 1), R("ntau", 0, 1))
-    copy(R("pixf", 0, 1), R("pix", 0, 1))
-    copy(R("onh", 0, 128), R("onesb", 0, 128))
-    ts(R("nonh", 0, 8), R("onesb", 0, 8), -1.0, None, A.mult)
-    ts(R("befh", 0, 8), R("bef", 0, 8), -1.0, None, A.mult)
-    copy(R("ich", 0, 16), R("icf", 0, 16))
-    group(R("pm", 0, 128), [(R("qm", 0, 128), R("qm", 0, 128))])
-    group(R("pm", 128, 256), [(R("am", 0, 128), R("qm", 0, 128))])
-    copy(R("selh", 0, 8), R("g2", 0, 128, 16))
-    copy(R("leq", 0, 128), R("pm", 128, 256))
-    for j in range(2):
-        n = str(j)
-        ts(R("iz" + n, 0, 1), R("pixf", 0, 1), 256.0 + 128.0 * j, None, A.add)
-        ts(R("mz" + n, 0, 128), R("pm", 0, 128), "iz" + n, None, A.mult)
-        tt(R("qz" + n, 0, 128), R("mz" + n, 0, 128), R("leq", 0, 128), A.subtract)
-    for t in range(RO):
-        fill(R("mw%d" % t, 0, CAP), 0.0)
-
-    outs_used, pieces, uses = [0], [0], [0]
+    def load(q, pairs, lat):
+        outs = [x for o, _ in pairs for x in o[1]]
+        loads.append(node(q, [lambda o=o, i=i: queues[q].dma_start(o[0], i) for o, i in pairs], [], outs, 0.06 * len(pairs),
+                          sem="l%d" % len(loads), inc=16, lat=lat))
 
     def store(out, in_):
-        node("Y", [lambda: g.sync.dma_start(out, in_[0])], in_[1], [], 0.06, sem="out%d" % outs_used[0], inc=16, lat=2.0)
-        outs_used[0] += 1
+        node("Y", [lambda: g.sync.dma_start(out, in_[0])], in_[1], [], 0.06, sem="out", inc=16, lat=2.0)
 
-    def send(t, B):
-        trs = []
+    def asel(out, in_, pattern, op, base, cm):
+        node("G", [lambda: g.affine_select(out[0], in_[0], pattern, op, 0.0, base, cm)], in_[1], out[1], 0.17 + 2 * out[2] * CY)
+
+    def iota(out, pattern, base, cm):
+        node("G", [lambda: g.iota(out[0], pattern, base, cm, allow_small_or_imprecise_dtypes=True)], [], out[1], 0.13 + 2 * out[2] * CY)
+
+    LO, HI = (0, 64), (64, 128)
+    HALF = (LO, HI)
+
+    def xn_of(s, t):
+        c = (2 * t + s) * H
+        return c
+
+    load("S", [(R("rowi", 0, 128, p=(j, j + 1)), x[:, 0:1]) for j, x in enumerate((T.th, T.wt, T.tau))], 2.0)
+    load("Y", [(R("kdn", 0, 512), T.kd[:, :])], 2.6)
+    load("Y", [(R("xb0", S // 2, S, p=p), T.x0[0:64, S // 2:S]) for p in HALF], 3.5)
+    load("Y", [(R("xb0", 0, S // 2, p=p), T.x0[0:64, 0:S // 2]) for p in HALF], 4.4)
+    load("Y", [(R("xb1", 0, S, p=p), T.x0[64:128, :]) for p in HALF], 6.5)
+
+    ib = R("ipad", 8, 136)
+    fill(R("onesb", 0, 512), 1.0)
+    names4 = ["pc", "pm", "pa0", "pa1"]
+    for b in range(4):
+        scan(R(names4[b], 0, 512), R("onesb", 0, 512), R("onesb", 0, 512), 512.0 * b - SH - 1.0, A.mult, A.add)
+    asel(R("ipad", 0, 144), R("onesb", 0, 144), [[-1, 144]], A.is_equal, 8, 1)
+    node("G", [lambda: g.iota(T.pix[:, 0:1], [[0, 1]], 0, 1)], [], C("pix")[1], 0.15)
+    iota(R("jd", 0, 128), [[1, 8], [0, 16]], 0, 0)
+    iota(R("c16", 0, 8), [[16, 8]], 0, 0)
+    iota(R("jm", 0, 128), [[0, 8], [1, 16]], 0, 0)
+    copy(R("sel", 0, 128), ib)
+    for w in (128, 256, 512):
+        copy(R("sel", w, 2 * w), R("sel", 0, w))
+    for h in range(2):
+        for k in range(2):
+            copy(R("rpf", 128 * h + 64 * k, 128 * h + 64 * k + 64), R("ipad", 8 + 64 * h, 72 + 64 * h))
+    copy(R("rpb", 0, 256), R("rpf", 0, 256))
+    for s in range(2):
+        for h in range(2):
+            copy(R("rowf", 128 * s + 64 * h, 128 * s + 64 * h + 64, p=(0, 3)), R("rowi", 64 * s, 64 * s + 64, p=(0, 3)))
+        group(R("pb0", 3 * s, 3 * s + 3), [(R("rowf", 128 * s, 128 * s + 128, p=(0, 3)), R("rpf", 0, 3, p=(0, 3)))])
+    copy(R("rep", 0, 6), R("pb0", 0, 6))
+    th = [R("rep", 0), R("rep", 3)]
+    copy(C("pixf"), C("pix"))
+    for name, fl, c, op in (("pr", "prf", 15, A.bitwise_and), ("pdi", "pdf", 4, A.arith_shift_right), ("pe_", "etaf", 6, A.arith_shift_right)):
+        ts(C(name), C("pix"), c, None, op)
+        copy(C(fl), C(name))
+    ts(R("g2", 0, 128), R("jd", 0, 128), C("pdf"), None, A.is_equal)
+    fill(R("l1", 0, 144), 0.0)
+    copy(R("l1", 15, 143, 16), R("g2", 0, 128, 16))
+    for s in range(2):
+        act(R("lw%d" % s, 0, 128), R("g2", 0, 128), AF.Copy, scale=R("rep", 3 * s + 1))
+    ts(R("far", 0, H), R("jm", 0, 128), C("prf"), -2097152.0, A.not_equal, A.mult)
+    ts(R("rz", 0, H), R("jm", 0, 128), 0.0, None, A.not_equal)
+    ts(C("lom"), C("prf"), 8.0, None, A.is_lt)
+    ts(C("him"), C("prf"), 8.0, None, A.is_ge)
+    ts(R("ilo", 0, 144), R("ipad", 0, 144), C("lom"), None, A.mult)
+    ts(R("ihi", 0, 144), R("ipad", 0, 144), C("him"), None, A.mult)
+    ts(C("zc"), C("etaf"), 128.0, C("prf"), A.mult, A.add)
+    ts(R("ich", 0, 8), R("c16", 0, 8), C("zc"), None, A.add)
+    ts(R("uc", 0, 8), R("ich", 0, 8), 613.0, None, A.mult)
+
+    ts(R("kdh", 0, 512), R("kdn", 0, 512), -2048.0, None, A.add)
+    for j in range(8):
+        b = ("pd0", "pd1", "pb1")[j % 3]
+        group(R(b, 0, 512), [(R("sel", j, 1024, 8), R("kdh", 0, 512))])
+        move(CPE[j], R("kdw", 512 * j, 512 * j + 512), R(b, 0, 512), 2048.0)
+
+    def lists(s, t):
+        B, z, pb, c = S + G * t, str(s), "pm" if t else "pb%d" % s, xn_of(s, t)
+        if not t:
+            for h, p in enumerate(HALF):
+                copy(R("xn", c, c + H, p=p), R("xb" + z, S - G + H * h, S - G + H * h + H, p=p))
+        group(R(pb, 384, 512), [(ib, R("far", 0, H)), (R("lw" + z, 0, 128), R("xn", c, c + H))])
+        scan(R("yf" + z, 0, H), R("rz", 0, H), R(pb, 384, 512), 0.0, A.mult, A.max)
+        tt(R("ui" + z, 0, 8), R("yf" + z, 15, H, 16), R("uc", 0, 8), A.add)
+        ts(R("uj" + z, 0, 8), R("ui" + z, 0, 8), 4095, None, A.bitwise_and)
+        copy(R("uo" + z, 0, 8), R("uj" + z, 0, 8))
+        src = IND(R("kdw", 0, U), R("uo" + z, 0, 8))
+        if KDE == "S":
+            act(R("yf" + z, 0, H), src, AF.Copy, bias=-0.484375, scale=B / 4096.0)
+        else:
+            ts(R("yf" + z, 0, H), src, B / 4096.0, -0.484375, A.mult, A.add)
+        ts(R("ek" + z, 0, H), R("yf" + z, 0, H), MAGIC, -MAGIC - SH, A.add, A.add)
+        ev, od = R("ek" + z, 0, H, 2), R("ek" + z, 1, H, 2)
+        group(R(pb, 384, 448), [(R("ilo", 8, 136), ev), (R("ilo", 0, 128), od)])
+        group(R(pb, 448, 512), [(R("ihi", 16, 144), ev), (R("ihi", 8, 136), od)])
+        ts(R("el" + z, 0, H), R(pb, 384, 512), SH, None, A.add)
+
+    lists(0, 0)
+    lists(1, 0)
+    for s in range(2):
+        for b in (2, 3, 0, 1):
+            c0, nt = 512 * b, ("xl1", "ad1")[s]
+            ts(R(nt, c0, c0 + 512), R("xb%d" % s, c0, c0 + 512), th[s], 8192.0, A.is_lt, A.mult)
+            tt(R("kh%d" % s, c0, c0 + 512), R(names4[b], 0, 512), R(nt, c0, c0 + 512), A.subtract)
+            tt(R("kl%d" % s, c0, c0 + 512), R(names4[b], 0, 512), R(nt, c0, c0 + 512), A.add)
+    for name, per, sg in (("rn8", 8, -1), ("rp8", 8, 1), ("rp16", 16, 1), ("rn16", 16, -1)):
+        iota(R(name, 0, RW), [[0, RW // per], [-32767 * sg, per]], 16384 * sg, 0)
+    copy(R("ih", 0, 128), ib)
+    ts(R("bigh", 0, 128), ib, 16384.0, None, A.mult)
+    act(R("iff", 0, 128), ib, AF.Copy)
+    act(R("nib", 0, 128), ib, AF.Copy, scale=-1.0)
+    ts(R("hib", 0, 128), ib, 1023.0 / 2048.0, None, A.mult)
+    fill(R("csh", 0, 128), SH)
+    fill(R("cns", 0, 128), -SH)
+    for s in range(2):
+        ts(C("nt%d" % s), R("rep", 3 * s + 2), LIM, None, A.mult)
+        copy(C("nb%d" % s), C("nt%d" % s))
+        fill(R("nq%d" % s, 0, 64), 0.0)
+    for k in range(2):
+        ts(R("ng2", 128 * k, 128 * k + 128), R("g2", 0, 128), -1.0, None, A.mult)
+    ts(C("cm"), C("pixf"), 2.0, 256.0, A.mult, A.add)
+    ts(R("wa", 0, 128), R("jm", 0, 128), C("prf"), None, A.is_lt)
+    ts(R("wb", 0, 128), R("jm", 0, 128), C("prf"), C("cm"), A.is_equal, A.mult)
+    fill(R("ow", 0, 128), 1.0)
+    tt(R("ow", 128, 256), R("wa", 0, 128), R("wb", 0, 128), A.add)
+    ts(R("nbef", 0, 8), R("jd", 0, 128, 16), C("pdf"), -1.0, A.is_ge, A.mult)
+    fill(R("none8", 0, 8), -1.0)
+    iota(R("mnm", 0, 512), [[G, RO], [1, 128]], S + NP, 0)
+    ts(C("eb"), C("etaf"), float(H), -float(NP), A.mult, A.add)
+    for k in range(2 * RO):
+        iota(R("mw", 768 * k, 768 * k + CAP), [[0, CAP]], 0, 0)
+    for t in range(RO):
+        store(T.ya[:, G * t + NP:G * t + G], R("mnm", 128 * t, 128 * t + 128))
+
+    def send(s, t, B):
+        trs, k = [], 2 * t + s
         for f in range(FO):
             to = T.cores[(rank + 1 + (FO * t + f) % (N - 1)) % N]
             rid, pid, _ = topo.addr(to)
@@ -319,111 +448,139 @@ def rank_program(g, core, T, topo):
             m = 0
             for e in topo.engines(core, to)[4 * f:4 * f + 4]:
                 m |= 1 << e
-            trs.append(RemoteDMATransfer(dst_ids=[DstId(rid=rid, pnc=pid)], dma_engine_mask=m, remote_sem=T.sem["ma%d" % t],
-                                         srcs=[T["mw%d" % t][:, 0:CAP]], dsts=[T.xb[:, b:b + CAP]]))
+            trs.append(RemoteDMATransfer(dst_ids=[DstId(rid=rid, pnc=pid)], dma_engine_mask=m, remote_sem=T.sem["ma%d" % k],
+                                         srcs=[T.mo[:, CAP * k:CAP * k + CAP]], dsts=[T["xb%d" % s][:, b:b + CAP]]))
         g.remote_dma_fused(trs, local_sem=T.sem.rl)
 
-    for t in range(RO):
-        B, Y = S + G * t, G * t
-        gp = str(t % 2)
+    pieces = [0]
+
+    def spread(tab, B, src, c, sem):
+        pairs = [(R(tab, B + H * h, B + H * h + H, p=p), R(src, c, c + H, p=HALF[h])) for h in range(2) for p in HALF]
+        node("Y", [lambda o=o, i=i: g.sync.dma_start(o[0], i[0]) for o, i in pairs], R(src, c, c + H)[1], R(tab, B, B + NP)[1],
+             0.06 * len(pairs), sem=sem, inc=16, lat=DLAT)
+
+    def step(s, t):
+        B, Y, z, k = S + G * t, G * t, str(s), 2 * t + s
         last = t == RO - 1
-        st = []
-        for c, (i0, i1) in enumerate(CH):
-            n, e = i1 - i0, 16 * (i1 - i0)
-            st.append((c, i0, i1, n, e, str(uses[0] % DEP), str(uses[0] % 2)))
-            uses[0] += 1
-
-        def names(c, i0, i1, n, e, b, l):
-            ch[0] = c
-            kids = IND(R("kw", 0, B), R("e16" + gp, i0, i1))
-            act(R("lk" + b, 0, e), kids, AF.Abs, n=e)
-            ts(R("hk" + b, 0, e), kids, -1792.0, -2048.0, A.add, A.max, n=e)
-            scan(R("hs" + b, 0, e), R("rneg", 0, e), R("hk" + b, 0, e), 0.0, A.add, A.max)
-            ts(R("no" + b, 0, n), R("hs" + b, 15, e, 16), -2000.0, None, A.is_lt)
-            tt(R("w" + b, 0, n), R("lk" + b, 0, e, 16), R("no" + b, 0, n), A.mult)
-            group(R("pl" + l, 0, n), [(R("ih", 0, 128), R("c17", 0, n)), (R("ih", 0, 128), R("hs" + b, 15, e, 16)),
-                                      (R("i84h", 0, 128), R("no" + b, 0, n)), (R("nif", 0, 128), R("w" + b, 0, n))])
-            scan(R("ls" + b, 0, e), R("rpos", 0, e), R("lk" + b, 0, e), 0.0, A.add, A.min, half=False)
-            copy(R("hl" + b, 0, n), R("pl" + l, 0, n))
-            tt(R("lof" + gp, i0, i1), R("pl" + l, 0, n), R("ls" + b, 15, e, 16), A.min)
-            copy(R("hl" + b, P, P + n), R("lof" + gp, i0, i1))
-
-        def values(c, i0, i1, n, e, b, l):
-            ch[0] = c
-            for j, (s0, s1) in enumerate(SUB.get(c, [(0, n)])):
-                f0, f1 = 16 * s0, 16 * s1
-                for name, h0, by in (("xl" + b, P, XLV), ("xh" + b, 0, XHV)):
-                    src = IND(R("xb", 0, B), R("hl" + b, h0 + s0, h0 + s1))
-                    if (c, j) in by:
-                        copy(R(name, f0, f1), src, n=f1 - f0)
+        cur[0] = k
+        pa, pb, xb = "pa" + z, "pb" + z, "xb" + z
+        rows = slice(64 * s, 64 * s + 64)
+        cn, mc = R("pc", NP * (t % 2), NP * (t % 2) + H), R("pc", NP * (t % 2) + H, NP * (t % 2) + NP)
+        if not s:
+            act(cn, R("mnm", H * t, H * t + H), AF.Identity, bias=C("eb"))
+            if not last:
+                act(mc, R("mnm", H * t, H * t + H), AF.Copy, bias=-SH)
+        for i0, i1 in NCH:
+            f0, f1 = 8 * i0, 8 * i1
+            la_, lb_ = R("el" + z, i0 // 2, i1 // 2), R("el" + z, 64 + i0 // 2, 64 + i1 // 2)
+            for tab, x, op, rs in (("kh", "h", A.max, "rn8"), ("kl", "l", A.min, "rp8")):
+                act(R(x + "a" + z, f0, f1), IND(R(tab + z, 0, B), la_), AF.Copy)
+                tt(R(x + "b" + z, f0, f1), IND(R(tab + z, 0, B), lb_), R(x + "a" + z, f0, f1), op)
+                for c0 in range(f0, f1, RW):
+                    c1 = min(f1, c0 + RW)
+                    scan(R(x + "s" + z, c0, c1), R(rs, 0, c1 - c0), R(x + "b" + z, c0, c1), 0.0, A.min if op == A.max else A.max, op)
+            hs, ls = R("hs" + z, f0 + 7, f1, 8), R("ls" + z, f0 + 7, f1, 8)
+            if Z16:
+                ts(R("z0" + z, i0, i1), R("ha" + z, f0, f1, 8), 8192.0, None, A.add)
+                ts(R("no" + z, i0, i1), hs, -2000.0, -1.0, A.is_lt, A.add)
+                group(R(pb, i0, i1), [(R("ih", 0, 128), R("z0" + z, i0, i1)), (R("bigh", 0, 128), R("no" + z, i0, i1))])
+            else:
+                ts(R("no" + z, i0, i1), hs, -2000.0, -0.5, A.is_lt, A.add)
+                group(R(pb, i0, i1), [(R("iff", 0, 128), R("ha" + z, f0, f1, 8)), (R("bigh", 0, 128), R("no" + z, i0, i1))])
+            tt(R(pb, H + i0, H + i1), R(pb, i0, i1), hs, A.max)
+            tt(R("lo" + z, i0, i1), R(pb, H + i0, H + i1), ls, A.min)
+            ts(R("hl" + z, H + i0, H + i1), R("lo" + z, i0, i1), SH, None, A.add)
+            ts(R("hl" + z, i0, i1), R(pb, H + i0, H + i1), SH, None, A.add)
+        group(R(pb, 0, H), [(ib, R("csh", 0, H)), (R("ih", 0, 128), R("lo" + z, 0, H))])
+        for (i0, i1), eh in zip(VP, XH[k]):
+            el = "S"
+            f0, f1 = 16 * i0, 16 * i1
+            move(el, R("xl" + z, f0, f1), IND(R(xb, 0, B), R("hl" + z, H + i0, H + i1)))
+            move(eh, R("xh" + z, f0, f1), IND(R(xb, 0, B), R("hl" + z, i0, i1)))
+            for c0 in range(f0, f1, 512):
+                d = "pd%d" % (pieces[0] % 2)
+                pieces[0] += 1
+                c1 = min(f1, c0 + 512)
+                for e0 in range(c0, c1, DW):
+                    e1 = min(c1, e0 + DW)
+                    group(R(d, e0 - c0, e1 - c0), [(R("nib", 0, 128), R("xh" + z, e0, e1)), (ib, R("xl" + z, e0, e1))])
+                act(R("ad" + z, c0, c1), R(d, 0, c1 - c0), AF.Abs)
+            for c0 in range(f0, f1, RW):
+                c1 = min(f1, c0 + RW)
+                scan(R("mn" + z, c0, c1), R("rp16", 0, c1 - c0), R("xh" + z, c0, c1), 0.0, A.max, A.min)
+                scan(R("ms" + z, c0, c1), R("rn16", 0, c1 - c0), R("xl" + z, c0, c1), 0.0, A.min, A.max)
+            for d0, d1 in DP:
+                if i0 < d1 <= i1:
+                    group(R(pa, d0, d1), [(R("l1", 15 - r_, 143 - r_), R("ad" + z, 16 * d0 + r_, 16 * d1, 16)) for r_ in range(16)])
+                    if RE == "S":
+                        act(R("r" + z, d0, d1), R(pa, d0, d1), AF.Relu, bias=C("nb" + z), scale=8192.0)
                     else:
-                        act(R(name, f0, f1), src, AF.Copy, n=f1 - f0)
-                if (c, j) in FUS:
-                    tt(R("df" + l, f0, f1), IND(R("xb", 0, B), R("hl" + b, s0, s1)), R("xl" + b, f0, f1), A.subtract, n=f1 - f0)
-                    act(R("ad" + b, f0, f1), R("df" + l, f0, f1), AF.Abs)
-                    continue
-                for c0 in range(f0, f1, 512):
-                    d = "pd%d" % (pieces[0] % 3)
-                    pieces[0] += 1
-                    c1 = min(f1, c0 + 512)
-                    assert c1 > c0
-                    group(R(d, 0, c1 - c0), [(R("nib", 0, 128), R("xh" + b, c0, c1)), (R("ib", 0, 128), R("xl" + b, c0, c1))])
-                    act(R("ad" + b, c0, c1), R(d, 0, c1 - c0), AF.Abs)
-            group(R("pq", 0, n), [(R("l1", 15 - r_, 143 - r_), R("ad" + b, r_, e, 16)) for r_ in range(16)])
-            act(R("r" + gp, i0, i1), R("pq", 0, n), AF.Relu, bias="nb%d" % t, scale=8192.0)
-            scan(R("mn" + b, 0, e), R("rpos", 0, e), R("xh" + b, 0, e), 0.0, A.add, A.min)
-            scan(R("ms" + b, 0, e), R("rneg", 0, e), R("xl" + b, 0, e), 0.0, A.add, A.max)
-            group(R("pl" + l, P, P + n), [(R("ib", 0, 128), R("cq", 0, n)), (R("hib", 0, 128), R("mn" + b, 15, e, 16)),
-                                          (R("hib", 0, 128), R("ms" + b, 15, e, 16))])
-            ts(R("xb", B + i0, B + i1), R("pl" + l, P, P + n), MAGIC, -MAGIC, A.add, A.add)
-            if not last:
-                ts(R("pw", i0, i1), R("xb", B + i0, B + i1), "thf", 8192.0, A.is_lt, A.mult)
-            tt(R("fb" + gp, i0, i1), R("r" + gp, i0, i1), R("pw", NP + i0, NP + i1), A.min)
-            tt(R("ab", Y + i0, Y + i1), R("fb" + gp, i0, i1), R("lof" + gp, i0, i1), A.max)
-            if not last:
-                tt(R("kw", B + i0, B + i1), R("ab", Y + i0, Y + i1), R("pw", i0, i1), A.subtract)
-                for u0, u1 in UH:
-                    if u1 == i1:
-                        next_u(t + 1, u0, u1)
-
-        ch[0] = 7
-        act(R("pw", NP, 2 * NP), R("ab", Y, Y + NP), AF.Copy)
-        for c in range(AHEAD):
-            names(*st[c])
-        for c in range(len(CH)):
-            values(*st[c])
-            if c + AHEAD < len(CH):
-                names(*st[c + AHEAD])
-        mw = "mw%d" % t
-        ch[0] = 9
-        for j in range(2):
-            m0, m1, c0, c1 = 128 * j, 128 * j + 128, 8 * j, 8 * j + 8
-            ncj = R("nc%d" % j, 0, 128)
-            group(R("pm", 0, 128), [(R("r" + gp, m0, m1), R("g2", 0, 128))])
-            ts(ncj, R("pm", 0, 128), 0.0, None, A.is_le)
-            tt(R("nq%d" % j, 0, 128), ncj, R("qz%d" % j, 0, 128), A.mult)
-            group(R("pm", 256 + c0, 256 + c1), [(R("ih", 0, 128), R("ich", c0, c1))]
-                  + ([(R("nc0", 0, 128), R("nonh", 0, 8))] if j else [])
-                  + [(ncj, R("befh", 0, 8)), (R("nq%d" % j, 0, 128), R("selh", 0, 8))])
-            copy(R("off", c0, c1), R("pm", 256 + c0, 256 + c1))
-            src, dst = R("xb", B + m0, B + m1), IND(R(mw, 0, 768), R("off", c0, c1))
-            node("V", [lambda src=src, dst=dst: g.vector.tensor_copy(dst[0], src[0])], src[1] + [("off", c0, c1)], [(mw, 0, 768)],
-                 0.06 + 0.003 * (m1 - m0))
-        k = node("G", [lambda t=t, B=B: send(t, B)], [(mw, 0, CAP)], [], 0.3, sem="rl", inc=8)
-        node("R", [None], [], [("xb", B + NP, B + G)], MLAT, sem="ma%d" % t, inc=8, preds=[k])
-        store(T.ya[:, Y:Y + G], R("ab", Y, Y + G))
-        store(T.yx[:, Y:Y + NP], R("xb", B, B + NP))
+                        ts(R("r" + z, d0, d1), R(pa, d0, d1), C("nb" + z), 8192.0, A.is_gt, A.mult)
+        c = xn_of(s, t + 1)
+        xn = R("xn", c, c + H)
+        group(R(pb, H, 2 * H), [(R("hib", 0, 128), R("mn" + z, 15, 2048, 16)), (R("hib", 0, 128), R("ms" + z, 15, 2048, 16))])
+        ts(xn, R(pb, H, 2 * H), MAGIC, -MAGIC, A.add, A.add)
         if not last:
-            nt = "nb%d" % (t + 1)
-            ts(R("pw", 0, 128), R("xb", B + NP, B + G), "thf", 8192.0, A.is_lt, A.mult)
-            tt(R("kw", B + NP, B + G), R("ab", Y + NP, Y + G), R("pw", 0, 128), A.subtract)
-            group(R("pm", 288, 296), [(R("onh", 0, 128), R("nc%d" % j, 0, 128, 16)) for j in range(2)])
-            node("V", [lambda: g.vector.tensor_reduce(R("cs", 0, 1)[0], T.pm[:, 288:296], AxisListType.X, A.add)],
-                 [("pm", 288, 296)], col("cs"), 0.064)
-            ts(R("ci", 0, 1), R("cs", 0, 1), -1.0, 2048.0, A.mult, A.add)
-            ts(R("cj", 0, 1), R("ci", 0, 1), 15, None, A.bitwise_and)
-            ts(R(nt, 0, 1), R("cj", 0, 1), -8192.0, "ntau", A.mult, A.add)
-        store(T.yx[:, Y + NP:Y + G], R("xb", B + NP, B + G))
+            lists(s, t + 1)
+            if "x" in REP:
+                spread(xb, B, "xn", c, "rx" + z)
+            else:
+                for h in range(2):
+                    group(R(pb, H + H * h, 2 * H + H * h), [(R("rpb", 128 * h, 128 * h + 128), xn)])
+                act(R(xb, B, B + NP), R(pb, H, 3 * H), AF.Copy)
+        group(R(pa, 128, 384), [(ib, R("ow", 0, 256)), (R("r" + z, 0, H), R("ng2", 0, 256))])
+        if NQE == "S":
+            act(R("nq" + z, 64, 320), R(pa, 128, 384), AF.Relu)
+        else:
+            ts(R("nq" + z, 64, 320), R(pa, 128, 384), 0.0, None, A.max)
+        group(R(pa, 384, 392), [(ib, R("ich", 0, 8)), (R("nq" + z, 0, 128), R("none8", 0, 8)), (R("nq" + z, 64, 192), R("nbef", 0, 8)),
+                                (R("nq" + z, 192, 320), R("g2", 0, 128, 16))])
+        copy(R("off" + z, 0, 8), R(pa, 384, 392))
+        dst = IND(R("mw", 768 * k, 768 * k + 768), R("off" + z, 0, 8))
+        node("V", [lambda: g.vector.tensor_copy(dst[0], xn[0])], xn[1] + dst[1][1:], dst[1][:1], 0.05 + SCY * CY * H)
+        group(R(pa, 400, 464), [(R("rpb", 128 * h, 128 * h + 128), R("mw", 768 * k, 768 * k + CAP)) for h in range(2)])
+        copy(R("mo", CAP * k, CAP * k + CAP), R(pa, 400, 464))
+        n = node("G", [lambda: send(s, t, B)], R("mo", CAP * k, CAP * k + CAP)[1], [], 0.3, sem="rl", inc=8)
+        node("R", [None], [], R(xb, B + NP, B + G)[1], MLAT, sem="ma%d" % k, inc=8, preds=[n])
+        an = R("ab", H * k, H * k + H)
+        tt(R("fb" + z, 0, H), R("r" + z, 0, H), cn, A.min)
+        tt(an, R(pb, 0, H), R("fb" + z, 0, H), A.max)
+        for h in range(2):
+            store(T.ya[rows, Y + H * h:Y + H * h + H], R("ab", H * k, H * k + H, p=HALF[h]))
+            if last:
+                store(T.yx[rows, Y + H * h:Y + H * h + H], R("xn", c, c + H, p=HALF[h]))
+        if not last:
+            if "k" in REP:
+                n8 = R("n8" + z, 0, H)
+                ts(n8, xn, th[s], 8192.0, A.is_lt, A.mult)
+                for j, mat in enumerate((R("nib", 0, 128), ib)):
+                    group(R(pb, H + H * j, 2 * H + H * j), [(ib, R("cns", 0, H)), (mat, n8)])
+                for j, tab in enumerate(("kh", "kl")):
+                    tt(R("kn" + z, H * j, H * j + H), R(pb, H + H * j, 2 * H + H * j), an, A.add)
+                    spread(tab + z, B, "kn" + z, H * j, "r" + tab + z)
+            else:
+                ts(R("n8" + z, 0, NP), R(xb, B, B + NP), th[s], 8192.0, A.is_lt, A.mult)
+                for h in range(2):
+                    group(R(pb, H * h, H * h + H), [(ib, R("cns", 0, H)), (R("rpf", 128 * h, 128 * h + 128), an)])
+                tt(R("kh" + z, B, B + NP), R(pb, 0, NP), R("n8" + z, 0, NP), A.subtract)
+                tt(R("kl" + z, B, B + NP), R(pb, 0, NP), R("n8" + z, 0, NP), A.add)
+            ts(R("n8" + z, NP, G), R(xb, B + NP, B + G), th[s], 8192.0, A.is_lt, A.mult)
+            tt(R("kh" + z, B + NP, B + G), mc, R("n8" + z, NP, G), A.subtract)
+            tt(R("kl" + z, B + NP, B + G), mc, R("n8" + z, NP, G), A.add)
+            if s:
+                group(R(pa, 464, 472), [(R("onesb", 0, 128), R("nq%d" % j, 64, 192, 16)) for j in range(2)])
+                node("V", [lambda: g.vector.tensor_reduce(C("cs")[0], T[pa][:, 464:472], AxisListType.X, A.add)],
+                     R(pa, 464, 472)[1], C("cs")[1], 0.064)
+                ts(C("cia"), C("cs"), -1.0, 2048.0, A.mult, A.add)
+                ts(C("cja"), C("cia"), 15, None, A.bitwise_and)
+                for j in range(2):
+                    ts(C("nb%d" % j), C("cja"), LIM, C("nt%d" % j), A.mult, A.add)
+        c0 = NP if last else 0
+        store(T.yx[rows, Y + c0:Y + G], R(xb, B + c0, B + G, p=LO))
+
+    for t in range(RO):
+        for s in range(2):
+            step(s, t)
 
     rest = [0.0] * len(nodes)
     users = [[] for _ in nodes]
@@ -433,6 +590,15 @@ def rank_program(g, core, T, topo):
         for p in nd["ps"]:
             rest[p] = max(rest[p], rest[k] + WAKE)
             users[p].append(k)
+    STATS["rest"], STATS["nodes"] = list(rest), nodes
+    for k in range(len(nodes) - 1, -1, -1):
+        nd = nodes[k]
+        if nd["step"] >= 0:
+            rest[k] -= STEPB * (nd["step"] // 2) + SOFF * (nd["step"] % 2)
+        else:
+            rest[k] = nd["cost"] + nd["lat"] + max([rest[u] + WAKE for u in users[k]] + [-1000.0])
+    for k in loads:
+        rest[k] = 1e6 - k
     left = [len(nd["ps"]) for nd in nodes]
     ready_at = [0.0] * len(nodes)
     ready = {q: [] for q in list(queues) + ["R"]}
@@ -441,11 +607,7 @@ def rank_program(g, core, T, topo):
         if not left[k]:
             ready[nd["q"]].append(k)
     order = []
-    for k, nd in enumerate(nodes):
-        rest[k] += BK.get(nd["kind"], 0.0)
-        if nd["q"] == "Y" and nd["kind"][-1] == "8":
-            rest[k] = 1e6 - k
-    while len(order) < len(nodes):
+    while len(order) < len(nodes) and "order" not in STATS:
         best = None
         for q, lst in ready.items():
             if lst:
@@ -457,14 +619,16 @@ def rank_program(g, core, T, topo):
         at = max(at, ready_at[k])
         ready[q].remove(k)
         order.append(k)
-        free[q] = at + nodes[k]["cost"]
+        done = at + nodes[k]["cost"]
+        free[q] = at if q == "R" else done
         for u in users[k]:
-            ready_at[u] = max(ready_at[u], free[q] + nodes[k]["lat"] + WAKE)
+            ready_at[u] = max(ready_at[u], done + nodes[k]["lat"] + WAKE)
             left[u] -= 1
             if not left[u]:
                 ready[nodes[u]["q"]].append(u)
-
-    STATS["end"] = max(free.values())
+    if "order" not in STATS:
+        STATS["order"] = shift(nodes, users, tighten(nodes, users, order))
+    order = loads + [k for k in STATS["order"] if k not in loads]
 
     count, waited, snap, token = {}, {}, {}, {}
     known = {q: {} for q in ready}

@@ -6,42 +6,43 @@ G = NP + FO * CAP
 TOT = S + RO * G
 KT = TOT - G
 H = NP // 2
+LAST = 2 * RO - 1
 NCH = [(0, 64), (64, 128)]
 VP = [(0, 32), (32, 64), (64, 96), (96, 128)]
-XH = ["SSSV"] + ["SSVV"] * 6 + ["SVVV"]
-DW = 512
+VPL = [(0, 32), (32, 64), (64, 96), (96, 128)]
+XL = ["SSSS"] * 8
+XH = ["SSSV"] + ["SSVV"] * 7
 DP = [(0, 64), (64, 128)]
-KDE = "S"
-NQE = "S"
 CPE = "SSSSSSSS"
-CPB = "SVSVSVSV"
-REP = ""
+FUS = 0
+PD = ["pd0", "pd1", "pm"]
 RW = 512
-Z16 = 1
-RE = "S"
-LIM = -8192.0 if RE == "S" else 1.0
-DLAT = 3.0
-TFIX = 0.0
 WAKE = 0.2
 GCY = 1.56
 SCY = 3.0
 CY = 0.00083
-TCY = 0.00083
 MLAT = 2.6
-DELTA = 0.2
-STEPB = 6.0
-SOFF = 7.0
-TRIES = 12000
+HALFGEN = 10.1
+FIRST = 10.5
+TRIES = (1500, 1200)
 SEED = 1
-SLACK = 0.05
-PIECED = ("ha", "la", "hb", "lb", "hs", "ls", "xl", "xh", "ad", "mn", "ms", "pa", "pb", "r0", "r1", "no", "lo", "hl")
-ROUNDS = 8
+WHEN = {
+    "S": "la1=0 ha1=1.2 la2=1.9 ha2=2.8 xl1=4.1 xl2=4.9 xh1=5.6 xh2=6.5 xl3=7.3 xh3=7.7 xl4=8 xh4=8.2 ad1=8.7 xl5=8.8 ad2=9.2 ad3=9.7 ad4=10.9"
+         " ad5=11.2 r1=12.8 nq1=13.7 xb1=14 yf1=16.4",
+    "V": "lb1=1 z1=1.7 ls1=1.9 hb1=2.1 lo1=2.8 lb2=2.9 hl1=3.6 hs1=3.7 hb2=3.9 lo2=4.7 z2=4.8 hl2=5.3 hs2=5.3 ls2=5.8 ms1=6.2 lo3=6.6 lo4=6.6"
+         " hl3=6.9 ms2=7 xh1=7.2 ms3=8.2 xh2=8.6 xh3=8.7 xh4=8.8 df1=9.2 mn1=9.3 mn3=9.9 mn2=10.1 ms4=10.3 ms5=10.4 mn4=10.9 mn5=10.9 xn1=11.9 nq1=13.6"
+         " off1=14.7 yf1=14.8 mw1=15 ui1=15.3 uj1=15.7 mo1=15.8 uo1=16.1 n81=16.2 fb1=16.8 fc1=16.8 ek1=16.9 ab1=18 el1=18.1 cia1=18.1"
+         " ek2=18.5 cja1=18.6 n82=19.4 fc2=19.7 kl2=19.7 kl1=19.8 kh2=20.7 kh1=20.8 fc3=22",
+    "T": "pb1=2.3 pa1=4.3 pb3=5.7 pb2=6.2 pd1=6.5 pd2=7.6 pd3=8.4 pb5=9.5 pd4=9.6 pd5=10.1 pb4=10.4 pa2=10.6 pb6=11.4 pa3=11.6 pc1=12.6 pb7=12.8"
+         " pa4=13.1 pb8=13.5 pb9=13.7 pc2=13.8 pa5=14.2 pa6=15.5 pa7=16.1 pb10=17.5 pb11=17.6 pb13=19.4 pb12=19.5",
+    "G": "-1=16.1", "R": "xb1=16.6", "Y": "-1=18.3 -2=18.3 -3=19.4 -4=19.5 -5=19.6",
+}
 STATS = {}
 MAGIC = 12582912.0
 SH = 1792.0
 F16, BF, F32 = "float16", "bfloat16", "float32"
 
-COLS = ["pixf", "prf", "pdf", "lom", "him", "zc", "etaf", "cs", "cm", "nb0", "nb1", "nt0", "nt1", "eb"]
+COLS = ["pixf", "prf", "pdf", "lom", "him", "zc", "etaf", "cs", "cm", "nb0", "nb1", "nt0", "nt1"]
 
 
 def _sb(n, dt):
@@ -50,15 +51,15 @@ def _sb(n, dt):
 
 SCRATCH = {
     "kdn": _sb(512, "int32"), "kdh": _sb(512, F16), "kdw": _sb(U, F32), "sel": _sb(1024, F16),
-    "onesb": _sb(512, BF),
+    "onesb": _sb(512, BF), "io": _sb(512, F32), "cbig": _sb(256, BF), "jj": _sb(256, BF), "cb": _sb(1024, BF), "df": _sb(512, BF),
     "ab": _sb(2 * RO * H, F32), "xn": _sb(2 * (RO + 1) * H, BF), "mw": _sb(2 * RO * 768, BF), "mo": _sb(2 * RO * CAP, BF),
     "mnm": _sb(RO * 128, F32),
-    "rn8": _sb(1024, BF), "rp8": _sb(1024, BF), "rn16": _sb(1024, BF), "rp16": _sb(1024, BF),
-    "ipad": _sb(144, BF), "nib": _sb(128, BF), "hib": _sb(128, F16), "ih": _sb(128, F16), "bigh": _sb(128, F16), "iff": _sb(128, F32),
-    "ilo": _sb(144, F16), "ihi": _sb(144, F16), "rpb": _sb(256, BF), "rpf": _sb(256, F32),
+    "rn8": _sb(RW, BF), "rp8": _sb(RW, BF), "rn16": _sb(RW, BF), "rp16": _sb(RW, BF),
+    "ipad": _sb(144, BF), "nib": _sb(128, BF), "hib": _sb(128, F16), "ih": _sb(128, F16), "bigh": _sb(128, F16),
+    "ilo": _sb(144, F16), "ihi": _sb(144, F16), "rpb": _sb(256, BF), "rph": _sb(256, F16), "i3": _sb(4, F32),
     "jd": _sb(128, BF), "jm": _sb(128, BF), "g2": _sb(128, BF), "ng2": _sb(256, BF), "l1": _sb(144, BF), "ow": _sb(256, BF),
     "wa": _sb(128, BF), "wb": _sb(128, BF), "nbef": _sb(8, BF), "none8": _sb(8, BF), "ich": _sb(8, BF), "c16": _sb(8, F32), "uc": _sb(8, F32),
-    "far": _sb(128, BF), "rz": _sb(128, BF), "csh": _sb(128, BF), "cns": _sb(128, BF),
+    "far": _sb(128, BF), "rz": _sb(128, BF), "csh": _sb(128, BF),
     "rowi": _sb(128, "int32"), "rowf": _sb(256, F32), "rep": _sb(8, F32),
     "fc": _sb(len(COLS), F32), "pix": _sb(1, "int32"), "pr": _sb(1, "int32"), "pe_": _sb(1, "int32"), "pdi": _sb(1, "int32"),
     "cia": _sb(1, "int32"), "cja": _sb(1, "int32"),
@@ -67,121 +68,195 @@ for _n in ("pd0", "pd1", "pa0", "pa1", "pb0", "pb1", "pc", "pm"):
     SCRATCH[_n] = ("psum", [128, 512], F32)
 for _s in "01":
     SCRATCH.update({
-        "xb" + _s: _sb(TOT, BF), "kh" + _s: _sb(KT, F32), "kl" + _s: _sb(KT, F32), "lw" + _s: _sb(144, BF),
+        "xb" + _s: _sb(TOT, BF), "kh" + _s: _sb(KT, F32), "kl" + _s: _sb(KT, F32), "lw" + _s: _sb(128, BF),
         "ha" + _s: _sb(1024, F32), "la" + _s: _sb(1024, F32), "hb" + _s: _sb(1024, F16), "lb" + _s: _sb(1024, F16),
-        "hs" + _s: _sb(1024, F16), "ls" + _s: _sb(1024, F16), "no" + _s: _sb(H, F16), "lo" + _s: _sb(H, F16), "hl" + _s: _sb(2 * H, "uint16"),
+        "hs" + _s: _sb(1024, F16), "ls" + _s: _sb(1024, F16), "z0" + _s: _sb(H, F16), "lo" + _s: _sb(2 * H, F16),
+        "hl" + _s: _sb(2 * H, "uint16"),
         "xl" + _s: _sb(2048, BF), "xh" + _s: _sb(2048, BF), "ad" + _s: _sb(2048, BF), "mn" + _s: _sb(2048, F16), "ms" + _s: _sb(2048, F16),
-        "z0" + _s: _sb(H, F16),
         "r" + _s: _sb(H, BF), "fb" + _s: _sb(H, F32), "nq" + _s: _sb(320, BF), "off" + _s: _sb(8, "uint16"), "n8" + _s: _sb(G, BF),
         "ui" + _s: _sb(8, "int32"), "uj" + _s: _sb(8, "int32"), "uo" + _s: _sb(8, "uint16"),
-        "kn" + _s: _sb(2 * H, F32), "yf" + _s: _sb(H, F32), "ek" + _s: _sb(H, F16), "el" + _s: _sb(H, "uint16"),
+        "yf" + _s: _sb(H, F32), "ek" + _s: _sb(2 * H, F16), "el" + _s: _sb(H, "uint16"),
     })
 
-SEMAPHORES = (["sv", "ss", "st", "sg", "rl", "out"] + ["ma%d" % k for k in range(2 * RO)] + ["l%d" % k for k in range(16)]
-              + [n + s for n in ("rx", "rkh", "rkl") for s in "01"])
+SEMAPHORES = ["sv", "ss", "st", "sg", "rl", "out"] + ["ma%d" % k for k in range(2 * RO)] + ["l%d" % k for k in range(8)]
 PSUM = [n for n, v in SCRATCH.items() if v[0] == "psum"]
 
 
-def place(nodes, seq, before, back):
-    at, busy = {}, {}
-    for k in seq:
-        nd = nodes[k]
-        t, d = (nd["lat"] if back else 0.0), nd["cost"]
-        for p in before[k]:
-            t = max(t, at[p] + nodes[p]["cost"] + (nd if back else nodes[p])["lat"] + WAKE)
-        if nd["q"] != "R":
-            lst = busy.setdefault(nd["q"], [])
-            j = len(lst)
-            while j and lst[j - 1][1] > t:
-                j -= 1
-            while j < len(lst) and lst[j][0] < t + d:
-                t = max(t, lst[j][1])
-                j += 1
-            lst.insert(j, (t, t + d))
-        at[k] = t
+def place(nodes, key, chain):
+    n = len(nodes)
+    users, left, after = [[] for _ in nodes], [len(nd["ps"]) for nd in nodes], {}
+    for k, nd in enumerate(nodes):
+        for p in nd["ps"]:
+            users[p].append(k)
+    for a, b in zip(chain, chain[1:]):
+        after[a] = b
+        left[b] += 1
+    ready, at, held, busy = [0.0] * n, [0.0] * n, set(), {}
+    for k0 in sorted(range(n), key=lambda k: (key[k], k)):
+        todo = [] if left[k0] else [k0]
+        held.add(k0)
+        while todo:
+            k = todo.pop()
+            nd = nodes[k]
+            t, d = ready[k], nd["cost"]
+            if nd["q"] != "R":
+                lst = busy.setdefault(nd["q"], [])
+                j = len(lst)
+                while j and lst[j - 1][1] > t:
+                    j -= 1
+                while j < len(lst) and lst[j][0] < t + d:
+                    t = max(t, lst[j][1])
+                    j += 1
+                lst.insert(j, (t, t + d))
+            at[k] = t
+            for u, e in [(u, t + d + nd["lat"] + WAKE) for u in users[k]] + ([(after[k], t + d)] if k in after else []):
+                ready[u] = max(ready[u], e)
+                left[u] -= 1
+                if not left[u] and u in held:
+                    todo.append(u)
     return at
 
 
-def tighten(nodes, users, order):
-    preds = [nd["ps"] for nd in nodes]
-    best = None
-    for _ in range(ROUNDS):
-        at = place(nodes, order, preds, False)
-        end = max(at[k] + nd["cost"] + nd["lat"] for k, nd in enumerate(nodes))
-        order = sorted(at, key=lambda k: (at[k], k))
-        if best is None or end < best[0]:
-            best = (end, order)
-        bk = place(nodes, sorted(at, key=lambda k: (-at[k] - nodes[k]["cost"], -k)), users, True)
-        order = sorted(bk, key=lambda k: (-bk[k] - nodes[k]["cost"], k))
-    STATS["end"] = best[0]
-    return best[1]
-
-
-def shift(nodes, users, order):
+def improve(nodes, order, tries, fixed):
     n = len(nodes)
-    npre = [len(nd["ps"]) for nd in nodes]
-    cost, tail, q = [nd["cost"] for nd in nodes], [nd["lat"] for nd in nodes], [nd["q"] for nd in nodes]
-    kind = [(nd["lab"][0].rstrip("01"), nd["lab"][1] if nd["step"] < 0 or nd["lab"][0][:2] in PIECED else 0, nd["q"], nd["step"] < 0)
-            for nd in nodes]
-    kinds = sorted(set(kind))
-    marks = [k for k in range(n) if q[k] == "R" or nodes[k]["lab"][0][:2] == "el"]
+    cost, q, step, kind = ([nd[x] for nd in nodes] for x in ("cost", "q", "step", "kind"))
+    out = [nd["cost"] + nd["lat"] + WAKE for nd in nodes]
+    fin = [nd["cost"] + nd["lat"] for nd in nodes]
+    who = {(step[k], q[k], kind[k]): k for k in range(n)}
+    reach, suc, npre = [0] * n, [[] for _ in nodes], [0] * n
+    for k, nd in enumerate(nodes):
+        for p in nd["ps"]:
+            reach[k] |= reach[p]
+        for p in nd["ps"]:
+            if not reach[k] >> p & 1:
+                suc[p].append(k)
+                npre[k] += 1
+        for p in nd["ps"]:
+            reach[k] |= 1 << p
+    prv, nxt, last = [-1] * n, [-1] * n, {}
+    for k in order:
+        if q[k] != "R":
+            prv[k] = last.get(q[k], -1)
+            if prv[k] >= 0:
+                nxt[prv[k]] = k
+            last[q[k]] = k
     seed = [SEED]
+    mails = [k for k in range(n) if q[k] == "R"]
 
-    def rnd():
+    def rnd(m):
         seed[0] = (seed[0] * 6364136223846793005 + 1442695040888963407) % 2 ** 64
-        return (seed[0] >> 11) / 2.0 ** 53
+        return (seed[0] >> 33) % m
 
-    def forward(key):
-        seq = sorted(range(n), key=lambda k: key[k])
-        left, ready, at, held = list(npre), [0.0] * n, [0.0] * n, [False] * n
-        busy, end = {x: [] for x in "VSTGY"}, 0.0
-        for k0 in seq:
-            if left[k0]:
-                held[k0] = True
+    def forward(prv, nxt):
+        left = [npre[k] + (prv[k] >= 0) for k in range(n)]
+        seq, head, end = [k for k in range(n) if not left[k]], [0.0] * n, 0.0
+        for k in seq:
+            h = head[k]
+            e = h + out[k]
+            if h + fin[k] > end:
+                end = h + fin[k]
+            for u in suc[k]:
+                if e > head[u]:
+                    head[u] = e
+                left[u] -= 1
+                if not left[u]:
+                    seq.append(u)
+            u = nxt[k]
+            if u >= 0:
+                e = h + cost[k]
+                if e > head[u]:
+                    head[u] = e
+                left[u] -= 1
+                if not left[u]:
+                    seq.append(u)
+        if len(seq) < n:
+            return None
+        return end + 0.3 * sum(head[k] for k in mails) / len(mails), end, head, seq
+
+    def put(prv, nxt, k, a):
+        p, x = prv[k], nxt[k]
+        if p >= 0:
+            nxt[p] = x
+        if x >= 0:
+            prv[x] = p
+        b = nxt[a]
+        prv[k], nxt[k], nxt[a] = a, b, k
+        if b >= 0:
+            prv[b] = k
+
+    cur = forward(prv, nxt)
+    best, until, since = (cur, list(prv), list(nxt)), {}, 0
+    for it in range(tries):
+        _, end, head, seq = cur
+        tail = [0.0] * n
+        for k in reversed(seq):
+            tail[k] = max([fin[k], cost[k] + tail[nxt[k]] if nxt[k] >= 0 else 0.0] + [out[k] + tail[u] for u in suc[k]])
+        k = [x for x in seq if head[x] == 0.0 and tail[x] > end - 1e-9]
+        k = k[rnd(len(k))]
+        runs = [[k]]
+        while True:
+            ways = [u for u in suc[k] if abs(out[k] + tail[u] - tail[k]) < 1e-9]
+            u = nxt[k]
+            if u >= 0 and abs(cost[k] + tail[u] - tail[k]) < 1e-9 and (not ways or rnd(2)):
+                runs[-1].append(u)
+            elif ways:
+                u = ways[rnd(len(ways))]
+                runs.append([u])
+            else:
+                break
+            k = u
+        moves = set()
+        for run in runs:
+            for u, v in [(x, run[-1]) for x in run[-9:-1]] + [(run[0], x) for x in run[1:9]]:
+                if not reach[v] >> u & 1 and (q[u] not in fixed or min(step[u], step[v]) < 0 or max(step[u], step[v]) == LAST):
+                    moves |= {(u, v, True), (u, v, False)}
+        moves, pick = sorted(moves), None
+        for _ in range(min(10, len(moves))):
+            u, v, late = moves.pop(rnd(len(moves)))
+            every = min(step[u], step[v]) >= 0 and rnd(8) > 0
+            p2, n2 = list(prv), list(nxt)
+            for d in range(-LAST, LAST + 1) if every else (0,):
+                a, b = who.get((step[u] + d, q[u], kind[u])), who.get((step[v] + d, q[u], kind[v]))
+                if a is None or b is None or (d and min(step[u], step[v]) + d < 0) or not 0 <= head[b] - head[a] <= 4.0:
+                    continue
+                if late:
+                    put(p2, n2, a, b)
+                elif p2[a] >= 0 and p2[a] != b:
+                    put(p2, n2, b, p2[a])
+            c = forward(p2, n2)
+            if c is None or (until.get((q[u], kind[u], kind[v]) if every else (u, v), -1) > it and c[0] >= best[0][0]):
                 continue
-            todo = [k0]
-            while todo:
-                k = todo.pop()
-                t, d = ready[k], cost[k]
-                if q[k] != "R":
-                    lst = busy[q[k]]
-                    j = len(lst)
-                    while j and lst[j - 1][1] > t:
-                        j -= 1
-                    while j < len(lst) and lst[j][0] < t + d:
-                        if lst[j][1] > t:
-                            t = lst[j][1]
-                        j += 1
-                    lst.insert(j, (t, t + d))
-                at[k] = t
-                e = t + d + tail[k]
-                if e > end:
-                    end = e
-                e += WAKE
-                for u in users[k]:
-                    if e > ready[u]:
-                        ready[u] = e
-                    left[u] -= 1
-                    if not left[u] and held[u]:
-                        todo.append(u)
-        return end + sum(at[k] for k in marks) / len(marks), at, end
+            if pick is None or c[0] < pick[0][0]:
+                pick = (c, p2, n2, (q[u], kind[v], kind[u]) if every else (v, u))
+        since += 1
+        if pick is not None and pick[0][0] < cur[0] + 0.6:
+            cur, prv, nxt, back = pick
+            until[back] = it + 8 + rnd(8)
+            if cur[0] < best[0][0] - 1e-9:
+                best, since = (cur, list(prv), list(nxt)), 0
+        if since > 150:
+            cur, prv, nxt, since = best[0], list(best[1]), list(best[2]), 0
+    STATS["end"] = best[0][1]
+    return sorted(range(n), key=lambda k: (best[0][2][k], k))
 
-    key = [0.0] * n
-    for j, k in enumerate(order):
-        key[k] = j
-    best = cur = forward(key)
-    for it in range(TRIES):
-        by = {}
-        for _ in range((1, 2, 4)[int(3 * rnd())]):
-            by[kinds[int(len(kinds) * rnd())]] = (2 * rnd() - 1) * (0.5, 1.5, 3.0)[int(3 * rnd())]
-        st = int(9 * rnd()) - 1 if rnd() < 1 / 3 else None
-        c = forward([cur[1][k] + (by.get(kind[k], 0.0) if st is None or nodes[k]["step"] == st else 0.0) for k in range(n)])
-        if c[0] <= cur[0] + SLACK * (1 - it / TRIES):
-            cur = c
-        if c[0] < best[0]:
-            best = c
-    STATS["end"] = best[2]
-    return sorted(range(n), key=lambda k: (best[1][k], k))
+
+def schedule(nodes):
+    n = len(nodes)
+    when = {q: dict((x.split("=")[0], float(x.split("=")[1])) for x in s.split()) for q, s in WHEN.items()}
+    key = [1e9] * n
+    for k in range(n - 1, -1, -1):
+        nd = nodes[k]
+        if nd["step"] >= 0:
+            key[k] = (FIRST + HALFGEN * (nd["step"] - 1) if nd["step"] else 0.0) + when[nd["q"]][nd["kind"]]
+        else:
+            key[k] -= nd["cost"] + nd["lat"] + WAKE
+        for p in nd["ps"]:
+            if nodes[p]["step"] < 0:
+                key[p] = min(key[p], key[k])
+    chain = sorted((k for k in range(n) if nodes[k]["q"] == "S" and nodes[k]["step"] >= 0), key=lambda k: (key[k], k))
+    at = place(nodes, key, chain)
+    order = sorted(range(n), key=lambda k: (at[k], k))
+    return improve(nodes, improve(nodes, order, TRIES[0], "S"), TRIES[1], "")
 
 
 def rank_program(g, core, T, topo):
@@ -191,7 +266,7 @@ def rank_program(g, core, T, topo):
     A, AF = AluOpType, ActivationFunctionType
     queues = {"V": g.vector, "S": g.scalar, "T": g.tensor, "G": g, "Y": g.sync}
     own = {"V": "sv", "S": "ss", "T": "st", "G": "sg"}
-    parts, cur = {}, [-1]
+    parts, cur, seen = {}, [-1], {}
 
     nodes, acc = [], {}
 
@@ -209,8 +284,8 @@ def rank_program(g, core, T, topo):
     def IND(win, off):
         return (win[0].indirect(off[0]), win[1] + off[1], 16 * off[2])
 
-    def clash(a, q, reg, w):
-        return a[0] < reg[2] and reg[1] < a[1] and a[5] < reg[4] and reg[3] < a[6] and (w or a[2])
+    def clash(a, reg, w):
+        return a[0] < reg[2] and reg[1] < a[1] and a[4] < reg[4] and reg[3] < a[5] and (w or a[2])
 
     bank = {n: [None, [], []] for n in PSUM}
 
@@ -218,37 +293,33 @@ def rank_program(g, core, T, topo):
         k, ps = len(nodes), set(preds)
         early = []
         for regs in parts.get(k, ()):
-            early.append({a[4] for reg in regs for a in acc.get(reg[0], ()) if clash(a, q, reg, False)})
-        before = {a[4] for reg in outs for a in acc.get(reg[0], ()) if clash(a, q, reg, True)}
+            early.append({a[3] for reg in regs for a in acc.get(reg[0], ()) if clash(a, reg, False)})
+        before = {a[3] for reg in outs for a in acc.get(reg[0], ()) if clash(a, reg, True)}
         for name in {reg[0] for reg in ins + outs if reg[0] in bank}:
             b = bank[name]
             if b[0] != q:
                 b[:] = [q, [], b[1]]
             b[1].append(k)
             before |= set(b[2])
-        ps |= before
-        for regs, w in ((ins, False), (outs, True)):
-            for reg in regs:
-                for a in acc.get(reg[0], ()):
-                    if a[4] != k and clash(a, q, reg, w):
-                        ps.add(a[4])
+        ps |= before | {a[3] for reg in ins for a in acc.get(reg[0], ()) if clash(a, reg, False)}
         for regs, w in ((ins, False), (outs, True)):
             for name, c0, c1, p0, p1 in regs:
                 lst = acc.setdefault(name, [])
                 if w:
-                    lst[:] = [a for a in lst if not (c0 <= a[0] and a[1] <= c1 and p0 <= a[5] and a[6] <= p1)]
-                lst.append((c0, c1, w, q, k, p0, p1))
-        nodes.append({"q": q, "fns": fns, "cost": cost, "sem": sem or own[q], "inc": inc, "ps": sorted(ps), "early": early,
-                      "before": before, "lat": lat, "step": cur[0], "lab": outs[0][:3] if outs else ("-", 0, 0)})
+                    lst[:] = [a for a in lst if not (c0 <= a[0] and a[1] <= c1 and p0 <= a[4] and a[5] <= p1)]
+                lst.append((c0, c1, w, k, p0, p1))
+        name = (outs[0][0] if outs else "-").rstrip("01")
+        name = "pd" if name in PD else name
+        seen[(cur[0], q, name)] = seen.get((cur[0], q, name), 0) + 1
+        nodes.append({"q": q, "fns": fns, "cost": cost, "sem": sem or own[q], "inc": inc, "ps": sorted(ps), "early": early, "before": before,
+                      "lat": lat, "step": cur[0], "kind": name + str(seen[(cur[0], q, name)]), "lab": outs[0][:3] if outs else ("-", 0, 0)})
         return k
-
-    def two(*rs):
-        return all(SCRATCH[x[1][0][0]][2] in (BF, F16, "uint16") for x in rs)
 
     def vcost(out, in_, *more):
         if len(in_[1]) > 1:
             return 0.05 + in_[2] * GCY * CY
-        return max(64, out[2] * (0.5 if two(out, in_, *more) else 1)) * CY
+        two = all(SCRATCH[x[1][0][0]][2] in (BF, F16, "uint16") for x in (out, in_) + more)
+        return max(64, out[2] * (0.5 if two else 1)) * CY
 
     def scal(x, ins):
         if isinstance(x, tuple):
@@ -301,7 +372,7 @@ def rank_program(g, core, T, topo):
             parts.setdefault(len(nodes), []).append(l[1] + r_[1])
             fns.append(lambda l=l, r_=r_, j=j: g.tensor.matmul(out[0], l[0], r_[0], j == 0, j == len(pairs) - 1))
             ins += [x for x in l[1] + r_[1] if x not in ins]
-            cost += TFIX + max(64, out[2]) * TCY * (4 if SCRATCH[l[1][0][0]][2] == F32 else 1)
+            cost += max(64, out[2]) * CY * (4 if SCRATCH[l[1][0][0]][2] == F32 else 1)
         node("T", fns, ins, out[1], cost)
 
     loads = []
@@ -314,46 +385,44 @@ def rank_program(g, core, T, topo):
     def store(out, in_):
         node("Y", [lambda: g.sync.dma_start(out, in_[0])], in_[1], [], 0.06, sem="out", inc=16, lat=2.0)
 
-    def asel(out, in_, pattern, op, base, cm):
-        node("G", [lambda: g.affine_select(out[0], in_[0], pattern, op, 0.0, base, cm)], in_[1], out[1], 0.17 + 2 * out[2] * CY)
-
-    def iota(out, pattern, base, cm):
+    def iota(out, pattern, base, cm=0):
         node("G", [lambda: g.iota(out[0], pattern, base, cm, allow_small_or_imprecise_dtypes=True)], [], out[1], 0.13 + 2 * out[2] * CY)
+
+    def gfill(out, c):
+        iota(out, [[0, out[2]]], int(c))
 
     LO, HI = (0, 64), (64, 128)
     HALF = (LO, HI)
-
-    def xn_of(s, t):
-        c = (2 * t + s) * H
-        return c
 
     load("S", [(R("rowi", 0, 128, p=(j, j + 1)), x[:, 0:1]) for j, x in enumerate((T.th, T.wt, T.tau))], 2.0)
     load("Y", [(R("kdn", 0, 512), T.kd[:, :])], 2.6)
     load("Y", [(R("xb0", S // 2, S, p=p), T.x0[0:64, S // 2:S]) for p in HALF], 3.5)
     load("Y", [(R("xb0", 0, S // 2, p=p), T.x0[0:64, 0:S // 2]) for p in HALF], 4.4)
-    load("Y", [(R("xb1", 0, S, p=p), T.x0[64:128, :]) for p in HALF], 6.5)
+    load("Y", [(R("xb1", 0, S, p=p), T.x0[64:128, :]) for p in HALF], 6.0)
 
     ib = R("ipad", 8, 136)
     fill(R("onesb", 0, 512), 1.0)
     names4 = ["pc", "pm", "pa0", "pa1"]
+    scan(R("io", 0, 512), R("onesb", 0, 512), R("onesb", 0, 512), -1.0, A.mult, A.add)
     for b in range(4):
-        scan(R(names4[b], 0, 512), R("onesb", 0, 512), R("onesb", 0, 512), 512.0 * b - SH - 1.0, A.mult, A.add)
-    asel(R("ipad", 0, 144), R("onesb", 0, 144), [[-1, 144]], A.is_equal, 8, 1)
+        move("S", R(names4[b], 0, 512), R("io", 0, 512), 512.0 * b - SH)
+    node("G", [lambda: g.affine_select(T.ipad[:, 0:144], T.onesb[:, 0:144], [[-1, 144]], A.is_equal, 0.0, 8, 1)],
+         R("onesb", 0, 144)[1], R("ipad", 0, 144)[1], 0.17 + 288 * CY)
     node("G", [lambda: g.iota(T.pix[:, 0:1], [[0, 1]], 0, 1)], [], C("pix")[1], 0.15)
-    iota(R("jd", 0, 128), [[1, 8], [0, 16]], 0, 0)
-    iota(R("c16", 0, 8), [[16, 8]], 0, 0)
-    iota(R("jm", 0, 128), [[0, 8], [1, 16]], 0, 0)
+    iota(R("jd", 0, 128), [[1, 8], [0, 16]], 0)
+    iota(R("c16", 0, 8), [[16, 8]], 0)
+    iota(R("jm", 0, 128), [[0, 8], [1, 16]], 0)
     copy(R("sel", 0, 128), ib)
     for w in (128, 256, 512):
         copy(R("sel", w, 2 * w), R("sel", 0, w))
     for h in range(2):
         for k in range(2):
-            copy(R("rpf", 128 * h + 64 * k, 128 * h + 64 * k + 64), R("ipad", 8 + 64 * h, 72 + 64 * h))
-    copy(R("rpb", 0, 256), R("rpf", 0, 256))
+            move("S", R("rpb", 128 * h + 64 * k, 128 * h + 64 * k + 64), R("ipad", 8 + 64 * h, 72 + 64 * h))
+    copy(R("i3", 0, 3, p=(0, 3)), R("ipad", 8, 11, p=(0, 3)))
     for s in range(2):
         for h in range(2):
             copy(R("rowf", 128 * s + 64 * h, 128 * s + 64 * h + 64, p=(0, 3)), R("rowi", 64 * s, 64 * s + 64, p=(0, 3)))
-        group(R("pb0", 3 * s, 3 * s + 3), [(R("rowf", 128 * s, 128 * s + 128, p=(0, 3)), R("rpf", 0, 3, p=(0, 3)))])
+        group(R("pb0", 3 * s, 3 * s + 3), [(R("rowf", 128 * s, 128 * s + 128, p=(0, 3)), R("i3", 0, 3, p=(0, 3)))])
     copy(R("rep", 0, 6), R("pb0", 0, 6))
     th = [R("rep", 0), R("rep", 3)]
     copy(C("pixf"), C("pix"))
@@ -361,7 +430,7 @@ def rank_program(g, core, T, topo):
         ts(C(name), C("pix"), c, None, op)
         copy(C(fl), C(name))
     ts(R("g2", 0, 128), R("jd", 0, 128), C("pdf"), None, A.is_equal)
-    fill(R("l1", 0, 144), 0.0)
+    gfill(R("l1", 0, 144), 0)
     copy(R("l1", 15, 143, 16), R("g2", 0, 128, 16))
     for s in range(2):
         act(R("lw%d" % s, 0, 128), R("g2", 0, 128), AF.Copy, scale=R("rep", 3 * s + 1))
@@ -381,61 +450,60 @@ def rank_program(g, core, T, topo):
         group(R(b, 0, 512), [(R("sel", j, 1024, 8), R("kdh", 0, 512))])
         move(CPE[j], R("kdw", 512 * j, 512 * j + 512), R(b, 0, 512), 2048.0)
 
-    def lists(s, t):
-        B, z, pb, c = S + G * t, str(s), "pm" if t else "pb%d" % s, xn_of(s, t)
-        if not t:
-            for h, p in enumerate(HALF):
-                copy(R("xn", c, c + H, p=p), R("xb" + z, S - G + H * h, S - G + H * h + H, p=p))
+    def lists(s, t, mid):
+        B, z, pb, c = S + G * t, str(s), "pb%d" % s, (2 * t + s) * H
         group(R(pb, 384, 512), [(ib, R("far", 0, H)), (R("lw" + z, 0, 128), R("xn", c, c + H))])
+        mid()
         scan(R("yf" + z, 0, H), R("rz", 0, H), R(pb, 384, 512), 0.0, A.mult, A.max)
         tt(R("ui" + z, 0, 8), R("yf" + z, 15, H, 16), R("uc", 0, 8), A.add)
         ts(R("uj" + z, 0, 8), R("ui" + z, 0, 8), 4095, None, A.bitwise_and)
         copy(R("uo" + z, 0, 8), R("uj" + z, 0, 8))
-        src = IND(R("kdw", 0, U), R("uo" + z, 0, 8))
-        if KDE == "S":
-            act(R("yf" + z, 0, H), src, AF.Copy, bias=-0.484375, scale=B / 4096.0)
-        else:
-            ts(R("yf" + z, 0, H), src, B / 4096.0, -0.484375, A.mult, A.add)
+        act(R("yf" + z, 0, H), IND(R("kdw", 0, U), R("uo" + z, 0, 8)), AF.Copy, bias=-0.484375, scale=B / 4096.0)
         ts(R("ek" + z, 0, H), R("yf" + z, 0, H), MAGIC, -MAGIC - SH, A.add, A.add)
         ev, od = R("ek" + z, 0, H, 2), R("ek" + z, 1, H, 2)
         group(R(pb, 384, 448), [(R("ilo", 8, 136), ev), (R("ilo", 0, 128), od)])
         group(R(pb, 448, 512), [(R("ihi", 16, 144), ev), (R("ihi", 8, 136), od)])
         ts(R("el" + z, 0, H), R(pb, 384, 512), SH, None, A.add)
 
-    lists(0, 0)
-    lists(1, 0)
+    for s in range(2):
+        for h, p in enumerate(HALF):
+            copy(R("xn", H * s, H * s + H, p=p), R("xb%d" % s, S - G + H * h, S - G + H * h + H, p=p))
+        lists(s, 0, lambda: None)
     for s in range(2):
         for b in (2, 3, 0, 1):
             c0, nt = 512 * b, ("xl1", "ad1")[s]
             ts(R(nt, c0, c0 + 512), R("xb%d" % s, c0, c0 + 512), th[s], 8192.0, A.is_lt, A.mult)
-            tt(R("kh%d" % s, c0, c0 + 512), R(names4[b], 0, 512), R(nt, c0, c0 + 512), A.subtract)
             tt(R("kl%d" % s, c0, c0 + 512), R(names4[b], 0, 512), R(nt, c0, c0 + 512), A.add)
-    for name, per, sg in (("rn8", 8, -1), ("rp8", 8, 1), ("rp16", 16, 1), ("rn16", 16, -1)):
-        iota(R(name, 0, RW), [[0, RW // per], [-32767 * sg, per]], 16384 * sg, 0)
+            tt(R("kh%d" % s, c0, c0 + 512), R(names4[b], 0, 512), R(nt, c0, c0 + 512), A.subtract)
+    for name, per, sg in (("rp8", 8, 1), ("rn8", 8, -1), ("rn16", 16, -1), ("rp16", 16, 1)):
+        iota(R(name, 0, RW), [[0, RW // per], [-32767 * sg, per]], 2048 * sg)
     copy(R("ih", 0, 128), ib)
-    ts(R("bigh", 0, 128), ib, 16384.0, None, A.mult)
-    act(R("iff", 0, 128), ib, AF.Copy)
     act(R("nib", 0, 128), ib, AF.Copy, scale=-1.0)
+    ts(R("bigh", 0, 128), ib, -64.0, None, A.mult)
+    copy(R("rph", 0, 256), R("rpb", 0, 256))
     ts(R("hib", 0, 128), ib, 1023.0 / 2048.0, None, A.mult)
-    fill(R("csh", 0, 128), SH)
-    fill(R("cns", 0, 128), -SH)
+    gfill(R("cbig", 0, 128), 131072)
+    gfill(R("cbig", 128, 256), -131072)
+    iota(R("jj", 0, 128), [[1, 128]], 0)
+    ts(C("cs"), C("etaf"), float(H), None, A.mult)
+    ts(R("jj", 128, 256), R("jj", 0, 128), C("cs"), None, A.add)
+    iota(R("cb", 0, 1024), [[G, RO], [NP - int(SH), 2], [0, 128]], S)
+    gfill(R("csh", 0, 128), SH)
     for s in range(2):
-        ts(C("nt%d" % s), R("rep", 3 * s + 2), LIM, None, A.mult)
-        copy(C("nb%d" % s), C("nt%d" % s))
-        fill(R("nq%d" % s, 0, 64), 0.0)
-    for k in range(2):
-        ts(R("ng2", 128 * k, 128 * k + 128), R("g2", 0, 128), -1.0, None, A.mult)
+        act(C("nt%d" % s), R("rep", 3 * s + 2), AF.Copy, scale=-8192.0)
+        act(C("nb%d" % s), R("rep", 3 * s + 2), AF.Copy, scale=-8192.0)
+        gfill(R("nq%d" % s, 0, 64), 0)
+        act(R("ng2", 128 * s, 128 * s + 128), R("g2", 0, 128), AF.Copy, scale=-1.0)
     ts(C("cm"), C("pixf"), 2.0, 256.0, A.mult, A.add)
     ts(R("wa", 0, 128), R("jm", 0, 128), C("prf"), None, A.is_lt)
     ts(R("wb", 0, 128), R("jm", 0, 128), C("prf"), C("cm"), A.is_equal, A.mult)
-    fill(R("ow", 0, 128), 1.0)
+    gfill(R("ow", 0, 128), 1)
     tt(R("ow", 128, 256), R("wa", 0, 128), R("wb", 0, 128), A.add)
     ts(R("nbef", 0, 8), R("jd", 0, 128, 16), C("pdf"), -1.0, A.is_ge, A.mult)
-    fill(R("none8", 0, 8), -1.0)
-    iota(R("mnm", 0, 512), [[G, RO], [1, 128]], S + NP, 0)
-    ts(C("eb"), C("etaf"), float(H), -float(NP), A.mult, A.add)
+    gfill(R("none8", 0, 8), -1)
+    iota(R("mnm", 0, 512), [[G, RO], [1, 128]], S + NP)
     for k in range(2 * RO):
-        iota(R("mw", 768 * k, 768 * k + CAP), [[0, CAP]], 0, 0)
+        gfill(R("mw", 768 * k, 768 * k + CAP), 0)
     for t in range(RO):
         store(T.ya[:, G * t + NP:G * t + G], R("mnm", 128 * t, 128 * t + 128))
 
@@ -454,11 +522,6 @@ def rank_program(g, core, T, topo):
 
     pieces = [0]
 
-    def spread(tab, B, src, c, sem):
-        pairs = [(R(tab, B + H * h, B + H * h + H, p=p), R(src, c, c + H, p=HALF[h])) for h in range(2) for p in HALF]
-        node("Y", [lambda o=o, i=i: g.sync.dma_start(o[0], i[0]) for o, i in pairs], R(src, c, c + H)[1], R(tab, B, B + NP)[1],
-             0.06 * len(pairs), sem=sem, inc=16, lat=DLAT)
-
     def step(s, t):
         B, Y, z, k = S + G * t, G * t, str(s), 2 * t + s
         last = t == RO - 1
@@ -467,69 +530,64 @@ def rank_program(g, core, T, topo):
         rows = slice(64 * s, 64 * s + 64)
         cn, mc = R("pc", NP * (t % 2), NP * (t % 2) + H), R("pc", NP * (t % 2) + H, NP * (t % 2) + NP)
         if not s:
-            act(cn, R("mnm", H * t, H * t + H), AF.Identity, bias=C("eb"))
+            group(cn, [(ib, R("jj", H, 2 * H)), (ib, R("cb", NP * t, NP * t + H))])
             if not last:
-                act(mc, R("mnm", H * t, H * t + H), AF.Copy, bias=-SH)
+                group(mc, [(ib, R("jj", 0, H)), (ib, R("cb", NP * t + H, NP * t + NP))])
         for i0, i1 in NCH:
-            f0, f1 = 8 * i0, 8 * i1
-            la_, lb_ = R("el" + z, i0 // 2, i1 // 2), R("el" + z, 64 + i0 // 2, 64 + i1 // 2)
-            for tab, x, op, rs in (("kh", "h", A.max, "rn8"), ("kl", "l", A.min, "rp8")):
-                act(R(x + "a" + z, f0, f1), IND(R(tab + z, 0, B), la_), AF.Copy)
-                tt(R(x + "b" + z, f0, f1), IND(R(tab + z, 0, B), lb_), R(x + "a" + z, f0, f1), op)
-                for c0 in range(f0, f1, RW):
-                    c1 = min(f1, c0 + RW)
-                    scan(R(x + "s" + z, c0, c1), R(rs, 0, c1 - c0), R(x + "b" + z, c0, c1), 0.0, A.min if op == A.max else A.max, op)
-            hs, ls = R("hs" + z, f0 + 7, f1, 8), R("ls" + z, f0 + 7, f1, 8)
-            if Z16:
-                ts(R("z0" + z, i0, i1), R("ha" + z, f0, f1, 8), 8192.0, None, A.add)
-                ts(R("no" + z, i0, i1), hs, -2000.0, -1.0, A.is_lt, A.add)
-                group(R(pb, i0, i1), [(R("ih", 0, 128), R("z0" + z, i0, i1)), (R("bigh", 0, 128), R("no" + z, i0, i1))])
-            else:
-                ts(R("no" + z, i0, i1), hs, -2000.0, -0.5, A.is_lt, A.add)
-                group(R(pb, i0, i1), [(R("iff", 0, 128), R("ha" + z, f0, f1, 8)), (R("bigh", 0, 128), R("no" + z, i0, i1))])
-            tt(R(pb, H + i0, H + i1), R(pb, i0, i1), hs, A.max)
-            tt(R("lo" + z, i0, i1), R(pb, H + i0, H + i1), ls, A.min)
-            ts(R("hl" + z, H + i0, H + i1), R("lo" + z, i0, i1), SH, None, A.add)
-            ts(R("hl" + z, i0, i1), R(pb, H + i0, H + i1), SH, None, A.add)
-        group(R(pb, 0, H), [(ib, R("csh", 0, H)), (R("ih", 0, 128), R("lo" + z, 0, H))])
-        for (i0, i1), eh in zip(VP, XH[k]):
-            el = "S"
+            f0, f1, n = 8 * i0, 8 * i1, i1 - i0
+            for tab, x, op, no, rs in (("kl", "l", A.min, A.max, "rp8"), ("kh", "h", A.max, A.min, "rn8")):
+                act(R(x + "a" + z, f0, f1), IND(R(tab + z, 0, B), R("el" + z, i0 // 2, i1 // 2)), AF.Copy)
+                tt(R(x + "b" + z, f0, f1), IND(R(tab + z, 0, B), R("el" + z, 64 + i0 // 2, 64 + i1 // 2)), R(x + "a" + z, f0, f1), op)
+                scan(R(x + "s" + z, f0, f1), R(rs, 0, f1 - f0), R(x + "b" + z, f0, f1), 0.0, no, op)
+            hs, ls, z0 = R("hs" + z, f0 + 7, f1, 8), R("ls" + z, f0 + 7, f1, 8), R("z0" + z, i0, i1)
+            ts(z0, R("la" + z, f0, f1, 8), -8192.0, None, A.add)
+            tl, tb = R(pb, H + i0, H + i1), R(pb, i0, i1) if i0 else R(pa, H, H + n)
+            group(tl, [(ib, R("cbig", 0, n)), (R("ih", 0, 128), z0), (R("bigh", 0, 128), ls)])
+            group(tb, [(ib, R("cbig", H, H + n)), (R("ih", 0, 128), z0), (R("bigh", 0, 128), hs)])
+            tt(R("lo" + z, i0 + i1, 2 * i1), tl, ls, A.min)
+            tt(R("lo" + z, 2 * i0, i0 + i1), tb, hs, A.max)
+            for a, b in ((2 * i0, 2 * i1),) if i0 else ((n, 2 * n), (0, n)):
+                ts(R("hl" + z, a, b), R("lo" + z, a, b), SH, None, A.add)
+        for i0, i1 in NCH:
+            group(R(pb, i0, i1), [(ib, R("csh", 0, i1 - i0)), (R("ih", 0, 128), R("lo" + z, i0 + i1, 2 * i1))])
+
+        def listof(i0, i1, low):
+            a, b = [x for x in NCH if x[0] <= i0 and i1 <= x[1]][0]
+            return IND(R(xb, 0, B), R("hl" + z, a + (b - a) * low + i0, a + (b - a) * low + i1))
+        vp = VPL if k == LAST else VP
+        for name, low, pcs in (("xl", 1, XL[k]), ("xh", 0, XH[k])):
+            starts = [j for j in range(len(vp)) if pcs[j].isupper()] + [len(vp)]
+            for j, j1 in zip(starts, starts[1:]):
+                move(pcs[j], R(name + z, 16 * vp[j][0], 16 * vp[j1 - 1][1]), listof(vp[j][0], vp[j1 - 1][1], low))
+        for i0, i1 in vp:
             f0, f1 = 16 * i0, 16 * i1
-            move(el, R("xl" + z, f0, f1), IND(R(xb, 0, B), R("hl" + z, H + i0, H + i1)))
-            move(eh, R("xh" + z, f0, f1), IND(R(xb, 0, B), R("hl" + z, i0, i1)))
-            for c0 in range(f0, f1, 512):
-                d = "pd%d" % (pieces[0] % 2)
+            if FUS and k == LAST and i1 == H:
+                d = R("df", 0, f1 - f0)
+                tt(d, listof(i0, i1, 0), R("xl" + z, f0, f1), A.subtract)
+            else:
+                d = R(PD[pieces[0] % len(PD)], 0, f1 - f0)
                 pieces[0] += 1
-                c1 = min(f1, c0 + 512)
-                for e0 in range(c0, c1, DW):
-                    e1 = min(c1, e0 + DW)
-                    group(R(d, e0 - c0, e1 - c0), [(R("nib", 0, 128), R("xh" + z, e0, e1)), (ib, R("xl" + z, e0, e1))])
-                act(R("ad" + z, c0, c1), R(d, 0, c1 - c0), AF.Abs)
-            for c0 in range(f0, f1, RW):
-                c1 = min(f1, c0 + RW)
-                scan(R("mn" + z, c0, c1), R("rp16", 0, c1 - c0), R("xh" + z, c0, c1), 0.0, A.max, A.min)
-                scan(R("ms" + z, c0, c1), R("rn16", 0, c1 - c0), R("xl" + z, c0, c1), 0.0, A.min, A.max)
+                group(d, [(R("nib", 0, 128), R("xh" + z, f0, f1)), (ib, R("xl" + z, f0, f1))])
+            act(R("ad" + z, f0, f1), d, AF.Abs)
+            scan(R("mn" + z, f0, f1), R("rp16", 0, f1 - f0), R("xh" + z, f0, f1), 0.0, A.max, A.min)
+            scan(R("ms" + z, f0, f1), R("rn16", 0, f1 - f0), R("xl" + z, f0, f1), 0.0, A.min, A.max)
             for d0, d1 in DP:
                 if i0 < d1 <= i1:
                     group(R(pa, d0, d1), [(R("l1", 15 - r_, 143 - r_), R("ad" + z, 16 * d0 + r_, 16 * d1, 16)) for r_ in range(16)])
-                    if RE == "S":
-                        act(R("r" + z, d0, d1), R(pa, d0, d1), AF.Relu, bias=C("nb" + z), scale=8192.0)
-                    else:
-                        ts(R("r" + z, d0, d1), R(pa, d0, d1), C("nb" + z), 8192.0, A.is_gt, A.mult)
-        c = xn_of(s, t + 1)
+        act(R("r" + z, 0, H), R(pa, 0, H), AF.Relu, bias=C("nb" + z), scale=8192.0)
+        c = (k + 2) * H
         xn = R("xn", c, c + H)
         group(R(pb, H, 2 * H), [(R("hib", 0, 128), R("mn" + z, 15, 2048, 16)), (R("hib", 0, 128), R("ms" + z, 15, 2048, 16))])
         ts(xn, R(pb, H, 2 * H), MAGIC, -MAGIC, A.add, A.add)
+
+        def both():
+            for h in range(2):
+                group(R(pb, H + H * h, 2 * H + H * h), [(R("rpb", 128 * h, 128 * h + 128), xn)])
+            act(R(xb, B, B + NP), R(pb, H, 3 * H), AF.Copy)
         if not last:
-            lists(s, t + 1)
-            if "x" in REP:
-                spread(xb, B, "xn", c, "rx" + z)
-            else:
-                for h in range(2):
-                    group(R(pb, H + H * h, 2 * H + H * h), [(R("rpb", 128 * h, 128 * h + 128), xn)])
-                act(R(xb, B, B + NP), R(pb, H, 3 * H), AF.Copy)
+            lists(s, t + 1, both)
         group(R(pa, 128, 384), [(ib, R("ow", 0, 256)), (R("r" + z, 0, H), R("ng2", 0, 256))])
-        if NQE == "S":
+        if k < LAST:
             act(R("nq" + z, 64, 320), R(pa, 128, 384), AF.Relu)
         else:
             ts(R("nq" + z, 64, 320), R(pa, 128, 384), 0.0, None, A.max)
@@ -550,23 +608,12 @@ def rank_program(g, core, T, topo):
             if last:
                 store(T.yx[rows, Y + H * h:Y + H * h + H], R("xn", c, c + H, p=HALF[h]))
         if not last:
-            if "k" in REP:
-                n8 = R("n8" + z, 0, H)
-                ts(n8, xn, th[s], 8192.0, A.is_lt, A.mult)
-                for j, mat in enumerate((R("nib", 0, 128), ib)):
-                    group(R(pb, H + H * j, 2 * H + H * j), [(ib, R("cns", 0, H)), (mat, n8)])
-                for j, tab in enumerate(("kh", "kl")):
-                    tt(R("kn" + z, H * j, H * j + H), R(pb, H + H * j, 2 * H + H * j), an, A.add)
-                    spread(tab + z, B, "kn" + z, H * j, "r" + tab + z)
-            else:
-                ts(R("n8" + z, 0, NP), R(xb, B, B + NP), th[s], 8192.0, A.is_lt, A.mult)
-                for h in range(2):
-                    group(R(pb, H * h, H * h + H), [(ib, R("cns", 0, H)), (R("rpf", 128 * h, 128 * h + 128), an)])
-                tt(R("kh" + z, B, B + NP), R(pb, 0, NP), R("n8" + z, 0, NP), A.subtract)
-                tt(R("kl" + z, B, B + NP), R(pb, 0, NP), R("n8" + z, 0, NP), A.add)
-            ts(R("n8" + z, NP, G), R(xb, B + NP, B + G), th[s], 8192.0, A.is_lt, A.mult)
-            tt(R("kh" + z, B + NP, B + G), mc, R("n8" + z, NP, G), A.subtract)
-            tt(R("kl" + z, B + NP, B + G), mc, R("n8" + z, NP, G), A.add)
+            ts(R("n8" + z, 0, NP), R(xb, B, B + NP), th[s], 8192.0, A.is_lt, A.mult)
+            ts(R("ek" + z, H, 2 * H), an, -SH, None, A.add)
+            for h in range(2):
+                group(R(pb, H * h, H * h + H), [(R("rph", 128 * h, 128 * h + 128), R("ek" + z, H, 2 * H))])
+            tt(R("kh" + z, B, B + NP), R(pb, 0, NP), R("n8" + z, 0, NP), A.subtract)
+            tt(R("kl" + z, B, B + NP), R(pb, 0, NP), R("n8" + z, 0, NP), A.add)
             if s:
                 group(R(pa, 464, 472), [(R("onesb", 0, 128), R("nq%d" % j, 64, 192, 16)) for j in range(2)])
                 node("V", [lambda: g.vector.tensor_reduce(C("cs")[0], T[pa][:, 464:472], AxisListType.X, A.add)],
@@ -574,7 +621,10 @@ def rank_program(g, core, T, topo):
                 ts(C("cia"), C("cs"), -1.0, 2048.0, A.mult, A.add)
                 ts(C("cja"), C("cia"), 15, None, A.bitwise_and)
                 for j in range(2):
-                    ts(C("nb%d" % j), C("cja"), LIM, C("nt%d" % j), A.mult, A.add)
+                    ts(C("nb%d" % j), C("cja"), -8192.0, C("nt%d" % j), A.mult, A.add)
+            ts(R("n8" + z, NP, G), R(xb, B + NP, B + G), th[s], 8192.0, A.is_lt, A.mult)
+            tt(R("kh" + z, B + NP, B + G), mc, R("n8" + z, NP, G), A.subtract)
+            tt(R("kl" + z, B + NP, B + G), mc, R("n8" + z, NP, G), A.add)
         c0 = NP if last else 0
         store(T.yx[rows, Y + c0:Y + G], R(xb, B + c0, B + G, p=LO))
 
@@ -582,56 +632,12 @@ def rank_program(g, core, T, topo):
         for s in range(2):
             step(s, t)
 
-    rest = [0.0] * len(nodes)
-    users = [[] for _ in nodes]
-    for k in range(len(nodes) - 1, -1, -1):
-        nd = nodes[k]
-        rest[k] += nd["cost"] + nd["lat"]
-        for p in nd["ps"]:
-            rest[p] = max(rest[p], rest[k] + WAKE)
-            users[p].append(k)
-    STATS["rest"], STATS["nodes"] = list(rest), nodes
-    for k in range(len(nodes) - 1, -1, -1):
-        nd = nodes[k]
-        if nd["step"] >= 0:
-            rest[k] -= STEPB * (nd["step"] // 2) + SOFF * (nd["step"] % 2)
-        else:
-            rest[k] = nd["cost"] + nd["lat"] + max([rest[u] + WAKE for u in users[k]] + [-1000.0])
-    for k in loads:
-        rest[k] = 1e6 - k
-    left = [len(nd["ps"]) for nd in nodes]
-    ready_at = [0.0] * len(nodes)
-    ready = {q: [] for q in list(queues) + ["R"]}
-    free = {q: 0.0 for q in ready}
-    for k, nd in enumerate(nodes):
-        if not left[k]:
-            ready[nd["q"]].append(k)
-    order = []
-    while len(order) < len(nodes) and "order" not in STATS:
-        best = None
-        for q, lst in ready.items():
-            if lst:
-                at = max(free[q], min(ready_at[k] for k in lst))
-                if best is None or at < best[0]:
-                    best = (at, q)
-        at, q = best
-        k = max((k for k in ready[q] if ready_at[k] <= at + DELTA), key=lambda k: (rest[k], -k))
-        at = max(at, ready_at[k])
-        ready[q].remove(k)
-        order.append(k)
-        done = at + nodes[k]["cost"]
-        free[q] = at if q == "R" else done
-        for u in users[k]:
-            ready_at[u] = max(ready_at[u], done + nodes[k]["lat"] + WAKE)
-            left[u] -= 1
-            if not left[u]:
-                ready[nodes[u]["q"]].append(u)
     if "order" not in STATS:
-        STATS["order"] = shift(nodes, users, tighten(nodes, users, order))
+        STATS["nodes"], STATS["order"] = nodes, schedule(nodes)
     order = loads + [k for k in STATS["order"] if k not in loads]
 
     count, waited, snap, token = {}, {}, {}, {}
-    known = {q: {} for q in ready}
+    known = {q: {} for q in "VSTGYR"}
     for k in order:
         nd = nodes[k]
         q, sem = nd["q"], nd["sem"]

@@ -1,3 +1,5 @@
+import math
+
 from concourse.bass import DstId, RemoteDMATransfer
 from concourse.mybir import AluOpType, ActivationFunctionType, AxisListType
 
@@ -7,42 +9,48 @@ TOT = S + RO * G
 KT = TOT - G
 H = NP // 2
 LAST = 2 * RO - 1
-NCH = [(0, 64), (64, 128)]
-VP = [(0, 32), (32, 64), (64, 96), (96, 128)]
-VPL = [(0, 32), (32, 64), (64, 96), (96, 128)]
-XL = ["SSSS"] * 8
-XH = ["SSSV"] + ["SSVV"] * 7
-DP = [(0, 64), (64, 128)]
-CPE = "SSSSSSSS"
-FUS = 0
-PD = ["pd0", "pd1", "pm"]
-RW = 512
-WAKE = 0.2
-GCY = 1.56
-SCY = 3.0
+NCH = [[(0, 64), (64, 128), (128, 192), (192, 256)]] * 8
+VP = [[(64, "S"), (64, "S"), (32, "S"), (32, "S"), (64, "V")]] * 8
+AB = [[64, 64, 32, 32, 64]] * 8
+ZT = "TVVV"
+KE = "V"
+OUT = {7: [(0, 7), (7, 8)]}
+CPE = "SSSSSSSV"
+KA = (1, 1, 1, 1)
+PD = ["pd0", "pd1", "pd2"]
+BN, BD, BM, BX, BP, BL = "pn", "pq", "pm", "px", "pc", "px"
+NAMES = {2: "pq", 3: "pd2", 0: "pm", 1: "pc"}
+RW = 1024
+CASES = [(1.56, 3.0, 0.2, 2.3, 2.2), (1.4, 3.0, 0.26, 2.8, 2.6), (1.2, 2.4, 0.16, 2.0, 1.9)]
 CY = 0.00083
-MLAT = 2.6
-HALFGEN = 10.1
-FIRST = 10.5
-TRIES = (1500, 1200)
-SEED = 1
-WHEN = {
-    "S": "la1=0 ha1=1.2 la2=1.9 ha2=2.8 xl1=4.1 xl2=4.9 xh1=5.6 xh2=6.5 xl3=7.3 xh3=7.7 xl4=8 xh4=8.2 ad1=8.7 xl5=8.8 ad2=9.2 ad3=9.7 ad4=10.9"
-         " ad5=11.2 r1=12.8 nq1=13.7 xb1=14 yf1=16.4",
-    "V": "lb1=1 z1=1.7 ls1=1.9 hb1=2.1 lo1=2.8 lb2=2.9 hl1=3.6 hs1=3.7 hb2=3.9 lo2=4.7 z2=4.8 hl2=5.3 hs2=5.3 ls2=5.8 ms1=6.2 lo3=6.6 lo4=6.6"
-         " hl3=6.9 ms2=7 xh1=7.2 ms3=8.2 xh2=8.6 xh3=8.7 xh4=8.8 df1=9.2 mn1=9.3 mn3=9.9 mn2=10.1 ms4=10.3 ms5=10.4 mn4=10.9 mn5=10.9 xn1=11.9 nq1=13.6"
-         " off1=14.7 yf1=14.8 mw1=15 ui1=15.3 uj1=15.7 mo1=15.8 uo1=16.1 n81=16.2 fb1=16.8 fc1=16.8 ek1=16.9 ab1=18 el1=18.1 cia1=18.1"
-         " ek2=18.5 cja1=18.6 n82=19.4 fc2=19.7 kl2=19.7 kl1=19.8 kh2=20.7 kh1=20.8 fc3=22",
-    "T": "pb1=2.3 pa1=4.3 pb3=5.7 pb2=6.2 pd1=6.5 pd2=7.6 pd3=8.4 pb5=9.5 pd4=9.6 pd5=10.1 pb4=10.4 pa2=10.6 pb6=11.4 pa3=11.6 pc1=12.6 pb7=12.8"
-         " pa4=13.1 pb8=13.5 pb9=13.7 pc2=13.8 pa5=14.2 pa6=15.5 pa7=16.1 pb10=17.5 pb11=17.6 pb13=19.4 pb12=19.5",
-    "G": "-1=16.1", "R": "xb1=16.6", "Y": "-1=18.3 -2=18.3 -3=19.4 -4=19.5 -5=19.6",
+FIRST = 2.0
+SEED, HEAT = 1, 0.0015
+WINDOWS = [(0.075, 0.36, 70000), (0.74, 1.1, 45000), (0.05, 0.3, 20000)]
+SHIFT = [0.0] * 7 + [-1.0]
+TAIL = {"Y": "-1' -2' " + " ".join("-%d" % j for j in range(3, 17)) + " -1 -2 -17 -18 -19 -20"}
+FRONT = {}
+HEAD = {
+    "G": "pix1 c161 jx1 jm1 jq1 cu1 j641 jd1 rn81 cbig1 rn161 mnm1 nq1 ow1 none81 mw1 kt1",
+    "V": "onesb1 fc1 pi3 io1 fc4 fc8 nbias1 nbias2 ipad1 pi1 pi6 sel1 fc2 fc7 sel2 fc10 i31 sel3 pi5 pi4 sel4 rowf1 rowf2 kdh1 rowf3 rowf4 gq1 gq2"
+         " far1 rz1 kdh2 rep1 fc6 fc5 lv1 fc12 uc1 xv1 fc13 kt1 fc14 xv2 fc15 kt2 lay1 xv3 yf1 fc16 xv4 ui1 lay2 uj1 kt3 uo1 kdw1 kt4 ek1 xv5"
+         " xv6 el1 el2 xv7 xv8",
+    "S": "pq1 pd1 pm1 pc1 kdw1 kdw2 kdw3 kdw4 kdw5 kdw6 kdw7 kt1 kt2 kt3 kt4",
+    "T": "pn1 pd1 pn2 pd2 pd3 pd4 pn3 pn4 pd5 pd6 px1 px2 pd7 pd8 px3 px4 pn5 pn6 pd9 pd10 pd11 pd12 px5 px6",
+}
+TURNS = {
+    "V": "z1' n81'' lh1' ks2' z2' hl1' kb3' nq1'' lh2' z3' yf1'' hl2' off1'' ks3' mw1'' ui1'' kb4' uj1'' lh3' ab1'' ks4' uo1'' ms1' hl3' lh4'"
+         " ek1'' hl4' kt1'' xv1' nm1'' xb1'' el1'' kt2'' ms5' ms4' ms3' el2'' fc1'' ms2' an1' cia1'' kb1 xn1' cja1'' ks1 fc3'' fc2'' kb2",
+    "S": "r1'' ka4' nq1'' xv1' xv2' ad1' xv3' ad2' xv4' ad3' ka1 ad5' ad4' ka2 ka3",
+    "T": "pn1' pm1'' pn2' pm2'' px4'' px6'' pn3' pn4' px3'' px5'' pm3'' pc2'' pc1'' pn5' pn6' pd1' pd2' pn7' pc4'' pn8' pc3'' pd3' pd4' px7''"
+         " px8'' pd5' pm4'' pq1' pd7' pd8' pm5'' pd6' pq2' px2' px1' pq3' pq4'",
+    "Y": "xb1' -1''", "G": "-1''",
 }
 STATS = {}
 MAGIC = 12582912.0
 SH = 1792.0
 F16, BF, F32 = "float16", "bfloat16", "float32"
 
-COLS = ["pixf", "prf", "pdf", "lom", "him", "zc", "etaf", "cs", "cm", "nb0", "nb1", "nt0", "nt1"]
+COLS = ["pixf", "prf", "pdf", "etaf", "p4f", "p6f", "plf", "sg", "ns", "lof", "zc", "tl", "te", "cs", "cm", "nb0", "nb1", "nt0", "nt1"]
 
 
 def _sb(n, dt):
@@ -51,56 +59,57 @@ def _sb(n, dt):
 
 SCRATCH = {
     "kdn": _sb(512, "int32"), "kdh": _sb(512, F16), "kdw": _sb(U, F32), "sel": _sb(1024, F16),
-    "onesb": _sb(512, BF), "io": _sb(512, F32), "cbig": _sb(256, BF), "jj": _sb(256, BF), "cb": _sb(1024, BF), "df": _sb(512, BF),
-    "ab": _sb(2 * RO * H, F32), "xn": _sb(2 * (RO + 1) * H, BF), "mw": _sb(2 * RO * 768, BF), "mo": _sb(2 * RO * CAP, BF),
-    "mnm": _sb(RO * 128, F32),
-    "rn8": _sb(RW, BF), "rp8": _sb(RW, BF), "rn16": _sb(RW, BF), "rp16": _sb(RW, BF),
-    "ipad": _sb(144, BF), "nib": _sb(128, BF), "hib": _sb(128, F16), "ih": _sb(128, F16), "bigh": _sb(128, F16),
-    "ilo": _sb(144, F16), "ihi": _sb(144, F16), "rpb": _sb(256, BF), "rph": _sb(256, F16), "i3": _sb(4, F32),
-    "jd": _sb(128, BF), "jm": _sb(128, BF), "g2": _sb(128, BF), "ng2": _sb(256, BF), "l1": _sb(144, BF), "ow": _sb(256, BF),
+    "onesb": _sb(512, BF), "io": _sb(512, F32), "nbias": _sb(8, F32), "cbig": _sb(256, BF), "jx": _sb(256, BF), "j64": _sb(144, BF),
+    "an": _sb(2 * RO * H, F32), "xn": _sb(2 * RO * H, BF), "mw": _sb(2 * RO * 768, BF), "rx": _sb(2 * RO * H, BF),
+    "mnm": _sb(RO * 128, F32), "bi": _sb(RO * H, F32), "rn4": _sb(RW, BF), "rn8": _sb(RW, BF), "rn16": _sb(RW, BF),
+    "ipad": _sb(128, BF), "ih": _sb(128, F16), "if": _sb(128, F32), "bigh": _sb(128, F16), "rp": _sb(128, BF), "rz3": _sb(192, BF), "hx": _sb(192, F16),
+    "nl": _sb(192, F16), "lay": _sb(4 * 144, F16), "i3": _sb(4, F16),
+    "jd": _sb(128, BF), "jm": _sb(128, BF), "g2": _sb(128, BF), "ng2": _sb(256, BF), "l1": _sb(208, BF), "ow": _sb(256, BF),
     "wa": _sb(128, BF), "wb": _sb(128, BF), "nbef": _sb(8, BF), "none8": _sb(8, BF), "ich": _sb(8, BF), "c16": _sb(8, F32), "uc": _sb(8, F32),
-    "far": _sb(128, BF), "rz": _sb(128, BF), "csh": _sb(128, BF),
-    "rowi": _sb(128, "int32"), "rowf": _sb(256, F32), "rep": _sb(8, F32),
-    "fc": _sb(len(COLS), F32), "pix": _sb(1, "int32"), "pr": _sb(1, "int32"), "pe_": _sb(1, "int32"), "pdi": _sb(1, "int32"),
-    "cia": _sb(1, "int32"), "cja": _sb(1, "int32"),
+    "jq": _sb(192, BF), "gq": _sb(384, BF), "cu": _sb(8, F32), "ab": _sb(2 * RO * H, F16), "rph": _sb(256, BF), "rps": _sb(256, F16), "far": _sb(32, BF), "rz": _sb(128, BF),
+    "rowi": _sb(128, "int32"), "rowf": _sb(256, F16), "rep": _sb(8, F32),
+    "fc": _sb(len(COLS), F32), "pix": _sb(1, "int32"), "pi": _sb(8, "int32"), "cia": _sb(1, "int32"), "cja": _sb(1, "int32"),
 }
-for _n in ("pd0", "pd1", "pa0", "pa1", "pb0", "pb1", "pc", "pm"):
+for _n in ("pd0", "pd1", "pd2", "pc", "pn", "pq", "pm", "px"):
     SCRATCH[_n] = ("psum", [128, 512], F32)
 for _s in "01":
     SCRATCH.update({
-        "xb" + _s: _sb(TOT, BF), "kh" + _s: _sb(KT, F32), "kl" + _s: _sb(KT, F32), "lw" + _s: _sb(128, BF),
-        "ha" + _s: _sb(1024, F32), "la" + _s: _sb(1024, F32), "hb" + _s: _sb(1024, F16), "lb" + _s: _sb(1024, F16),
-        "hs" + _s: _sb(1024, F16), "ls" + _s: _sb(1024, F16), "z0" + _s: _sb(H, F16), "lo" + _s: _sb(2 * H, F16),
-        "hl" + _s: _sb(2 * H, "uint16"),
-        "xl" + _s: _sb(2048, BF), "xh" + _s: _sb(2048, BF), "ad" + _s: _sb(2048, BF), "mn" + _s: _sb(2048, F16), "ms" + _s: _sb(2048, F16),
-        "r" + _s: _sb(H, BF), "fb" + _s: _sb(H, F32), "nq" + _s: _sb(320, BF), "off" + _s: _sb(8, "uint16"), "n8" + _s: _sb(G, BF),
+        "xb" + _s: _sb(TOT, BF), "kt" + _s: _sb(KT, F32), "lv" + _s: _sb(384, BF),
+        "ka" + _s: _sb(2048, F32), "kb" + _s: _sb(2048, F16), "ks" + _s: _sb(2048, F16),
+        "z" + _s: _sb(NP, F16), "lh" + _s: _sb(NP, F16), "hl" + _s: _sb(NP, "uint16"),
+        "xv" + _s: _sb(4096, BF), "ad" + _s: _sb(2048, BF), "ms" + _s: _sb(4096, F16),
+        "r" + _s: _sb(H, BF), "nq" + _s: _sb(320, BF), "off" + _s: _sb(8, "uint16"), "nm" + _s: _sb(128, BF),
+        "n8" + _s: _sb(H, BF),
         "ui" + _s: _sb(8, "int32"), "uj" + _s: _sb(8, "int32"), "uo" + _s: _sb(8, "uint16"),
-        "yf" + _s: _sb(H, F32), "ek" + _s: _sb(2 * H, F16), "el" + _s: _sb(H, "uint16"),
+        "yf" + _s: _sb(H, F32), "ek" + _s: _sb(H, F16), "el" + _s: _sb(NP, "uint16"),
     })
 
-SEMAPHORES = ["sv", "ss", "st", "sg", "rl", "out"] + ["ma%d" % k for k in range(2 * RO)] + ["l%d" % k for k in range(8)]
+SEMAPHORES = ["sv", "ss", "st", "sg", "rl", "out", "ga"] + [x + str(k) for x in ("ma", "l", "sx", "sk") for k in range(2 * RO)]
 PSUM = [n for n, v in SCRATCH.items() if v[0] == "psum"]
 
 
-def place(nodes, key, chain):
-    n = len(nodes)
-    users, left, after = [[] for _ in nodes], [len(nd["ps"]) for nd in nodes], {}
-    for k, nd in enumerate(nodes):
-        for p in nd["ps"]:
+def prices(nodes, case):
+    gc, sc, wake, mail, dma = case
+    cost = [nd["cost"][0] + CY * (nd["cost"][1] + gc * nd["cost"][2] + sc * nd["cost"][3]) for nd in nodes]
+    lat = [{"m": mail + FIRST * (nd["step"] in (0, LAST - 1)), "d": dma, "g": -wake}.get(nd["lat"], nd["lat"]) for nd in nodes]
+    return cost, [c + x for c, x in zip(cost, lat)], wake
+
+
+def place(q, before, cost, out, key):
+    n = len(q)
+    users, left = [[] for _ in q], [len(x) for x in before]
+    for k in range(n):
+        for p in before[k]:
             users[p].append(k)
-    for a, b in zip(chain, chain[1:]):
-        after[a] = b
-        left[b] += 1
     ready, at, held, busy = [0.0] * n, [0.0] * n, set(), {}
     for k0 in sorted(range(n), key=lambda k: (key[k], k)):
         todo = [] if left[k0] else [k0]
         held.add(k0)
         while todo:
             k = todo.pop()
-            nd = nodes[k]
-            t, d = ready[k], nd["cost"]
-            if nd["q"] != "R":
-                lst = busy.setdefault(nd["q"], [])
+            t, d = ready[k], cost[k]
+            if q[k] != "R":
+                lst = busy.setdefault(q[k], [])
                 j = len(lst)
                 while j and lst[j - 1][1] > t:
                     j -= 1
@@ -109,154 +118,218 @@ def place(nodes, key, chain):
                     j += 1
                 lst.insert(j, (t, t + d))
             at[k] = t
-            for u, e in [(u, t + d + nd["lat"] + WAKE) for u in users[k]] + ([(after[k], t + d)] if k in after else []):
-                ready[u] = max(ready[u], e)
+            for u in users[k]:
+                ready[u] = max(ready[u], t + out[k])
                 left[u] -= 1
                 if not left[u] and u in held:
                     todo.append(u)
     return at
 
 
-def improve(nodes, order, tries, fixed):
+def schedule(nodes):
     n = len(nodes)
-    cost, q, step, kind = ([nd[x] for nd in nodes] for x in ("cost", "q", "step", "kind"))
-    out = [nd["cost"] + nd["lat"] + WAKE for nd in nodes]
-    fin = [nd["cost"] + nd["lat"] for nd in nodes]
-    who = {(step[k], q[k], kind[k]): k for k in range(n)}
-    reach, suc, npre = [0] * n, [[] for _ in nodes], [0] * n
+    q, step, kind = ([nd[x] for nd in nodes] for x in ("q", "step", "kind"))
+    reach, suc, pre = [0] * n, [[] for _ in nodes], [[] for _ in nodes]
     for k, nd in enumerate(nodes):
         for p in nd["ps"]:
             reach[k] |= reach[p]
         for p in nd["ps"]:
             if not reach[k] >> p & 1:
                 suc[p].append(k)
-                npre[k] += 1
+                pre[k].append(p)
         for p in nd["ps"]:
             reach[k] |= 1 << p
-    prv, nxt, last = [-1] * n, [-1] * n, {}
-    for k in order:
-        if q[k] != "R":
-            prv[k] = last.get(q[k], -1)
-            if prv[k] >= 0:
-                nxt[prv[k]] = k
-            last[q[k]] = k
-    seed = [SEED]
-    mails = [k for k in range(n) if q[k] == "R"]
+    npre = [len(x) for x in pre]
+    cases = [prices(nodes, c) for c in CASES]
+    cases = [(cost, fin, [f + wake for f in fin]) for cost, fin, wake in cases]
 
-    def rnd(m):
-        seed[0] = (seed[0] * 6364136223846793005 + 1442695040888963407) % 2 ** 64
-        return (seed[0] >> 33) % m
+    def links(order):
+        prv, nxt, last = [-1] * n, [-1] * n, {}
+        for k in order:
+            if q[k] != "R":
+                prv[k] = last.get(q[k], -1)
+                if prv[k] >= 0:
+                    nxt[prv[k]] = k
+                last[q[k]] = k
+        return prv, nxt
 
-    def forward(prv, nxt):
+    def forward(prv, nxt, bare=False):
         left = [npre[k] + (prv[k] >= 0) for k in range(n)]
-        seq, head, end = [k for k in range(n) if not left[k]], [0.0] * n, 0.0
+        seq = [k for k in range(n) if not left[k]]
         for k in seq:
-            h = head[k]
-            e = h + out[k]
-            if h + fin[k] > end:
-                end = h + fin[k]
             for u in suc[k]:
-                if e > head[u]:
-                    head[u] = e
                 left[u] -= 1
                 if not left[u]:
                     seq.append(u)
             u = nxt[k]
             if u >= 0:
-                e = h + cost[k]
-                if e > head[u]:
-                    head[u] = e
                 left[u] -= 1
                 if not left[u]:
                     seq.append(u)
         if len(seq) < n:
             return None
-        return end + 0.3 * sum(head[k] for k in mails) / len(mails), end, head, seq
-
-    def put(prv, nxt, k, a):
-        p, x = prv[k], nxt[k]
-        if p >= 0:
-            nxt[p] = x
-        if x >= 0:
-            prv[x] = p
-        b = nxt[a]
-        prv[k], nxt[k], nxt[a] = a, b, k
-        if b >= 0:
-            prv[b] = k
-
-    cur = forward(prv, nxt)
-    best, until, since = (cur, list(prv), list(nxt)), {}, 0
-    for it in range(tries):
-        _, end, head, seq = cur
-        tail = [0.0] * n
-        for k in reversed(seq):
-            tail[k] = max([fin[k], cost[k] + tail[nxt[k]] if nxt[k] >= 0 else 0.0] + [out[k] + tail[u] for u in suc[k]])
-        k = [x for x in seq if head[x] == 0.0 and tail[x] > end - 1e-9]
-        k = k[rnd(len(k))]
-        runs = [[k]]
-        while True:
-            ways = [u for u in suc[k] if abs(out[k] + tail[u] - tail[k]) < 1e-9]
-            u = nxt[k]
-            if u >= 0 and abs(cost[k] + tail[u] - tail[k]) < 1e-9 and (not ways or rnd(2)):
-                runs[-1].append(u)
-            elif ways:
-                u = ways[rnd(len(ways))]
-                runs.append([u])
-            else:
-                break
-            k = u
-        moves = set()
-        for run in runs:
-            for u, v in [(x, run[-1]) for x in run[-9:-1]] + [(run[0], x) for x in run[1:9]]:
-                if not reach[v] >> u & 1 and (q[u] not in fixed or min(step[u], step[v]) < 0 or max(step[u], step[v]) == LAST):
-                    moves |= {(u, v, True), (u, v, False)}
-        moves, pick = sorted(moves), None
-        for _ in range(min(10, len(moves))):
-            u, v, late = moves.pop(rnd(len(moves)))
-            every = min(step[u], step[v]) >= 0 and rnd(8) > 0
-            p2, n2 = list(prv), list(nxt)
-            for d in range(-LAST, LAST + 1) if every else (0,):
-                a, b = who.get((step[u] + d, q[u], kind[u])), who.get((step[v] + d, q[u], kind[v]))
-                if a is None or b is None or (d and min(step[u], step[v]) + d < 0) or not 0 <= head[b] - head[a] <= 4.0:
+        heads, ends = [], []
+        for cost, fin, out in cases:
+            head = [0.0] * n
+            for k in seq:
+                if bare and step[k] < 0:
                     continue
-                if late:
-                    put(p2, n2, a, b)
-                elif p2[a] >= 0 and p2[a] != b:
-                    put(p2, n2, b, p2[a])
-            c = forward(p2, n2)
-            if c is None or (until.get((q[u], kind[u], kind[v]) if every else (u, v), -1) > it and c[0] >= best[0][0]):
+                h = head[k]
+                e = h + out[k] - (FIRST if bare and q[k] == "R" and step[k] == 0 else 0.0)
+                for u in suc[k]:
+                    if e > head[u]:
+                        head[u] = e
+                u = nxt[k]
+                if u >= 0 and h + cost[k] > head[u]:
+                    head[u] = h + cost[k]
+            heads.append(head)
+            ends.append(max(h + f for h, f in zip(head, fin)))
+        return sum(e / w for e, w in zip(ends, weight)), ends, heads, seq
+
+    weight = [max(sum(c for c, x in zip(cost, q) if x == e) for e in "VST") for cost, _, _ in cases]
+
+    who = {(step[k], q[k], kind[k]): k for k in range(n)}
+
+    def timed(turns, shift):
+        cost, fin, out = cases[0]
+        row = [who.get((j - x.count("'"), e, x.rstrip("'"))) for j in range(LAST + 4) for e, s in turns.items() for x in s.split()]
+        end = [who[(LAST - x.count("'"), e, x.rstrip("'"))] for e, s in TAIL.items() for x in s.split()]
+        front = [who[(x.count("+"), e, x.rstrip("+"))] for e, s in FRONT.items() for x in s.split()]
+        row = front + [k for k in row if k is not None and step[k] >= 0 and k not in end + front] + end
+        head = forward(*links(row + sorted(k for k in set(range(n)) - set(row) if step[k] >= 0)), True)[2][0]
+        key, row = [0.0] * n, {}
+        for k in range(n - 1, -1, -1):
+            if step[k] >= 0:
+                key[k] = head[k] + shift[step[k]]
+            else:
+                key[k] = min([20.0] + [key[u] - out[k] for u in suc[k]])
+                if cost[k] > 0.2:
+                    key[k] = row[q[k]] = min(key[k], row.get(q[k], 20.0) - cost[k])
+        row = [k for k in range(n) if nodes[k]["first"]] + [who[(-1, e, x)] for e, s in HEAD.items() for x in s.split()]
+        head = forward(*links(row))[2][0]
+        for k in row:
+            key[k] = head[k] - 100.0
+        at = place(q, pre, cost, out, key)
+        t0 = min(at[k] - key[k] for k in range(n) if step[k] == 0 and q[k] == "S")
+        key = [key[k] + t0 if step[k] >= 0 else at[k] for k in range(n)]
+        for k in range(n):
+            key[k] = max([key[k]] + [key[p] for p in pre[k]])
+        c = links(sorted(range(n), key=lambda k: (not nodes[k]["first"], key[k] * (not nodes[k]["first"]), k)))
+        return (forward(*c),) + c
+
+    STATS["timed"], STATS["cases"], STATS["weight"], STATS["graph"] = timed, cases, weight, (forward, reach, pre, suc)
+    if not TURNS:
+        return list(range(n))
+    best = timed(TURNS, SHIFT)
+    STATS["placed"] = best[0][1]
+    seed = [SEED]
+
+    def rnd():
+        seed[0] = (seed[0] * 6364136223846793005 + 1442695040888963407) % 2 ** 64
+        return ((seed[0] >> 33) + 1) / 2.0 ** 31
+
+    def polish(state, lo, hi, tries):
+        (_, _, heads, seq), prv, nxt = state
+        spot = {k: j for j, k in enumerate(sorted(range(n), key=lambda k: (heads[0][k], seq.index(k))))}
+        win = sorted((k for k in seq if lo <= heads[0][k] < hi), key=spot.get)
+        ix = {k: j for j, k in enumerate(win)}
+        m, rows = len(win), {}
+        for k in win:
+            if q[k] != "R":
+                rows.setdefault(q[k], []).append(ix[k])
+        users = [[ix[u] for u in suc[k] if u in ix] for k in win]
+        need = [sum(p in ix for p in pre[k]) for k in win]
+        fixed = []
+        for (cost, fin, out), head, w in zip(cases, heads, weight):
+            tail = [0.0] * n
+            for k in reversed(seq):
+                tail[k] = max([fin[k], cost[k] + tail[nxt[k]] if nxt[k] >= 0 else 0.0] + [out[k] + tail[u] for u in suc[k]])
+            ends = {e: (prv[win[r[0]]], nxt[win[r[-1]]]) for e, r in rows.items()}
+            fixed.append(([max([0.0] + [head[p] + out[p] for p in pre[k] if p not in ix]) for k in win],
+                          [max([fin[k]] + [out[k] + tail[u] for u in suc[k] if u not in ix]) for k in win],
+                          {e: (head[a] + cost[a] if a >= 0 else 0.0, tail[b] if b >= 0 else 0.0) for e, (a, b) in ends.items()},
+                          [cost[k] for k in win], [out[k] for k in win], w))
+
+        def score(tight=False):
+            left, after = list(need), [-1] * m
+            for r in rows.values():
+                for a, b in zip(r, r[1:]):
+                    after[a] = b
+                    left[b] += 1
+            way = [j for j in range(m) if not left[j]]
+            for j in way:
+                for u in users[j]:
+                    left[u] -= 1
+                    if not left[u]:
+                        way.append(u)
+                u = after[j]
+                if u >= 0:
+                    left[u] -= 1
+                    if not left[u]:
+                        way.append(u)
+            if len(way) < m:
+                return None
+            total = 0.0
+            for ready, rest, ends, cost, out, w in fixed:
+                t = list(ready)
+                for e, r in rows.items():
+                    t[r[0]] = max(t[r[0]], ends[e][0])
+                for j in way:
+                    h = t[j]
+                    x = h + out[j]
+                    for u in users[j]:
+                        if x > t[u]:
+                            t[u] = x
+                    u = after[j]
+                    if u >= 0 and h + cost[j] > t[u]:
+                        t[u] = h + cost[j]
+                ways = sorted([a + b for a, b in zip(t, rest)] + [t[r[-1]] + cost[r[-1]] + ends[e][1] for e, r in rows.items()])
+                total += (ways[-1] + 0.02 * sum(ways[-10:])) / w
+                if tight:
+                    back = list(rest)
+                    for e, r in rows.items():
+                        back[r[-1]] = max(back[r[-1]], cost[r[-1]] + ends[e][1])
+                    for j in reversed(way):
+                        back[j] = max([back[j], cost[j] + back[after[j]] if after[j] >= 0 else 0.0] + [out[j] + back[u] for u in users[j]])
+                    hot.extend(j for j in free if t[j] + back[j] > ways[-1] - 0.05)
+            return total
+
+        free = [j for j in range(m) if q[win[j]] not in "RY" and not nodes[win[j]]["first"]]
+        now, hot = score(), []
+        keep = (now, {e: list(r) for e, r in rows.items()})
+        for it in range(tries):
+            if it % 25 == 0:
+                del hot[:]
+                score(True)
+            pool = hot if hot and rnd() < 0.6 else free
+            j = pool[int(rnd() * len(pool)) % len(pool)]
+            r = rows[q[win[j]]]
+            a = r.index(j)
+            b = a + int(1.0 - 2.0 * math.log(rnd())) * (1 if rnd() < 0.5 else -1)
+            if not 0 <= b < len(r) or nodes[win[r[b]]]["first"]:
                 continue
-            if pick is None or c[0] < pick[0][0]:
-                pick = (c, p2, n2, (q[u], kind[v], kind[u]) if every else (v, u))
-        since += 1
-        if pick is not None and pick[0][0] < cur[0] + 0.6:
-            cur, prv, nxt, back = pick
-            until[back] = it + 8 + rnd(8)
-            if cur[0] < best[0][0] - 1e-9:
-                best, since = (cur, list(prv), list(nxt)), 0
-        if since > 150:
-            cur, prv, nxt, since = best[0], list(best[1]), list(best[2]), 0
-    STATS["end"] = best[0][1]
-    return sorted(range(n), key=lambda k: (best[0][2][k], k))
+            r.insert(b, r.pop(a))
+            c = score()
+            if c is not None and c < now - HEAT * (1.0 - it / tries) * math.log(rnd()):
+                now = c
+                if c < keep[0]:
+                    keep = (c, {e: list(x) for e, x in rows.items()})
+            else:
+                r.insert(a, r.pop(b))
+        for r in keep[1].values():
+            for at, j in zip(sorted(spot[win[x]] for x in r), r):
+                spot[win[j]] = at
+        c = links(sorted(range(n), key=spot.get))
+        return (forward(*c),) + c
 
-
-def schedule(nodes):
-    n = len(nodes)
-    when = {q: dict((x.split("=")[0], float(x.split("=")[1])) for x in s.split()) for q, s in WHEN.items()}
-    key = [1e9] * n
-    for k in range(n - 1, -1, -1):
-        nd = nodes[k]
-        if nd["step"] >= 0:
-            key[k] = (FIRST + HALFGEN * (nd["step"] - 1) if nd["step"] else 0.0) + when[nd["q"]][nd["kind"]]
-        else:
-            key[k] -= nd["cost"] + nd["lat"] + WAKE
-        for p in nd["ps"]:
-            if nodes[p]["step"] < 0:
-                key[p] = min(key[p], key[k])
-    chain = sorted((k for k in range(n) if nodes[k]["q"] == "S" and nodes[k]["step"] >= 0), key=lambda k: (key[k], k))
-    at = place(nodes, key, chain)
-    order = sorted(range(n), key=lambda k: (at[k], k))
-    return improve(nodes, improve(nodes, order, TRIES[0], "S"), TRIES[1], "")
+    for lo, hi, tries in WINDOWS:
+        end = best[0][1][0]
+        c = polish(best, lo * end, hi * end, tries)
+        if c[0][0] <= best[0][0]:
+            best = c
+    STATS["end"], STATS["best"] = best[0][1], best
+    rank = {k: j for j, k in enumerate(best[0][3])}
+    return sorted(range(n), key=lambda k: (best[0][2][0][k], rank[k]))
 
 
 def rank_program(g, core, T, topo):
@@ -266,7 +339,7 @@ def rank_program(g, core, T, topo):
     A, AF = AluOpType, ActivationFunctionType
     queues = {"V": g.vector, "S": g.scalar, "T": g.tensor, "G": g, "Y": g.sync}
     own = {"V": "sv", "S": "ss", "T": "st", "G": "sg"}
-    parts, cur, seen = {}, [-1], {}
+    parts, cur, seen, opened = {}, [-1], {}, {}
 
     nodes, acc = [], {}
 
@@ -289,7 +362,7 @@ def rank_program(g, core, T, topo):
 
     bank = {n: [None, [], []] for n in PSUM}
 
-    def node(q, fns, ins, outs, cost, sem=None, inc=1, preds=(), lat=0.0):
+    def node(q, fns, ins, outs, cost, sem=None, inc=1, preds=(), lat=0.0, soft=()):
         k, ps = len(nodes), set(preds)
         early = []
         for regs in parts.get(k, ()):
@@ -311,15 +384,15 @@ def rank_program(g, core, T, topo):
         name = (outs[0][0] if outs else "-").rstrip("01")
         name = "pd" if name in PD else name
         seen[(cur[0], q, name)] = seen.get((cur[0], q, name), 0) + 1
-        nodes.append({"q": q, "fns": fns, "cost": cost, "sem": sem or own[q], "inc": inc, "ps": sorted(ps), "early": early, "before": before,
-                      "lat": lat, "step": cur[0], "kind": name + str(seen[(cur[0], q, name)]), "lab": outs[0][:3] if outs else ("-", 0, 0)})
+        nodes.append({"q": q, "fns": fns, "cost": cost, "sem": sem or own[q], "inc": inc, "ps": sorted(ps | set(soft)), "soft": set(soft) - ps, "early": early, "before": before,
+                      "lat": lat, "alone": False, "first": False, "step": cur[0], "kind": name + str(seen[(cur[0], q, name)])})
         return k
 
     def vcost(out, in_, *more):
         if len(in_[1]) > 1:
-            return 0.05 + in_[2] * GCY * CY
+            return (0.05, 0, in_[2], 0)
         two = all(SCRATCH[x[1][0][0]][2] in (BF, F16, "uint16") for x in (out, in_) + more)
-        return max(64, out[2] * (0.5 if two else 1)) * CY
+        return (0.0, max(64, out[2] * (0.5 if two else 1)), 0, 0)
 
     def scal(x, ins):
         if isinstance(x, tuple):
@@ -341,7 +414,7 @@ def rank_program(g, core, T, topo):
     def tt(out, in0, in1, op):
         ps = any(x[1][0][0] in PSUM for x in (in0, in1))
         node("V", [lambda: g.vector.tensor_tensor(out[0], in0[0], in1[0], op)], in0[1] + in1[1], out[1],
-             vcost(out, in0) if len(in0[1]) > 1 else max(64, out[2] * (1 if ps else 2)) * CY)
+             vcost(out, in0) if len(in0[1]) > 1 else (0.0, max(64, out[2] * (1 if ps else 2)), 0, 0))
 
     def scan(out, d0, d1, init, op0, op1):
         node("V", [lambda: g.vector.tensor_tensor_scan(out[0], d0[0], d1[0], init, op0, op1)], d0[1] + d1[1], out[1], vcost(out, d0, d1))
@@ -356,37 +429,49 @@ def rank_program(g, core, T, topo):
         if scale is not None:
             kw["scale"] = scal(scale, ins)
         node("S", [lambda: g.scalar.activation(out[0], in_[0], func, **kw)], ins, out[1],
-             0.065 + in_[2] * GCY * CY if len(in_[1]) > 1 else 0.04 + max(64, out[2]) * CY)
+             (0.065, 0, in_[2], 0) if len(in_[1]) > 1 else (0.04, max(64, out[2]), 0, 0))
 
-    def move(e, out, in_, add=0.0):
+    def move(e, out, in_, scale=None):
         if e == "S":
-            act(out, in_, AF.Copy, bias=add if add else None)
-        elif add:
-            ts(out, in_, add, None, A.add)
+            act(out, in_, AF.Copy, scale=scale)
+        elif scale is not None:
+            ts(out, in_, scale, None, A.mult)
         else:
             copy(out, in_)
 
-    def group(out, pairs):
-        fns, ins, cost = [], [], 0.0
-        for j, (l, r_) in enumerate(pairs):
-            parts.setdefault(len(nodes), []).append(l[1] + r_[1])
-            fns.append(lambda l=l, r_=r_, j=j: g.tensor.matmul(out[0], l[0], r_[0], j == 0, j == len(pairs) - 1))
-            ins += [x for x in l[1] + r_[1] if x not in ins]
-            cost += max(64, out[2]) * CY * (4 if SCRATCH[l[1][0][0]][2] == F32 else 1)
-        node("T", fns, ins, out[1], cost)
+    def group(out, pairs, cut=()):
+        for j0, j1 in zip((0,) + cut, cut + (len(pairs),)):
+            fns, ins, cost = [], [], 0.0
+            for j in range(j0, j1):
+                l, r_ = pairs[j]
+                parts.setdefault(len(nodes), []).append(l[1] + r_[1])
+                fns.append(lambda l=l, r_=r_, j=j: g.tensor.matmul(out[0], l[0], r_[0], j == 0, j == len(pairs) - 1))
+                ins += [x for x in l[1] + r_[1] if x not in ins]
+                cost += max(64, out[2]) * (4 if SCRATCH[l[1][0][0]][2] == F32 else 1)
+            name = out[1][0][0]
+            k = node("T", fns, ins, out[1], (0.0, cost, 0, 0), preds=opened.get(name, ()))
+            opened[name] = [k] if cut else []
+            if j0:
+                nodes[k]["before"].discard(k - 1)
+                nodes[k - 1]["lat"] = "g"
 
     loads = []
 
     def load(q, pairs, lat):
         outs = [x for o, _ in pairs for x in o[1]]
-        loads.append(node(q, [lambda o=o, i=i: queues[q].dma_start(o[0], i) for o, i in pairs], [], outs, 0.06 * len(pairs),
+        loads.append(node(q, [lambda o=o, i=i: queues[q].dma_start(o[0], i) for o, i in pairs], [], outs, (0.06 * len(pairs), 0, 0, 0),
                           sem="l%d" % len(loads), inc=16, lat=lat))
+        nodes[-1]["first"] = True
 
-    def store(out, in_):
-        node("Y", [lambda: g.sync.dma_start(out, in_[0])], in_[1], [], 0.06, sem="out", inc=16, lat=2.0)
+    def spread(pairs, sem):
+        node("Y", [lambda o=o, i=i: g.sync.dma_start(o[0], i[0]) for o, i in pairs], [x for _, i in pairs for x in i[1]],
+             [x for o, _ in pairs for x in o[1]], (0.06 * len(pairs), 0, 0, 0), sem=sem, inc=16, lat="d")
+
+    def store(out, in_, after=()):
+        node("Y", [lambda: g.sync.dma_start(out, in_[0])], in_[1], [], (0.06, 0, 0, 0), sem="out", inc=16, lat="d", preds=after)
 
     def iota(out, pattern, base, cm=0):
-        node("G", [lambda: g.iota(out[0], pattern, base, cm, allow_small_or_imprecise_dtypes=True)], [], out[1], 0.13 + 2 * out[2] * CY)
+        node("G", [lambda: g.iota(out[0], pattern, base, cm, allow_small_or_imprecise_dtypes=True)], [], out[1], (0.13, 2 * out[2], 0, 0))
 
     def gfill(out, c):
         iota(out, [[0, out[2]]], int(c))
@@ -394,104 +479,124 @@ def rank_program(g, core, T, topo):
     LO, HI = (0, 64), (64, 128)
     HALF = (LO, HI)
 
+    def to_half(name, h):
+        return R(name, 64 - 64 * h, 192 - 64 * h)
+
     load("S", [(R("rowi", 0, 128, p=(j, j + 1)), x[:, 0:1]) for j, x in enumerate((T.th, T.wt, T.tau))], 2.0)
-    load("Y", [(R("kdn", 0, 512), T.kd[:, :])], 2.6)
+    load("Y", [(R("kdn", 0, 256), T.kd[:, 0:U // 2])], 2.2)
+    load("Y", [(R("kdn", 256, 512), T.kd[:, U // 2:U])], 2.7)
     load("Y", [(R("xb0", S // 2, S, p=p), T.x0[0:64, S // 2:S]) for p in HALF], 3.5)
     load("Y", [(R("xb0", 0, S // 2, p=p), T.x0[0:64, 0:S // 2]) for p in HALF], 4.4)
     load("Y", [(R("xb1", 0, S, p=p), T.x0[64:128, :]) for p in HALF], 6.0)
 
-    ib = R("ipad", 8, 136)
+    ib = R("ipad", 0, 128)
     fill(R("onesb", 0, 512), 1.0)
-    names4 = ["pc", "pm", "pa0", "pa1"]
-    scan(R("io", 0, 512), R("onesb", 0, 512), R("onesb", 0, 512), -1.0, A.mult, A.add)
-    for b in range(4):
-        move("S", R(names4[b], 0, 512), R("io", 0, 512), 512.0 * b - SH)
-    node("G", [lambda: g.affine_select(T.ipad[:, 0:144], T.onesb[:, 0:144], [[-1, 144]], A.is_equal, 0.0, 8, 1)],
-         R("onesb", 0, 144)[1], R("ipad", 0, 144)[1], 0.17 + 288 * CY)
-    node("G", [lambda: g.iota(T.pix[:, 0:1], [[0, 1]], 0, 1)], [], C("pix")[1], 0.15)
+    node("G", [lambda: g.iota(T.pix[:, 0:1], [[0, 1]], 0, 1)], [], C("pix")[1], (0.15, 0, 0, 0))
+    iota(R("jx", 0, 256), [[1, 256]], 0)
     iota(R("jd", 0, 128), [[1, 8], [0, 16]], 0)
     iota(R("c16", 0, 8), [[16, 8]], 0)
     iota(R("jm", 0, 128), [[0, 8], [1, 16]], 0)
+    copy(C("pixf"), C("pix"))
+    for j, (fl, c, op) in enumerate((("prf", 15, A.bitwise_and), ("pdf", 4, A.arith_shift_right), ("etaf", 6, A.arith_shift_right),
+                                     ("p4f", 8, A.bitwise_and), ("p6f", 63, A.bitwise_and), ("plf", 48, A.bitwise_and))):
+        ts(R("pi", j), C("pix"), c, None, op)
+        copy(C(fl), R("pi", j))
+    ts(ib, R("jx", 0, 128), C("pixf"), None, A.is_equal)
+    ts(C("sg"), C("etaf"), 2.0, -1.0, A.mult, A.add)
+    ts(C("ns"), C("etaf"), -2.0, 1.0, A.mult, A.add)
+    ts(C("lof"), C("etaf"), -1.0, 1.0, A.mult, A.add)
+    scan(R("io", 0, 512), R("onesb", 0, 512), R("onesb", 0, 512), -1.0, A.mult, A.add)
+    ts(R("nbias", 0, 8), R("c16", 0, 8), 32.0, -SH, A.mult, A.add)
+    ts(R("nbias", 0, 8), R("nbias", 0, 8), C("sg"), None, A.mult)
+    for b, name in NAMES.items():
+        act(R(name, 0, 512), R("io", 0, 512), AF.Identity, bias=R("nbias", b), scale=C("sg"))
     copy(R("sel", 0, 128), ib)
     for w in (128, 256, 512):
         copy(R("sel", w, 2 * w), R("sel", 0, w))
-    for h in range(2):
-        for k in range(2):
-            move("S", R("rpb", 128 * h + 64 * k, 128 * h + 64 * k + 64), R("ipad", 8 + 64 * h, 72 + 64 * h))
-    copy(R("i3", 0, 3, p=(0, 3)), R("ipad", 8, 11, p=(0, 3)))
+    copy(R("i3", 0, 3, p=(0, 3)), R("ipad", 0, 3, p=(0, 3)))
     for s in range(2):
         for h in range(2):
-            copy(R("rowf", 128 * s + 64 * h, 128 * s + 64 * h + 64, p=(0, 3)), R("rowi", 64 * s, 64 * s + 64, p=(0, 3)))
-        group(R("pb0", 3 * s, 3 * s + 3), [(R("rowf", 128 * s, 128 * s + 128, p=(0, 3)), R("i3", 0, 3, p=(0, 3)))])
-    copy(R("rep", 0, 6), R("pb0", 0, 6))
+            ts(R("rowf", 128 * s + 64 * h, 128 * s + 64 * h + 64, p=(0, 3)), R("rowi", 64 * s, 64 * s + 64, p=(0, 3)), -2048.0, None, A.add)
+        group(R(BN, 3 * s, 3 * s + 3), [(R("rowf", 128 * s, 128 * s + 128, p=(0, 3)), R("i3", 0, 3, p=(0, 3)))])
+    ts(R("rep", 0, 6), R(BN, 0, 6), 2048.0, None, A.add)
     th = [R("rep", 0), R("rep", 3)]
-    copy(C("pixf"), C("pix"))
-    for name, fl, c, op in (("pr", "prf", 15, A.bitwise_and), ("pdi", "pdf", 4, A.arith_shift_right), ("pe_", "etaf", 6, A.arith_shift_right)):
-        ts(C(name), C("pix"), c, None, op)
-        copy(C(fl), C(name))
     ts(R("g2", 0, 128), R("jd", 0, 128), C("pdf"), None, A.is_equal)
-    gfill(R("l1", 0, 144), 0)
-    copy(R("l1", 15, 143, 16), R("g2", 0, 128, 16))
-    for s in range(2):
-        act(R("lw%d" % s, 0, 128), R("g2", 0, 128), AF.Copy, scale=R("rep", 3 * s + 1))
-    ts(R("far", 0, H), R("jm", 0, 128), C("prf"), -2097152.0, A.not_equal, A.mult)
+    ts(R("far", 0, 32), R("jm", 0, 32), C("prf"), -2097152.0, A.not_equal, A.mult)
     ts(R("rz", 0, H), R("jm", 0, 128), 0.0, None, A.not_equal)
-    ts(C("lom"), C("prf"), 8.0, None, A.is_lt)
-    ts(C("him"), C("prf"), 8.0, None, A.is_ge)
-    ts(R("ilo", 0, 144), R("ipad", 0, 144), C("lom"), None, A.mult)
-    ts(R("ihi", 0, 144), R("ipad", 0, 144), C("him"), None, A.mult)
     ts(C("zc"), C("etaf"), 128.0, C("prf"), A.mult, A.add)
     ts(R("ich", 0, 8), R("c16", 0, 8), C("zc"), None, A.add)
-    ts(R("uc", 0, 8), R("ich", 0, 8), 613.0, None, A.mult)
+    iota(R("cu", 0, 8), [[64, 2], [128, 2], [32, 2]], 0)
+    ts(C("tl"), C("prf"), 2.0, C("etaf"), A.mult, A.add)
+    ts(R("uc", 0, 8), R("cu", 0, 8), C("tl"), 613.0, A.add, A.mult)
+    iota(R("j64", 0, 128), [[0, 2], [1, 64]], 0)
+    ts(C("te"), C("etaf"), 8.0, C("p6f"), A.mult, A.add)
+    ts(C("te"), C("te"), C("p4f"), None, A.subtract)
+    for L in range(2):
+        ts(C("cs"), C("p4f"), 8.0 * L, None, A.is_equal)
+        ts(R("lay", H * L, H * L + H), R("j64", 0, 128), C("te"), C("cs"), A.is_equal, A.mult)
 
-    ts(R("kdh", 0, 512), R("kdn", 0, 512), -2048.0, None, A.add)
+    for j in range(2):
+        ts(R("kdh", 256 * j, 256 * j + 256), R("kdn", 256 * j, 256 * j + 256), -2048.0, None, A.add)
     for j in range(8):
-        b = ("pd0", "pd1", "pb1")[j % 3]
-        group(R(b, 0, 512), [(R("sel", j, 1024, 8), R("kdh", 0, 512))])
-        move(CPE[j], R("kdw", 512 * j, 512 * j + 512), R(b, 0, 512), 2048.0)
+        b = ("pd0", "pd1", BN)[j % 3]
+        for e in range(2):
+            group(R(b, 256 * e, 256 * e + 256), [(R("sel", (2 * j + e) % 8, 1024, 8), R("kdh", 256 * (j // 4), 256 * (j // 4) + 256))])
+        move(CPE[j], R("kdw", 512 * j, 512 * j + 512), R(b, 0, 512))
 
-    def lists(s, t, mid):
-        B, z, pb, c = S + G * t, str(s), "pb%d" % s, (2 * t + s) * H
-        group(R(pb, 384, 512), [(ib, R("far", 0, H)), (R("lw" + z, 0, 128), R("xn", c, c + H))])
-        mid()
-        scan(R("yf" + z, 0, H), R("rz", 0, H), R(pb, 384, 512), 0.0, A.mult, A.max)
+    def lists(s, t, src, c0, far):
+        B, z = S + G * t, str(s)
+        for j in range(2):
+            for h in range(2):
+                a, b = 128 + 64 * j + 32 * h, c0 + far * h + 64 * j
+                group(R(BX, a, a + 32), [(ib, R("far", 0, 32))]
+                      + [(R("lv" + z, 192 * h + 64 - 64 * e, 192 * h + 192 - 64 * e), R(src, b + e, b + 64, 2)) for e in range(2)])
+        scan(R("yf" + z, 0, H), R("rz", 0, H), R(BX, 128, 256), 0.0, A.mult, A.max)
         tt(R("ui" + z, 0, 8), R("yf" + z, 15, H, 16), R("uc", 0, 8), A.add)
         ts(R("uj" + z, 0, 8), R("ui" + z, 0, 8), 4095, None, A.bitwise_and)
         copy(R("uo" + z, 0, 8), R("uj" + z, 0, 8))
-        act(R("yf" + z, 0, H), IND(R("kdw", 0, U), R("uo" + z, 0, 8)), AF.Copy, bias=-0.484375, scale=B / 4096.0)
-        ts(R("ek" + z, 0, H), R("yf" + z, 0, H), MAGIC, -MAGIC - SH, A.add, A.add)
-        ev, od = R("ek" + z, 0, H, 2), R("ek" + z, 1, H, 2)
-        group(R(pb, 384, 448), [(R("ilo", 8, 136), ev), (R("ilo", 0, 128), od)])
-        group(R(pb, 448, 512), [(R("ihi", 16, 144), ev), (R("ihi", 8, 136), od)])
-        ts(R("el" + z, 0, H), R(pb, 384, 512), SH, None, A.add)
+        copy(R("ek" + z, 0, H), IND(R("kdw", 0, U), R("uo" + z, 0, 8)))
+        for L in range(2):
+            group(R(BL, NP + H * L, NP + H * L + H), [(R("lay", H * L, H * L + H), R("ek" + z, 0, H))])
+        for L in range(2):
+            ts(R("el" + z, H * L, H * L + H), R(BL, NP + H * L, NP + H * L + H), B / 4096.0, B / 2.0 - 0.484375, A.mult, A.add)
 
+    iota(R("jq", 0, 192), [[16, 12], [0, 16]], -64)
+    for h in range(2):
+        ts(R("gq", 192 * h, 192 * h + 192), R("jq", 0, 192), C("plf"), C(("lof", "etaf")[h]), A.is_equal, A.mult)
     for s in range(2):
-        for h, p in enumerate(HALF):
-            copy(R("xn", H * s, H * s + H, p=p), R("xb%d" % s, S - G + H * h, S - G + H * h + H, p=p))
-        lists(s, 0, lambda: None)
+        ts(R("lv%d" % s, 0, 384), R("gq", 0, 384), R("rep", 3 * s + 1), None, A.mult)
+        lists(s, 0, "xb%d" % s, S - G, H)
     for s in range(2):
-        for b in (2, 3, 0, 1):
-            c0, nt = 512 * b, ("xl1", "ad1")[s]
-            ts(R(nt, c0, c0 + 512), R("xb%d" % s, c0, c0 + 512), th[s], 8192.0, A.is_lt, A.mult)
-            tt(R("kl%d" % s, c0, c0 + 512), R(names4[b], 0, 512), R(nt, c0, c0 + 512), A.add)
-            tt(R("kh%d" % s, c0, c0 + 512), R(names4[b], 0, 512), R(nt, c0, c0 + 512), A.subtract)
-    for name, per, sg in (("rp8", 8, 1), ("rn8", 8, -1), ("rn16", 16, -1), ("rp16", 16, 1)):
-        iota(R(name, 0, RW), [[0, RW // per], [-32767 * sg, per]], 2048 * sg)
-    copy(R("ih", 0, 128), ib)
-    act(R("nib", 0, 128), ib, AF.Copy, scale=-1.0)
+        for b, name in NAMES.items():
+            c0, nt = 512 * b, "xv1"
+            mask = R(nt, 2048 * s + c0, 2048 * s + c0 + 512)
+            ts(mask, R("xb%d" % s, c0, c0 + 512), th[s], -8192.0, A.is_lt, A.mult)
+            if s:
+                act(R("kt1", c0, c0 + 512), R("io", 0, 512), AF.Identity, bias=R("nbias", b), scale=C("sg"))
+            else:
+                tt(R("kt0", c0, c0 + 512), R(name, 0, 512), mask, A.add)
+    node("G", [lambda: g.dma_start(T.kt1[:, 0:S], T.xv1[:, S:2 * S], accum_op=A.add)], R("xv1", S, 2 * S)[1] + R("kt1", 0, S)[1], R("kt1", 0, S)[1],
+         (1.0, 0, 0, 0), sem="ga", inc=16, lat=7.0)
+    for per in (8, 16):
+        iota(R("rn%d" % per, 0, RW), [[0, RW // per], [32767, per]], -2048)
+    for name in ("if", "ih"):
+        copy(R(name, 0, 128), ib)
     ts(R("bigh", 0, 128), ib, -64.0, None, A.mult)
-    copy(R("rph", 0, 256), R("rpb", 0, 256))
-    ts(R("hib", 0, 128), ib, 1023.0 / 2048.0, None, A.mult)
-    gfill(R("cbig", 0, 128), 131072)
-    gfill(R("cbig", 128, 256), -131072)
-    iota(R("jj", 0, 128), [[1, 128]], 0)
-    ts(C("cs"), C("etaf"), float(H), None, A.mult)
-    ts(R("jj", 128, 256), R("jj", 0, 128), C("cs"), None, A.add)
-    iota(R("cb", 0, 1024), [[G, RO], [NP - int(SH), 2], [0, 128]], S)
-    gfill(R("csh", 0, 128), SH)
+    iota(R("cbig", 0, 256), [[8192, 2], [0, 128]], -131072)
+    ts(R("rp", 0, 128), R("j64", 0, 128), C("p6f"), None, A.is_equal)
+    ts(C("tl"), C("p6f"), 64.0, None, A.add)
+    ts(R("rz3", 0, 192), R("jx", 0, 192), C("tl"), None, A.is_equal)
+    ts(R("hx", 0, 192), R("rz3", 0, 192), C("ns"), 1023.0 / 2048.0, A.mult, A.mult)
+    ts(R("nl", 0, 192), R("rz3", 0, 192), C("etaf"), -1.0, A.is_gt, A.mult)
+    ts(C("tl"), C("plf"), 78.0, C("etaf"), A.add, A.add)
+    ts(R("l1", 0, 208), R("jx", 0, 208), C("tl"), None, A.is_equal)
+    for h, p in enumerate(HALF):
+        iota(R("bi", 0, RO * H, p=p), [[G, RO], [1, H]], S + H * h - int(SH))
+        nodes[-1]["alone"] = True
+    for name in ("nt0", "nb0"):
+        c0 = COLS.index(name)
+        act(R("fc", c0, c0 + 2), R("rep", 2, 6, 3), AF.Copy, scale=-8192.0)
     for s in range(2):
-        act(C("nt%d" % s), R("rep", 3 * s + 2), AF.Copy, scale=-8192.0)
-        act(C("nb%d" % s), R("rep", 3 * s + 2), AF.Copy, scale=-8192.0)
         gfill(R("nq%d" % s, 0, 64), 0)
         act(R("ng2", 128 * s, 128 * s + 128), R("g2", 0, 128), AF.Copy, scale=-1.0)
     ts(C("cm"), C("pixf"), 2.0, 256.0, A.mult, A.add)
@@ -506,18 +611,31 @@ def rank_program(g, core, T, topo):
         gfill(R("mw", 768 * k, 768 * k + CAP), 0)
     for t in range(RO):
         store(T.ya[:, G * t + NP:G * t + G], R("mnm", 128 * t, 128 * t + 128))
+    ts(C("cs"), C("sg"), -SH, None, A.mult)
+    mc = [R("pc", 0, 128), R("pc", 128, 256), R(BM, 0, 128)]
+    act(R("pc", 0, 256), R("mnm", 0, 256), AF.Identity, bias=C("cs"), scale=C("sg"))
+    act(mc[2], R("mnm", 256, 384), AF.Identity, bias=C("cs"), scale=C("sg"))
+    for h in range(2):
+        ts(R("rph", H * h, H * h + H), R("rp", 0, H), C(("lof", "etaf")[h]), None, A.mult)
+        ts(R("rps", H * h, H * h + 64), R("rph", H * h, H * h + 64), -1.0, None, A.mult)
+        copy(R("rps", H * h + 64, H * h + H), R("rph", H * h + 64, H * h + H))
 
-    def send(s, t, B):
+    def lanes(a, t):
+        to = [T.cores[(a + 1 + (FO * t + f) % (N - 1)) % N] for f in range(FO)]
+        may = [topo.engines(T.cores[a], x) for x in to]
+        both = [e for e in may[0] if e in may[1]]
+        if t and len(may[0]) != len(may[1]):
+            use = [[e for e in x if e not in both] or both for x in may]
+        else:
+            use = [both[:len(both) // 2], both[len(both) // 2:]]
+        return (to[0], use[0]), (to[1], use[1]), len(use[0]) + len(use[1])
+
+    def send(s, t):
         trs, k = [], 2 * t + s
-        for f in range(FO):
-            to = T.cores[(rank + 1 + (FO * t + f) % (N - 1)) % N]
+        for f, (to, use) in enumerate(lanes(rank, t)[:2]):
             rid, pid, _ = topo.addr(to)
-            b = B + NP + CAP * f
-            m = 0
-            for e in topo.engines(core, to)[4 * f:4 * f + 4]:
-                m |= 1 << e
-            trs.append(RemoteDMATransfer(dst_ids=[DstId(rid=rid, pnc=pid)], dma_engine_mask=m, remote_sem=T.sem["ma%d" % k],
-                                         srcs=[T.mo[:, CAP * k:CAP * k + CAP]], dsts=[T["xb%d" % s][:, b:b + CAP]]))
+            trs.append(RemoteDMATransfer(dst_ids=[DstId(rid=rid, pnc=pid)], dma_engine_mask=sum(1 << e for e in use), remote_sem=T.sem["ma%d" % k],
+                                         srcs=[T.mw[:, 768 * k:768 * k + CAP]], dsts=[T.rx[:, H * k + CAP * f:H * k + CAP * f + CAP]]))
         g.remote_dma_fused(trs, local_sem=T.sem.rl)
 
     pieces = [0]
@@ -526,107 +644,114 @@ def rank_program(g, core, T, topo):
         B, Y, z, k = S + G * t, G * t, str(s), 2 * t + s
         last = t == RO - 1
         cur[0] = k
-        pa, pb, xb = "pa" + z, "pb" + z, "xb" + z
+        xb, kt = "xb" + z, "kt" + z
         rows = slice(64 * s, 64 * s + 64)
-        cn, mc = R("pc", NP * (t % 2), NP * (t % 2) + H), R("pc", NP * (t % 2) + H, NP * (t % 2) + NP)
-        if not s:
-            group(cn, [(ib, R("jj", H, 2 * H)), (ib, R("cb", NP * t, NP * t + H))])
-            if not last:
-                group(mc, [(ib, R("jj", 0, H)), (ib, R("cb", NP * t + H, NP * t + NP))])
-        for i0, i1 in NCH:
-            f0, f1, n = 8 * i0, 8 * i1, i1 - i0
-            for tab, x, op, no, rs in (("kl", "l", A.min, A.max, "rp8"), ("kh", "h", A.max, A.min, "rn8")):
-                act(R(x + "a" + z, f0, f1), IND(R(tab + z, 0, B), R("el" + z, i0 // 2, i1 // 2)), AF.Copy)
-                tt(R(x + "b" + z, f0, f1), IND(R(tab + z, 0, B), R("el" + z, 64 + i0 // 2, 64 + i1 // 2)), R(x + "a" + z, f0, f1), op)
-                scan(R(x + "s" + z, f0, f1), R(rs, 0, f1 - f0), R(x + "b" + z, f0, f1), 0.0, no, op)
-            hs, ls, z0 = R("hs" + z, f0 + 7, f1, 8), R("ls" + z, f0 + 7, f1, 8), R("z0" + z, i0, i1)
-            ts(z0, R("la" + z, f0, f1, 8), -8192.0, None, A.add)
-            tl, tb = R(pb, H + i0, H + i1), R(pb, i0, i1) if i0 else R(pa, H, H + n)
-            group(tl, [(ib, R("cbig", 0, n)), (R("ih", 0, 128), z0), (R("bigh", 0, 128), ls)])
-            group(tb, [(ib, R("cbig", H, H + n)), (R("ih", 0, 128), z0), (R("bigh", 0, 128), hs)])
-            tt(R("lo" + z, i0 + i1, 2 * i1), tl, ls, A.min)
-            tt(R("lo" + z, 2 * i0, i0 + i1), tb, hs, A.max)
-            for a, b in ((2 * i0, 2 * i1),) if i0 else ((n, 2 * n), (0, n)):
-                ts(R("hl" + z, a, b), R("lo" + z, a, b), SH, None, A.add)
-        for i0, i1 in NCH:
-            group(R(pb, i0, i1), [(ib, R("csh", 0, i1 - i0)), (R("ih", 0, 128), R("lo" + z, i0 + i1, 2 * i1))])
-
-        def listof(i0, i1, low):
-            a, b = [x for x in NCH if x[0] <= i0 and i1 <= x[1]][0]
-            return IND(R(xb, 0, B), R("hl" + z, a + (b - a) * low + i0, a + (b - a) * low + i1))
-        vp = VPL if k == LAST else VP
-        for name, low, pcs in (("xl", 1, XL[k]), ("xh", 0, XH[k])):
-            starts = [j for j in range(len(vp)) if pcs[j].isupper()] + [len(vp)]
-            for j, j1 in zip(starts, starts[1:]):
-                move(pcs[j], R(name + z, 16 * vp[j][0], 16 * vp[j1 - 1][1]), listof(vp[j][0], vp[j1 - 1][1], low))
-        for i0, i1 in vp:
-            f0, f1 = 16 * i0, 16 * i1
-            if FUS and k == LAST and i1 == H:
-                d = R("df", 0, f1 - f0)
-                tt(d, listof(i0, i1, 0), R("xl" + z, f0, f1), A.subtract)
+        for n0, n1 in NCH[k]:
+            f0, f1 = 8 * n0, 8 * n1
+            kids = [IND(R(kt, 0, B), R("el" + z, H * L + n0 // 2, H * L + n1 // 2)) for L in range(2)]
+            ka, kb = R("ka" + z, f0, f1), R("kb" + z, f0, f1)
+            w = (n1 - n0) // KA[n0 // 64]
+            for a in range(n0, n1, w):
+                act(R("ka" + z, 8 * a, 8 * (a + w)), IND(R(kt, 0, B), R("el" + z, a // 2, (a + w) // 2)), AF.Copy)
+            tt(kb, kids[1], ka, A.max)
+            scan(R("ks" + z, f0, f1), R("rn8", 0, f1 - f0), kb, 0.0, A.min, A.max)
+            m, z0, c = R("ks" + z, f0 + 7, f1, 8), R("z" + z, n0, n1), R(BN, n0, n1)
+            if ZT[n0 // 64] == "T":
+                group(c, [(ib, R("cbig", H, H + n1 - n0)), (R("if", 0, 128), R("ka" + z, f0, f1, 8)), (R("bigh", 0, 128), m)], (2,))
             else:
-                d = R(PD[pieces[0] % len(PD)], 0, f1 - f0)
+                ts(z0, R("ka" + z, f0, f1, 8), 8192.0, None, A.add)
+                group(c, [(ib, R("cbig", 0, n1 - n0)), (R("ih", 0, 128), z0), (R("bigh", 0, 128), m)], (2,))
+            tt(R("lh" + z, n0, n1), c, m, A.max)
+            ts(R("hl" + z, n0, n1), R("lh" + z, n0, n1), C("sg"), SH, A.mult, A.add)
+        n0, done, tiles = 0, 0, list(AB[k])
+        for w, e in VP[k]:
+            n1 = n0 + w
+            move(e, R("xv" + z, 16 * n0, 16 * n1), IND(R(xb, 0, B), R("hl" + z, n0, n1)), C("ns"))
+            for a in range(n0, n1, RW // 16):
+                b = min(n1, a + RW // 16)
+                scan(R("ms" + z, 16 * a, 16 * b), R("rn16", 0, 16 * (b - a)), R("xv" + z, 16 * a, 16 * b), 0.0, A.min, A.max)
+            while tiles and done + tiles[0] <= n1:
+                b = done + tiles.pop(0)
+                d = R(PD[pieces[0] % len(PD)], 0, 8 * (b - done))
                 pieces[0] += 1
-                group(d, [(R("nib", 0, 128), R("xh" + z, f0, f1)), (ib, R("xl" + z, f0, f1))])
-            act(R("ad" + z, f0, f1), d, AF.Abs)
-            scan(R("mn" + z, f0, f1), R("rp16", 0, f1 - f0), R("xh" + z, f0, f1), 0.0, A.max, A.min)
-            scan(R("ms" + z, f0, f1), R("rn16", 0, f1 - f0), R("xl" + z, f0, f1), 0.0, A.min, A.max)
-            for d0, d1 in DP:
-                if i0 < d1 <= i1:
-                    group(R(pa, d0, d1), [(R("l1", 15 - r_, 143 - r_), R("ad" + z, 16 * d0 + r_, 16 * d1, 16)) for r_ in range(16)])
-        act(R("r" + z, 0, H), R(pa, 0, H), AF.Relu, bias=C("nb" + z), scale=8192.0)
-        c = (k + 2) * H
-        xn = R("xn", c, c + H)
-        group(R(pb, H, 2 * H), [(R("hib", 0, 128), R("mn" + z, 15, 2048, 16)), (R("hib", 0, 128), R("ms" + z, 15, 2048, 16))])
-        ts(xn, R(pb, H, 2 * H), MAGIC, -MAGIC, A.add, A.add)
+                group(d, [(to_half("rz3", e_), R("xv" + z, 16 * done + e_, 16 * b, 2)) for e_ in range(2)], (1,) if b - done > 32 else ())
+                act(R("ad" + z, 8 * done, 8 * b), d, AF.Abs)
+                done = b
+                if done % H == 0:
+                    j = done // H - 1
+                    group(R(BD, 64 * j, 64 * j + 64),
+                          [(R("l1", 78 - 64 * h - 2 * p2, 206 - 64 * h - 2 * p2), R("ad" + z, 512 * (2 * j + h) + p2, 512 * (2 * j + h + 1), 8))
+                           for h in ((1, 0) if j and VP[k][1][1] == "S" else (0, 1)) for p2 in range(8)], (8,))
+            n0 = n1
+        r = R("r" + z, 0, H)
+        act(r, R(BD, 0, H), AF.Relu, bias=C("nb" + z), scale=8192.0)
+        xn = R("xn", H * k, H * k + H)
+        for j in range(2):
+            group(R(BX, 64 * j, 64 * j + 64), [(to_half("hx", h), R("ms" + z, 1024 * (2 * j + h) + 15, 1024 * (2 * j + h + 1), 16)) for h in range(2)])
+        ts(xn, R(BX, 0, H), MAGIC, -MAGIC, A.add, A.add)
+        ahead = []
+        if not last:
+            spread([(R(xb, B + H * h, B + H * h + H, p=p), R("xn", H * k, H * k + H, p=HALF[h])) for h in range(2) for p in HALF], "sx%d" % k)
+            ahead.append(len(nodes) - 1)
+            lists(s, t + 1, "xn", H * k, 0)
+        ab, landed = R("ab", H * k, H * k + H), []
 
-        def both():
+        def names():
+            for j in range(2):
+                group(R(BP, NP + 64 * j, NP + 64 * j + 64), [(to_half("nl", h), R("lh" + z, 64 * (2 * j + h), 64 * (2 * j + h + 1))) for h in range(2)]
+                      + [(ib, R("r" + z, 64 * j, 64 * j + 64))])
+            tt(ab, R(BP, NP, NP + H), R("bi", H * t, H * t + H), A.min)
+            for k0, k1 in OUT.get(k, ()):
+                ts(R("an", H * k0, H * k1), R("ab", H * k0, H * k1), SH, None, A.add)
+                for j in range(k0, k1):
+                    for h in range(2):
+                        c0 = G * (j // 2) + H * h
+                        store(T.ya[64 * (j % 2):64 * (j % 2) + 64, c0:c0 + H], R("an", H * j, H * j + H, p=HALF[h]))
+        if last:
             for h in range(2):
-                group(R(pb, H + H * h, 2 * H + H * h), [(R("rpb", 128 * h, 128 * h + 128), xn)])
-            act(R(xb, B, B + NP), R(pb, H, 3 * H), AF.Copy)
-        if not last:
-            lists(s, t + 1, both)
-        group(R(pa, 128, 384), [(ib, R("ow", 0, 256)), (R("r" + z, 0, H), R("ng2", 0, 256))])
+                store(T.yx[rows, Y + H * h:Y + H * h + H], R("xn", H * k, H * k + H, p=HALF[h]))
+        if k == LAST:
+            names()
+        group(R(BM, 128, 384), [(ib, R("ow", 0, 256)), (r, R("ng2", 0, 256))], (1,))
         if k < LAST:
-            act(R("nq" + z, 64, 320), R(pa, 128, 384), AF.Relu)
+            act(R("nq" + z, 64, 320), R(BM, 128, 384), AF.Relu)
         else:
-            ts(R("nq" + z, 64, 320), R(pa, 128, 384), 0.0, None, A.max)
-        group(R(pa, 384, 392), [(ib, R("ich", 0, 8)), (R("nq" + z, 0, 128), R("none8", 0, 8)), (R("nq" + z, 64, 192), R("nbef", 0, 8)),
+            ts(R("nq" + z, 64, 320), R(BM, 128, 384), 0.0, None, A.max)
+        group(R(BM, 384, 392), [(ib, R("ich", 0, 8)), (R("nq" + z, 0, 128), R("none8", 0, 8)), (R("nq" + z, 64, 192), R("nbef", 0, 8)),
                                 (R("nq" + z, 192, 320), R("g2", 0, 128, 16))])
-        copy(R("off" + z, 0, 8), R(pa, 384, 392))
+        copy(R("off" + z, 0, 8), R(BM, 384, 392))
         dst = IND(R("mw", 768 * k, 768 * k + 768), R("off" + z, 0, 8))
-        node("V", [lambda: g.vector.tensor_copy(dst[0], xn[0])], xn[1] + dst[1][1:], dst[1][:1], 0.05 + SCY * CY * H)
-        group(R(pa, 400, 464), [(R("rpb", 128 * h, 128 * h + 128), R("mw", 768 * k, 768 * k + CAP)) for h in range(2)])
-        copy(R("mo", CAP * k, CAP * k + CAP), R(pa, 400, 464))
-        n = node("G", [lambda: send(s, t, B)], R("mo", CAP * k, CAP * k + CAP)[1], [], 0.3, sem="rl", inc=8)
-        node("R", [None], [], R(xb, B + NP, B + G)[1], MLAT, sem="ma%d" % k, inc=8, preds=[n])
-        an = R("ab", H * k, H * k + H)
-        tt(R("fb" + z, 0, H), R("r" + z, 0, H), cn, A.min)
-        tt(an, R(pb, 0, H), R("fb" + z, 0, H), A.max)
-        for h in range(2):
-            store(T.ya[rows, Y + H * h:Y + H * h + H], R("ab", H * k, H * k + H, p=HALF[h]))
-            if last:
-                store(T.yx[rows, Y + H * h:Y + H * h + H], R("xn", c, c + H, p=HALF[h]))
+        node("V", [lambda: g.vector.tensor_copy(dst[0], xn[0])], xn[1] + dst[1][1:], dst[1][:1], (0.05, 0, 0, H))
+        n = node("G", [lambda: send(s, t)], R("mw", 768 * k, 768 * k + CAP)[1], [], (0.3, 0, 0, 0), sem="rl", inc=lanes(rank, t)[2], soft=ahead)
+        node("R", [None], [], R("rx", H * k, H * k + H)[1], (0.0, 0, 0, 0), sem="ma%d" % k, preds=[n], lat="m",
+             inc=sum(len(lanes((rank - 1 - (FO * t + f) % (N - 1)) % N, t)[f][1]) for f in range(FO)))
+        if k < LAST:
+            names()
         if not last:
-            ts(R("n8" + z, 0, NP), R(xb, B, B + NP), th[s], 8192.0, A.is_lt, A.mult)
-            ts(R("ek" + z, H, 2 * H), an, -SH, None, A.add)
+            ts(R("n8" + z, 0, H), xn, th[s], -8192.0, A.is_lt, A.mult)
             for h in range(2):
-                group(R(pb, H * h, H * h + H), [(R("rph", 128 * h, 128 * h + 128), R("ek" + z, H, 2 * H))])
-            tt(R("kh" + z, B, B + NP), R(pb, 0, NP), R("n8" + z, 0, NP), A.subtract)
-            tt(R("kl" + z, B, B + NP), R(pb, 0, NP), R("n8" + z, 0, NP), A.add)
-            if s:
-                group(R(pa, 464, 472), [(R("onesb", 0, 128), R("nq%d" % j, 64, 192, 16)) for j in range(2)])
-                node("V", [lambda: g.vector.tensor_reduce(C("cs")[0], T[pa][:, 464:472], AxisListType.X, A.add)],
-                     R(pa, 464, 472)[1], C("cs")[1], 0.064)
-                ts(C("cia"), C("cs"), -1.0, 2048.0, A.mult, A.add)
-                ts(C("cja"), C("cia"), 15, None, A.bitwise_and)
-                for j in range(2):
-                    ts(C("nb%d" % j), C("cja"), -8192.0, C("nt%d" % j), A.mult, A.add)
-            ts(R("n8" + z, NP, G), R(xb, B + NP, B + G), th[s], 8192.0, A.is_lt, A.mult)
-            tt(R("kh" + z, B + NP, B + G), mc, R("n8" + z, NP, G), A.subtract)
-            tt(R("kl" + z, B + NP, B + G), mc, R("n8" + z, NP, G), A.add)
-        c0 = NP if last else 0
-        store(T.yx[rows, Y + c0:Y + G], R(xb, B + c0, B + G, p=LO))
+                group(R("pc", NP + H * h, NP + H * h + H), [(R("rph", H * h, H * h + H), R("n8" + z, 0, H)), (R("rps", H * h, H * h + H), ab)])
+            move(KE, R(kt, B, B + NP), R("pc", NP, 2 * NP))
+        mail = R(BM, 384, 512)
+        if last:
+            for j in range(2 * s):
+                group(mail, [(R("rp", 0, 128), R("rx", H * (k - 1 + j), H * (k + j)))])
+                copy(R("xb%d" % j, B + NP, B + G), mail)
+                store(T.yx[64 * j:64 * j + 64, Y + NP:Y + G], R("xb%d" % j, B + NP, B + G, p=LO))
+            return
+        group(mail, [(R("rp", 0, 128), R("rx", H * k, H * k + H))])
+        ts(R("nm" + z, 0, 128), mail, th[s], 8192.0, A.is_lt, A.mult)
+        tt(R(kt, B + NP, B + G), mc[t], R("nm" + z, 0, 128), A.subtract)
+        copy(R(xb, B + NP, B + G), mail)
+        if s:
+            group(R(BM, 376, 384), [(R("onesb", 0, 128), R("nq%d" % j, 64, 192, 16)) for j in range(2)])
+            node("V", [lambda: g.vector.tensor_reduce(C("cs")[0], T[BM][:, 376:384], AxisListType.X, A.add)],
+                 R(BM, 376, 384)[1], C("cs")[1], (0.0, 64, 0, 0))
+            ts(C("cia"), C("cs"), -1.0, 2048.0, A.mult, A.add)
+            ts(C("cja"), C("cia"), 15, None, A.bitwise_and)
+            for j in range(2):
+                ts(C("nb%d" % j), C("cja"), -8192.0, C("nt%d" % j), A.mult, A.add)
+        store(T.yx[rows, Y:Y + G], R(xb, B, B + G, p=LO))
 
     for t in range(RO):
         for s in range(2):
@@ -636,16 +761,21 @@ def rank_program(g, core, T, topo):
         STATS["nodes"], STATS["order"] = nodes, schedule(nodes)
     order = loads + [k for k in STATS["order"] if k not in loads]
 
-    count, waited, snap, token = {}, {}, {}, {}
+    count, waited, snap, token, made = {}, {}, {}, {}, []
     known = {q: {} for q in "VSTGYR"}
     for k in order:
         nd = nodes[k]
         q, sem = nd["q"], nd["sem"]
         kn = known[q]
         for j, fn in enumerate(nd["fns"]):
-            need, ps = {}, set() if j else set(nd["ps"])
+            need, ps = {}, set() if j else set(nd["ps"]) - nd["soft"]
             if nd["early"]:
                 ps = nd["early"][j] if j else nd["before"] | nd["early"][0]
+            if q == "G":
+                if made and (nd["alone"] or nodes[made[-1]]["alone"]):
+                    ps = ps | {made[-1]}
+                if sem == "sg":
+                    made.append(k)
             for p in ps:
                 s, n = token[p]
                 if q != "R" and kn.get(s, 0) < n:

import math

from concourse.bass import DstId, RemoteDMATransfer
from concourse.mybir import AluOpType, ActivationFunctionType, AxisListType

N, S, U, NP, CAP, FO, RO = 8, 2048, 4096, 256, 64, 2, 4
G = NP + FO * CAP
TOT = S + RO * G
KT = TOT - G
H = NP // 2
LAST = 2 * RO - 1
NCH = [[(0, 64), (64, 128), (128, 192), (192, 256)]] * 8
VP = [[(64, "S"), (64, "S"), (32, "S"), (32, "S"), (64, "V")]] * 8
AB = [[64, 64, 32, 32, 64]] * 8
ZT = "TVVV"
KE = "V"
OUT = {7: [(0, 7), (7, 8)]}
CPE = "SSSSSSSV"
KA = (1, 1, 1, 1)
PD = ["pd0", "pd1", "pd2"]
BN, BD, BM, BX, BP, BL = "pn", "pq", "pm", "px", "pc", "px"
NAMES = {2: "pq", 3: "pd2", 0: "pm", 1: "pc"}
RW = 1024
CASES = [(1.56, 3.0, 0.2, 2.3, 2.2), (1.4, 3.0, 0.26, 2.8, 2.6), (1.2, 2.4, 0.16, 2.0, 1.9)]
CY = 0.00083
FIRST = 2.0
SEED, HEAT = 1, 0.0015
WINDOWS = [(0.075, 0.36, 70000), (0.74, 1.1, 45000), (0.05, 0.3, 20000)]
SHIFT = [0.0] * 7 + [-1.0]
TAIL = {"Y": "-1' -2' " + " ".join("-%d" % j for j in range(3, 17)) + " -1 -2 -17 -18 -19 -20"}
FRONT = {}
HEAD = {
    "G": "pix1 c161 jx1 jm1 jq1 cu1 j641 jd1 rn81 cbig1 rn161 mnm1 nq1 ow1 none81 mw1 kt1",
    "V": "onesb1 fc1 pi3 io1 fc4 fc8 nbias1 nbias2 ipad1 pi1 pi6 sel1 fc2 fc7 sel2 fc10 i31 sel3 pi5 pi4 sel4 rowf1 rowf2 kdh1 rowf3 rowf4 gq1 gq2"
         " far1 rz1 kdh2 rep1 fc6 fc5 lv1 fc12 uc1 xv1 fc13 kt1 fc14 xv2 fc15 kt2 lay1 xv3 yf1 fc16 xv4 ui1 lay2 uj1 kt3 uo1 kdw1 kt4 ek1 xv5"
         " xv6 el1 el2 xv7 xv8",
    "S": "pq1 pd1 pm1 pc1 kdw1 kdw2 kdw3 kdw4 kdw5 kdw6 kdw7 kt1 kt2 kt3 kt4",
    "T": "pn1 pd1 pn2 pd2 pd3 pd4 pn3 pn4 pd5 pd6 px1 px2 pd7 pd8 px3 px4 pn5 pn6 pd9 pd10 pd11 pd12 px5 px6",
}
TURNS = {
    "V": "z1' n81'' lh1' ks2' z2' hl1' kb3' nq1'' lh2' z3' yf1'' hl2' off1'' ks3' mw1'' ui1'' kb4' uj1'' lh3' ab1'' ks4' uo1'' ms1' hl3' lh4'"
         " ek1'' hl4' kt1'' xv1' nm1'' xb1'' el1'' kt2'' ms5' ms4' ms3' el2'' fc1'' ms2' an1' cia1'' kb1 xn1' cja1'' ks1 fc3'' fc2'' kb2",
    "S": "r1'' ka4' nq1'' xv1' xv2' ad1' xv3' ad2' xv4' ad3' ka1 ad5' ad4' ka2 ka3",
    "T": "pn1' pm1'' pn2' pm2'' px4'' px6'' pn3' pn4' px3'' px5'' pm3'' pc2'' pc1'' pn5' pn6' pd1' pd2' pn7' pc4'' pn8' pc3'' pd3' pd4' px7''"
         " px8'' pd5' pm4'' pq1' pd7' pd8' pm5'' pd6' pq2' px2' px1' pq3' pq4'",
    "Y": "xb1' -1''", "G": "-1''",
}
STATS = {}
MAGIC = 12582912.0
SH = 1792.0
F16, BF, F32 = "float16", "bfloat16", "float32"

COLS = ["pixf", "prf", "pdf", "etaf", "p4f", "p6f", "plf", "sg", "ns", "lof", "zc", "tl", "te", "cs", "cm", "nb0", "nb1", "nt0", "nt1"]


def _sb(n, dt):
    return ("sbuf", [128, n], dt)


SCRATCH = {
    "kdn": _sb(512, "int32"), "kdh": _sb(512, F16), "kdw": _sb(U, F32), "sel": _sb(1024, F16),
    "onesb": _sb(512, BF), "io": _sb(512, F32), "nbias": _sb(8, F32), "cbig": _sb(256, BF), "jx": _sb(256, BF), "j64": _sb(144, BF),
    "an": _sb(2 * RO * H, F32), "xn": _sb(2 * RO * H, BF), "mw": _sb(2 * RO * 768, BF), "rx": _sb(2 * RO * H, BF),
    "mnm": _sb(RO * 128, F32), "bi": _sb(RO * H, F32), "rn4": _sb(RW, BF), "rn8": _sb(RW, BF), "rn16": _sb(RW, BF),
    "ipad": _sb(128, BF), "ih": _sb(128, F16), "if": _sb(128, F32), "bigh": _sb(128, F16), "rp": _sb(128, BF), "rz3": _sb(192, BF), "hx": _sb(192, F16),
    "nl": _sb(192, F16), "lay": _sb(4 * 144, F16), "i3": _sb(4, F16),
    "jd": _sb(128, BF), "jm": _sb(128, BF), "g2": _sb(128, BF), "ng2": _sb(256, BF), "l1": _sb(208, BF), "ow": _sb(256, BF),
    "wa": _sb(128, BF), "wb": _sb(128, BF), "nbef": _sb(8, BF), "none8": _sb(8, BF), "ich": _sb(8, BF), "c16": _sb(8, F32), "uc": _sb(8, F32),
    "jq": _sb(192, BF), "gq": _sb(384, BF), "cu": _sb(8, F32), "ab": _sb(2 * RO * H, F16), "rph": _sb(256, BF), "rps": _sb(256, F16), "far": _sb(32, BF), "rz": _sb(128, BF),
    "rowi": _sb(128, "int32"), "rowf": _sb(256, F16), "rep": _sb(8, F32),
    "fc": _sb(len(COLS), F32), "pix": _sb(1, "int32"), "pi": _sb(8, "int32"), "cia": _sb(1, "int32"), "cja": _sb(1, "int32"),
}
for _n in ("pd0", "pd1", "pd2", "pc", "pn", "pq", "pm", "px"):
    SCRATCH[_n] = ("psum", [128, 512], F32)
for _s in "01":
    SCRATCH.update({
        "xb" + _s: _sb(TOT, BF), "kt" + _s: _sb(KT, F32), "lv" + _s: _sb(384, BF),
        "ka" + _s: _sb(2048, F32), "kb" + _s: _sb(2048, F16), "ks" + _s: _sb(2048, F16),
        "z" + _s: _sb(NP, F16), "lh" + _s: _sb(NP, F16), "hl" + _s: _sb(NP, "uint16"),
        "xv" + _s: _sb(4096, BF), "ad" + _s: _sb(2048, BF), "ms" + _s: _sb(4096, F16),
        "r" + _s: _sb(H, BF), "nq" + _s: _sb(320, BF), "off" + _s: _sb(8, "uint16"), "nm" + _s: _sb(128, BF),
        "n8" + _s: _sb(H, BF),
        "ui" + _s: _sb(8, "int32"), "uj" + _s: _sb(8, "int32"), "uo" + _s: _sb(8, "uint16"),
        "yf" + _s: _sb(H, F32), "ek" + _s: _sb(H, F16), "el" + _s: _sb(NP, "uint16"),
    })

SEMAPHORES = ["sv", "ss", "st", "sg", "rl", "out", "ga"] + [x + str(k) for x in ("ma", "l", "sx", "sk") for k in range(2 * RO)]
PSUM = [n for n, v in SCRATCH.items() if v[0] == "psum"]


def prices(nodes, case):
    gc, sc, wake, mail, dma = case
    cost = [nd["cost"][0] + CY * (nd["cost"][1] + gc * nd["cost"][2] + sc * nd["cost"][3]) for nd in nodes]
    lat = [{"m": mail + FIRST * (nd["step"] in (0, LAST - 1)), "d": dma, "g": -wake}.get(nd["lat"], nd["lat"]) for nd in nodes]
    return cost, [c + x for c, x in zip(cost, lat)], wake


def place(q, before, cost, out, key):
    n = len(q)
    users, left = [[] for _ in q], [len(x) for x in before]
    for k in range(n):
        for p in before[k]:
            users[p].append(k)
    ready, at, held, busy = [0.0] * n, [0.0] * n, set(), {}
    for k0 in sorted(range(n), key=lambda k: (key[k], k)):
        todo = [] if left[k0] else [k0]
        held.add(k0)
        while todo:
            k = todo.pop()
            t, d = ready[k], cost[k]
            if q[k] != "R":
                lst = busy.setdefault(q[k], [])
                j = len(lst)
                while j and lst[j - 1][1] > t:
                    j -= 1
                while j < len(lst) and lst[j][0] < t + d:
                    t = max(t, lst[j][1])
                    j += 1
                lst.insert(j, (t, t + d))
            at[k] = t
            for u in users[k]:
                ready[u] = max(ready[u], t + out[k])
                left[u] -= 1
                if not left[u] and u in held:
                    todo.append(u)
    return at


def schedule(nodes):
    n = len(nodes)
    q, step, kind = ([nd[x] for nd in nodes] for x in ("q", "step", "kind"))
    reach, suc, pre = [0] * n, [[] for _ in nodes], [[] for _ in nodes]
    for k, nd in enumerate(nodes):
        for p in nd["ps"]:
            reach[k] |= reach[p]
        for p in nd["ps"]:
            if not reach[k] >> p & 1:
                suc[p].append(k)
                pre[k].append(p)
        for p in nd["ps"]:
            reach[k] |= 1 << p
    npre = [len(x) for x in pre]
    cases = [prices(nodes, c) for c in CASES]
    cases = [(cost, fin, [f + wake for f in fin]) for cost, fin, wake in cases]

    def links(order):
        prv, nxt, last = [-1] * n, [-1] * n, {}
        for k in order:
            if q[k] != "R":
                prv[k] = last.get(q[k], -1)
                if prv[k] >= 0:
                    nxt[prv[k]] = k
                last[q[k]] = k
        return prv, nxt

    def forward(prv, nxt, bare=False):
        left = [npre[k] + (prv[k] >= 0) for k in range(n)]
        seq = [k for k in range(n) if not left[k]]
        for k in seq:
            for u in suc[k]:
                left[u] -= 1
                if not left[u]:
                    seq.append(u)
            u = nxt[k]
            if u >= 0:
                left[u] -= 1
                if not left[u]:
                    seq.append(u)
        if len(seq) < n:
            return None
        heads, ends = [], []
        for cost, fin, out in cases:
            head = [0.0] * n
            for k in seq:
                if bare and step[k] < 0:
                    continue
                h = head[k]
                e = h + out[k] - (FIRST if bare and q[k] == "R" and step[k] == 0 else 0.0)
                for u in suc[k]:
                    if e > head[u]:
                        head[u] = e
                u = nxt[k]
                if u >= 0 and h + cost[k] > head[u]:
                    head[u] = h + cost[k]
            heads.append(head)
            ends.append(max(h + f for h, f in zip(head, fin)))
        return sum(e / w for e, w in zip(ends, weight)), ends, heads, seq

    weight = [max(sum(c for c, x in zip(cost, q) if x == e) for e in "VST") for cost, _, _ in cases]

    who = {(step[k], q[k], kind[k]): k for k in range(n)}

    def timed(turns, shift):
        cost, fin, out = cases[0]
        row = [who.get((j - x.count("'"), e, x.rstrip("'"))) for j in range(LAST + 4) for e, s in turns.items() for x in s.split()]
        end = [who[(LAST - x.count("'"), e, x.rstrip("'"))] for e, s in TAIL.items() for x in s.split()]
        front = [who[(x.count("+"), e, x.rstrip("+"))] for e, s in FRONT.items() for x in s.split()]
        row = front + [k for k in row if k is not None and step[k] >= 0 and k not in end + front] + end
        head = forward(*links(row + sorted(k for k in set(range(n)) - set(row) if step[k] >= 0)), True)[2][0]
        key, row = [0.0] * n, {}
        for k in range(n - 1, -1, -1):
            if step[k] >= 0:
                key[k] = head[k] + shift[step[k]]
            else:
                key[k] = min([20.0] + [key[u] - out[k] for u in suc[k]])
                if cost[k] > 0.2:
                    key[k] = row[q[k]] = min(key[k], row.get(q[k], 20.0) - cost[k])
        row = [k for k in range(n) if nodes[k]["first"]] + [who[(-1, e, x)] for e, s in HEAD.items() for x in s.split()]
        head = forward(*links(row))[2][0]
        for k in row:
            key[k] = head[k] - 100.0
        at = place(q, pre, cost, out, key)
        t0 = min(at[k] - key[k] for k in range(n) if step[k] == 0 and q[k] == "S")
        key = [key[k] + t0 if step[k] >= 0 else at[k] for k in range(n)]
        for k in range(n):
            key[k] = max([key[k]] + [key[p] for p in pre[k]])
        c = links(sorted(range(n), key=lambda k: (not nodes[k]["first"], key[k] * (not nodes[k]["first"]), k)))
        return (forward(*c),) + c

    STATS["timed"], STATS["cases"], STATS["weight"], STATS["graph"] = timed, cases, weight, (forward, reach, pre, suc)
    if not TURNS:
        return list(range(n))
    best = timed(TURNS, SHIFT)
    STATS["placed"] = best[0][1]
    seed = [SEED]

    def rnd():
        seed[0] = (seed[0] * 6364136223846793005 + 1442695040888963407) % 2 ** 64
        return ((seed[0] >> 33) + 1) / 2.0 ** 31

    def polish(state, lo, hi, tries):
        (_, _, heads, seq), prv, nxt = state
        spot = {k: j for j, k in enumerate(sorted(range(n), key=lambda k: (heads[0][k], seq.index(k))))}
        win = sorted((k for k in seq if lo <= heads[0][k] < hi), key=spot.get)
        ix = {k: j for j, k in enumerate(win)}
        m, rows = len(win), {}
        for k in win:
            if q[k] != "R":
                rows.setdefault(q[k], []).append(ix[k])
        users = [[ix[u] for u in suc[k] if u in ix] for k in win]
        need = [sum(p in ix for p in pre[k]) for k in win]
        fixed = []
        for (cost, fin, out), head, w in zip(cases, heads, weight):
            tail = [0.0] * n
            for k in reversed(seq):
                tail[k] = max([fin[k], cost[k] + tail[nxt[k]] if nxt[k] >= 0 else 0.0] + [out[k] + tail[u] for u in suc[k]])
            ends = {e: (prv[win[r[0]]], nxt[win[r[-1]]]) for e, r in rows.items()}
            fixed.append(([max([0.0] + [head[p] + out[p] for p in pre[k] if p not in ix]) for k in win],
                          [max([fin[k]] + [out[k] + tail[u] for u in suc[k] if u not in ix]) for k in win],
                          {e: (head[a] + cost[a] if a >= 0 else 0.0, tail[b] if b >= 0 else 0.0) for e, (a, b) in ends.items()},
                          [cost[k] for k in win], [out[k] for k in win], w))

        def score(tight=False):
            left, after = list(need), [-1] * m
            for r in rows.values():
                for a, b in zip(r, r[1:]):
                    after[a] = b
                    left[b] += 1
            way = [j for j in range(m) if not left[j]]
            for j in way:
                for u in users[j]:
                    left[u] -= 1
                    if not left[u]:
                        way.append(u)
                u = after[j]
                if u >= 0:
                    left[u] -= 1
                    if not left[u]:
                        way.append(u)
            if len(way) < m:
                return None
            total = 0.0
            for ready, rest, ends, cost, out, w in fixed:
                t = list(ready)
                for e, r in rows.items():
                    t[r[0]] = max(t[r[0]], ends[e][0])
                for j in way:
                    h = t[j]
                    x = h + out[j]
                    for u in users[j]:
                        if x > t[u]:
                            t[u] = x
                    u = after[j]
                    if u >= 0 and h + cost[j] > t[u]:
                        t[u] = h + cost[j]
                ways = sorted([a + b for a, b in zip(t, rest)] + [t[r[-1]] + cost[r[-1]] + ends[e][1] for e, r in rows.items()])
                total += (ways[-1] + 0.02 * sum(ways[-10:])) / w
                if tight:
                    back = list(rest)
                    for e, r in rows.items():
                        back[r[-1]] = max(back[r[-1]], cost[r[-1]] + ends[e][1])
                    for j in reversed(way):
                        back[j] = max([back[j], cost[j] + back[after[j]] if after[j] >= 0 else 0.0] + [out[j] + back[u] for u in users[j]])
                    hot.extend(j for j in free if t[j] + back[j] > ways[-1] - 0.05)
            return total

        free = [j for j in range(m) if q[win[j]] not in "RY" and not nodes[win[j]]["first"]]
        now, hot = score(), []
        keep = (now, {e: list(r) for e, r in rows.items()})
        for it in range(tries):
            if it % 25 == 0:
                del hot[:]
                score(True)
            pool = hot if hot and rnd() < 0.6 else free
            j = pool[int(rnd() * len(pool)) % len(pool)]
            r = rows[q[win[j]]]
            a = r.index(j)
            b = a + int(1.0 - 2.0 * math.log(rnd())) * (1 if rnd() < 0.5 else -1)
            if not 0 <= b < len(r) or nodes[win[r[b]]]["first"]:
                continue
            r.insert(b, r.pop(a))
            c = score()
            if c is not None and c < now - HEAT * (1.0 - it / tries) * math.log(rnd()):
                now = c
                if c < keep[0]:
                    keep = (c, {e: list(x) for e, x in rows.items()})
            else:
                r.insert(a, r.pop(b))
        for r in keep[1].values():
            for at, j in zip(sorted(spot[win[x]] for x in r), r):
                spot[win[j]] = at
        c = links(sorted(range(n), key=spot.get))
        return (forward(*c),) + c

    for lo, hi, tries in WINDOWS:
        end = best[0][1][0]
        c = polish(best, lo * end, hi * end, tries)
        if c[0][0] <= best[0][0]:
            best = c
    STATS["end"], STATS["best"] = best[0][1], best
    rank = {k: j for j, k in enumerate(best[0][3])}
    return sorted(range(n), key=lambda k: (best[0][2][0][k], rank[k]))


def rank_program(g, core, T, topo):
    rank = T.rank_of(core)
    if rank is None:
        return
    A, AF = AluOpType, ActivationFunctionType
    queues = {"V": g.vector, "S": g.scalar, "T": g.tensor, "G": g, "Y": g.sync}
    own = {"V": "sv", "S": "ss", "T": "st", "G": "sg"}
    parts, cur, seen, opened = {}, [-1], {}, {}

    nodes, acc = [], {}

    def R(name, c0, c1=None, step=1, p=(0, 128)):
        if name in COLS:
            c0 = COLS.index(name)
            name, c1 = "fc", c0 + 1
        elif c1 is None:
            c1 = c0 + 1
        return (T[name][p[0]:p[1], c0:c1:step] if step > 1 else T[name][p[0]:p[1], c0:c1], [(name, c0, c1) + tuple(p)], -((c0 - c1) // step))

    def C(name):
        return R(name, 0)

    def IND(win, off):
        return (win[0].indirect(off[0]), win[1] + off[1], 16 * off[2])

    def clash(a, reg, w):
        return a[0] < reg[2] and reg[1] < a[1] and a[4] < reg[4] and reg[3] < a[5] and (w or a[2])

    bank = {n: [None, [], []] for n in PSUM}

    def node(q, fns, ins, outs, cost, sem=None, inc=1, preds=(), lat=0.0, soft=()):
        k, ps = len(nodes), set(preds)
        early = []
        for regs in parts.get(k, ()):
            early.append({a[3] for reg in regs for a in acc.get(reg[0], ()) if clash(a, reg, False)})
        before = {a[3] for reg in outs for a in acc.get(reg[0], ()) if clash(a, reg, True)}
        for name in {reg[0] for reg in ins + outs if reg[0] in bank}:
            b = bank[name]
            if b[0] != q:
                b[:] = [q, [], b[1]]
            b[1].append(k)
            before |= set(b[2])
        ps |= before | {a[3] for reg in ins for a in acc.get(reg[0], ()) if clash(a, reg, False)}
        for regs, w in ((ins, False), (outs, True)):
            for name, c0, c1, p0, p1 in regs:
                lst = acc.setdefault(name, [])
                if w:
                    lst[:] = [a for a in lst if not (c0 <= a[0] and a[1] <= c1 and p0 <= a[4] and a[5] <= p1)]
                lst.append((c0, c1, w, k, p0, p1))
        name = (outs[0][0] if outs else "-").rstrip("01")
        name = "pd" if name in PD else name
        seen[(cur[0], q, name)] = seen.get((cur[0], q, name), 0) + 1
        nodes.append({"q": q, "fns": fns, "cost": cost, "sem": sem or own[q], "inc": inc, "ps": sorted(ps | set(soft)), "soft": set(soft) - ps, "early": early, "before": before,
                      "lat": lat, "alone": False, "first": False, "step": cur[0], "kind": name + str(seen[(cur[0], q, name)])})
        return k

    def vcost(out, in_, *more):
        if len(in_[1]) > 1:
            return (0.05, 0, in_[2], 0)
        two = all(SCRATCH[x[1][0][0]][2] in (BF, F16, "uint16") for x in (out, in_) + more)
        return (0.0, max(64, out[2] * (0.5 if two else 1)), 0, 0)

    def scal(x, ins):
        if isinstance(x, tuple):
            ins += x[1]
            return x[0]
        return x

    def copy(out, in_):
        node("V", [lambda: g.vector.tensor_copy(out[0], in_[0])], in_[1], out[1], vcost(out, in_))

    def ts(out, in0, s1, s2, op0, op1=None):
        ins = list(in0[1])
        s1, s2 = scal(s1, ins), scal(s2, ins)
        if op1 is None:
            node("V", [lambda: g.vector.tensor_scalar(out[0], in0[0], s1, None, op0)], ins, out[1], vcost(out, in0))
        else:
            node("V", [lambda: g.vector.tensor_scalar(out[0], in0[0], s1, s2, op0, op1)], ins, out[1], vcost(out, in0))

    def tt(out, in0, in1, op):
        ps = any(x[1][0][0] in PSUM for x in (in0, in1))
        node("V", [lambda: g.vector.tensor_tensor(out[0], in0[0], in1[0], op)], in0[1] + in1[1], out[1],
             vcost(out, in0) if len(in0[1]) > 1 else (0.0, max(64, out[2] * (1 if ps else 2)), 0, 0))

    def scan(out, d0, d1, init, op0, op1):
        node("V", [lambda: g.vector.tensor_tensor_scan(out[0], d0[0], d1[0], init, op0, op1)], d0[1] + d1[1], out[1], vcost(out, d0, d1))

    def fill(out, c):
        node("V", [lambda: g.vector.memset(out[0], c)], [], out[1], vcost(out, out))

    def act(out, in_, func, bias=None, scale=None):
        kw, ins = {}, list(in_[1])
        if bias is not None:
            kw["bias"] = scal(bias, ins)
        if scale is not None:
            kw["scale"] = scal(scale, ins)
        node("S", [lambda: g.scalar.activation(out[0], in_[0], func, **kw)], ins, out[1],
             (0.065, 0, in_[2], 0) if len(in_[1]) > 1 else (0.04, max(64, out[2]), 0, 0))

    def move(e, out, in_, scale=None):
        if e == "S":
            act(out, in_, AF.Copy, scale=scale)
        elif scale is not None:
            ts(out, in_, scale, None, A.mult)
        else:
            copy(out, in_)

    def group(out, pairs, cut=()):
        for j0, j1 in zip((0,) + cut, cut + (len(pairs),)):
            fns, ins, cost = [], [], 0.0
            for j in range(j0, j1):
                l, r_ = pairs[j]
                parts.setdefault(len(nodes), []).append(l[1] + r_[1])
                fns.append(lambda l=l, r_=r_, j=j: g.tensor.matmul(out[0], l[0], r_[0], j == 0, j == len(pairs) - 1))
                ins += [x for x in l[1] + r_[1] if x not in ins]
                cost += max(64, out[2]) * (4 if SCRATCH[l[1][0][0]][2] == F32 else 1)
            name = out[1][0][0]
            k = node("T", fns, ins, out[1], (0.0, cost, 0, 0), preds=opened.get(name, ()))
            opened[name] = [k] if cut else []
            if j0:
                nodes[k]["before"].discard(k - 1)
                nodes[k - 1]["lat"] = "g"

    loads = []

    def load(q, pairs, lat):
        outs = [x for o, _ in pairs for x in o[1]]
        loads.append(node(q, [lambda o=o, i=i: queues[q].dma_start(o[0], i) for o, i in pairs], [], outs, (0.06 * len(pairs), 0, 0, 0),
                          sem="l%d" % len(loads), inc=16, lat=lat))
        nodes[-1]["first"] = True

    def spread(pairs, sem):
        node("Y", [lambda o=o, i=i: g.sync.dma_start(o[0], i[0]) for o, i in pairs], [x for _, i in pairs for x in i[1]],
             [x for o, _ in pairs for x in o[1]], (0.06 * len(pairs), 0, 0, 0), sem=sem, inc=16, lat="d")

    def store(out, in_, after=()):
        node("Y", [lambda: g.sync.dma_start(out, in_[0])], in_[1], [], (0.06, 0, 0, 0), sem="out", inc=16, lat="d", preds=after)

    def iota(out, pattern, base, cm=0):
        node("G", [lambda: g.iota(out[0], pattern, base, cm, allow_small_or_imprecise_dtypes=True)], [], out[1], (0.13, 2 * out[2], 0, 0))

    def gfill(out, c):
        iota(out, [[0, out[2]]], int(c))

    LO, HI = (0, 64), (64, 128)
    HALF = (LO, HI)

    def to_half(name, h):
        return R(name, 64 - 64 * h, 192 - 64 * h)

    load("S", [(R("rowi", 0, 128, p=(j, j + 1)), x[:, 0:1]) for j, x in enumerate((T.th, T.wt, T.tau))], 2.0)
    load("Y", [(R("kdn", 0, 256), T.kd[:, 0:U // 2])], 2.2)
    load("Y", [(R("kdn", 256, 512), T.kd[:, U // 2:U])], 2.7)
    load("Y", [(R("xb0", S // 2, S, p=p), T.x0[0:64, S // 2:S]) for p in HALF], 3.5)
    load("Y", [(R("xb0", 0, S // 2, p=p), T.x0[0:64, 0:S // 2]) for p in HALF], 4.4)
    load("Y", [(R("xb1", 0, S, p=p), T.x0[64:128, :]) for p in HALF], 6.0)

    ib = R("ipad", 0, 128)
    fill(R("onesb", 0, 512), 1.0)
    node("G", [lambda: g.iota(T.pix[:, 0:1], [[0, 1]], 0, 1)], [], C("pix")[1], (0.15, 0, 0, 0))
    iota(R("jx", 0, 256), [[1, 256]], 0)
    iota(R("jd", 0, 128), [[1, 8], [0, 16]], 0)
    iota(R("c16", 0, 8), [[16, 8]], 0)
    iota(R("jm", 0, 128), [[0, 8], [1, 16]], 0)
    copy(C("pixf"), C("pix"))
    for j, (fl, c, op) in enumerate((("prf", 15, A.bitwise_and), ("pdf", 4, A.arith_shift_right), ("etaf", 6, A.arith_shift_right),
                                     ("p4f", 8, A.bitwise_and), ("p6f", 63, A.bitwise_and), ("plf", 48, A.bitwise_and))):
        ts(R("pi", j), C("pix"), c, None, op)
        copy(C(fl), R("pi", j))
    ts(ib, R("jx", 0, 128), C("pixf"), None, A.is_equal)
    ts(C("sg"), C("etaf"), 2.0, -1.0, A.mult, A.add)
    ts(C("ns"), C("etaf"), -2.0, 1.0, A.mult, A.add)
    ts(C("lof"), C("etaf"), -1.0, 1.0, A.mult, A.add)
    scan(R("io", 0, 512), R("onesb", 0, 512), R("onesb", 0, 512), -1.0, A.mult, A.add)
    ts(R("nbias", 0, 8), R("c16", 0, 8), 32.0, -SH, A.mult, A.add)
    ts(R("nbias", 0, 8), R("nbias", 0, 8), C("sg"), None, A.mult)
    for b, name in NAMES.items():
        act(R(name, 0, 512), R("io", 0, 512), AF.Identity, bias=R("nbias", b), scale=C("sg"))
    copy(R("sel", 0, 128), ib)
    for w in (128, 256, 512):
        copy(R("sel", w, 2 * w), R("sel", 0, w))
    copy(R("i3", 0, 3, p=(0, 3)), R("ipad", 0, 3, p=(0, 3)))
    for s in range(2):
        for h in range(2):
            ts(R("rowf", 128 * s + 64 * h, 128 * s + 64 * h + 64, p=(0, 3)), R("rowi", 64 * s, 64 * s + 64, p=(0, 3)), -2048.0, None, A.add)
        group(R(BN, 3 * s, 3 * s + 3), [(R("rowf", 128 * s, 128 * s + 128, p=(0, 3)), R("i3", 0, 3, p=(0, 3)))])
    ts(R("rep", 0, 6), R(BN, 0, 6), 2048.0, None, A.add)
    th = [R("rep", 0), R("rep", 3)]
    ts(R("g2", 0, 128), R("jd", 0, 128), C("pdf"), None, A.is_equal)
    ts(R("far", 0, 32), R("jm", 0, 32), C("prf"), -2097152.0, A.not_equal, A.mult)
    ts(R("rz", 0, H), R("jm", 0, 128), 0.0, None, A.not_equal)
    ts(C("zc"), C("etaf"), 128.0, C("prf"), A.mult, A.add)
    ts(R("ich", 0, 8), R("c16", 0, 8), C("zc"), None, A.add)
    iota(R("cu", 0, 8), [[64, 2], [128, 2], [32, 2]], 0)
    ts(C("tl"), C("prf"), 2.0, C("etaf"), A.mult, A.add)
    ts(R("uc", 0, 8), R("cu", 0, 8), C("tl"), 613.0, A.add, A.mult)
    iota(R("j64", 0, 128), [[0, 2], [1, 64]], 0)
    ts(C("te"), C("etaf"), 8.0, C("p6f"), A.mult, A.add)
    ts(C("te"), C("te"), C("p4f"), None, A.subtract)
    for L in range(2):
        ts(C("cs"), C("p4f"), 8.0 * L, None, A.is_equal)
        ts(R("lay", H * L, H * L + H), R("j64", 0, 128), C("te"), C("cs"), A.is_equal, A.mult)

    for j in range(2):
        ts(R("kdh", 256 * j, 256 * j + 256), R("kdn", 256 * j, 256 * j + 256), -2048.0, None, A.add)
    for j in range(8):
        b = ("pd0", "pd1", BN)[j % 3]
        for e in range(2):
            group(R(b, 256 * e, 256 * e + 256), [(R("sel", (2 * j + e) % 8, 1024, 8), R("kdh", 256 * (j // 4), 256 * (j // 4) + 256))])
        move(CPE[j], R("kdw", 512 * j, 512 * j + 512), R(b, 0, 512))

    def lists(s, t, src, c0, far):
        B, z = S + G * t, str(s)
        for j in range(2):
            for h in range(2):
                a, b = 128 + 64 * j + 32 * h, c0 + far * h + 64 * j
                group(R(BX, a, a + 32), [(ib, R("far", 0, 32))]
                      + [(R("lv" + z, 192 * h + 64 - 64 * e, 192 * h + 192 - 64 * e), R(src, b + e, b + 64, 2)) for e in range(2)])
        scan(R("yf" + z, 0, H), R("rz", 0, H), R(BX, 128, 256), 0.0, A.mult, A.max)
        tt(R("ui" + z, 0, 8), R("yf" + z, 15, H, 16), R("uc", 0, 8), A.add)
        ts(R("uj" + z, 0, 8), R("ui" + z, 0, 8), 4095, None, A.bitwise_and)
        copy(R("uo" + z, 0, 8), R("uj" + z, 0, 8))
        copy(R("ek" + z, 0, H), IND(R("kdw", 0, U), R("uo" + z, 0, 8)))
        for L in range(2):
            group(R(BL, NP + H * L, NP + H * L + H), [(R("lay", H * L, H * L + H), R("ek" + z, 0, H))])
        for L in range(2):
            ts(R("el" + z, H * L, H * L + H), R(BL, NP + H * L, NP + H * L + H), B / 4096.0, B / 2.0 - 0.484375, A.mult, A.add)

    iota(R("jq", 0, 192), [[16, 12], [0, 16]], -64)
    for h in range(2):
        ts(R("gq", 192 * h, 192 * h + 192), R("jq", 0, 192), C("plf"), C(("lof", "etaf")[h]), A.is_equal, A.mult)
    for s in range(2):
        ts(R("lv%d" % s, 0, 384), R("gq", 0, 384), R("rep", 3 * s + 1), None, A.mult)
        lists(s, 0, "xb%d" % s, S - G, H)
    for s in range(2):
        for b, name in NAMES.items():
            c0, nt = 512 * b, "xv1"
            mask = R(nt, 2048 * s + c0, 2048 * s + c0 + 512)
            ts(mask, R("xb%d" % s, c0, c0 + 512), th[s], -8192.0, A.is_lt, A.mult)
            if s:
                act(R("kt1", c0, c0 + 512), R("io", 0, 512), AF.Identity, bias=R("nbias", b), scale=C("sg"))
            else:
                tt(R("kt0", c0, c0 + 512), R(name, 0, 512), mask, A.add)
    node("G", [lambda: g.dma_start(T.kt1[:, 0:S], T.xv1[:, S:2 * S], accum_op=A.add)], R("xv1", S, 2 * S)[1] + R("kt1", 0, S)[1], R("kt1", 0, S)[1],
         (1.0, 0, 0, 0), sem="ga", inc=16, lat=7.0)
    for per in (8, 16):
        iota(R("rn%d" % per, 0, RW), [[0, RW // per], [32767, per]], -2048)
    for name in ("if", "ih"):
        copy(R(name, 0, 128), ib)
    ts(R("bigh", 0, 128), ib, -64.0, None, A.mult)
    iota(R("cbig", 0, 256), [[8192, 2], [0, 128]], -131072)
    ts(R("rp", 0, 128), R("j64", 0, 128), C("p6f"), None, A.is_equal)
    ts(C("tl"), C("p6f"), 64.0, None, A.add)
    ts(R("rz3", 0, 192), R("jx", 0, 192), C("tl"), None, A.is_equal)
    ts(R("hx", 0, 192), R("rz3", 0, 192), C("ns"), 1023.0 / 2048.0, A.mult, A.mult)
    ts(R("nl", 0, 192), R("rz3", 0, 192), C("etaf"), -1.0, A.is_gt, A.mult)
    ts(C("tl"), C("plf"), 78.0, C("etaf"), A.add, A.add)
    ts(R("l1", 0, 208), R("jx", 0, 208), C("tl"), None, A.is_equal)
    for h, p in enumerate(HALF):
        iota(R("bi", 0, RO * H, p=p), [[G, RO], [1, H]], S + H * h - int(SH))
        nodes[-1]["alone"] = True
    for name in ("nt0", "nb0"):
        c0 = COLS.index(name)
        act(R("fc", c0, c0 + 2), R("rep", 2, 6, 3), AF.Copy, scale=-8192.0)
    for s in range(2):
        gfill(R("nq%d" % s, 0, 64), 0)
        act(R("ng2", 128 * s, 128 * s + 128), R("g2", 0, 128), AF.Copy, scale=-1.0)
    ts(C("cm"), C("pixf"), 2.0, 256.0, A.mult, A.add)
    ts(R("wa", 0, 128), R("jm", 0, 128), C("prf"), None, A.is_lt)
    ts(R("wb", 0, 128), R("jm", 0, 128), C("prf"), C("cm"), A.is_equal, A.mult)
    gfill(R("ow", 0, 128), 1)
    tt(R("ow", 128, 256), R("wa", 0, 128), R("wb", 0, 128), A.add)
    ts(R("nbef", 0, 8), R("jd", 0, 128, 16), C("pdf"), -1.0, A.is_ge, A.mult)
    gfill(R("none8", 0, 8), -1)
    iota(R("mnm", 0, 512), [[G, RO], [1, 128]], S + NP)
    for k in range(2 * RO):
        gfill(R("mw", 768 * k, 768 * k + CAP), 0)
    for t in range(RO):
        store(T.ya[:, G * t + NP:G * t + G], R("mnm", 128 * t, 128 * t + 128))
    ts(C("cs"), C("sg"), -SH, None, A.mult)
    mc = [R("pc", 0, 128), R("pc", 128, 256), R(BM, 0, 128)]
    act(R("pc", 0, 256), R("mnm", 0, 256), AF.Identity, bias=C("cs"), scale=C("sg"))
    act(mc[2], R("mnm", 256, 384), AF.Identity, bias=C("cs"), scale=C("sg"))
    for h in range(2):
        ts(R("rph", H * h, H * h + H), R("rp", 0, H), C(("lof", "etaf")[h]), None, A.mult)
        ts(R("rps", H * h, H * h + 64), R("rph", H * h, H * h + 64), -1.0, None, A.mult)
        copy(R("rps", H * h + 64, H * h + H), R("rph", H * h + 64, H * h + H))

    def lanes(a, t):
        to = [T.cores[(a + 1 + (FO * t + f) % (N - 1)) % N] for f in range(FO)]
        may = [topo.engines(T.cores[a], x) for x in to]
        both = [e for e in may[0] if e in may[1]]
        if t and len(may[0]) != len(may[1]):
            use = [[e for e in x if e not in both] or both for x in may]
        else:
            use = [both[:len(both) // 2], both[len(both) // 2:]]
        return (to[0], use[0]), (to[1], use[1]), len(use[0]) + len(use[1])

    def send(s, t):
        trs, k = [], 2 * t + s
        for f, (to, use) in enumerate(lanes(rank, t)[:2]):
            rid, pid, _ = topo.addr(to)
            trs.append(RemoteDMATransfer(dst_ids=[DstId(rid=rid, pnc=pid)], dma_engine_mask=sum(1 << e for e in use), remote_sem=T.sem["ma%d" % k],
                                         srcs=[T.mw[:, 768 * k:768 * k + CAP]], dsts=[T.rx[:, H * k + CAP * f:H * k + CAP * f + CAP]]))
        g.remote_dma_fused(trs, local_sem=T.sem.rl)

    pieces = [0]

    def step(s, t):
        B, Y, z, k = S + G * t, G * t, str(s), 2 * t + s
        last = t == RO - 1
        cur[0] = k
        xb, kt = "xb" + z, "kt" + z
        rows = slice(64 * s, 64 * s + 64)
        for n0, n1 in NCH[k]:
            f0, f1 = 8 * n0, 8 * n1
            kids = [IND(R(kt, 0, B), R("el" + z, H * L + n0 // 2, H * L + n1 // 2)) for L in range(2)]
            ka, kb = R("ka" + z, f0, f1), R("kb" + z, f0, f1)
            w = (n1 - n0) // KA[n0 // 64]
            for a in range(n0, n1, w):
                act(R("ka" + z, 8 * a, 8 * (a + w)), IND(R(kt, 0, B), R("el" + z, a // 2, (a + w) // 2)), AF.Copy)
            tt(kb, kids[1], ka, A.max)
            scan(R("ks" + z, f0, f1), R("rn8", 0, f1 - f0), kb, 0.0, A.min, A.max)
            m, z0, c = R("ks" + z, f0 + 7, f1, 8), R("z" + z, n0, n1), R(BN, n0, n1)
            if ZT[n0 // 64] == "T":
                group(c, [(ib, R("cbig", H, H + n1 - n0)), (R("if", 0, 128), R("ka" + z, f0, f1, 8)), (R("bigh", 0, 128), m)], (2,))
            else:
                ts(z0, R("ka" + z, f0, f1, 8), 8192.0, None, A.add)
                group(c, [(ib, R("cbig", 0, n1 - n0)), (R("ih", 0, 128), z0), (R("bigh", 0, 128), m)], (2,))
            tt(R("lh" + z, n0, n1), c, m, A.max)
            ts(R("hl" + z, n0, n1), R("lh" + z, n0, n1), C("sg"), SH, A.mult, A.add)
        n0, done, tiles = 0, 0, list(AB[k])
        for w, e in VP[k]:
            n1 = n0 + w
            move(e, R("xv" + z, 16 * n0, 16 * n1), IND(R(xb, 0, B), R("hl" + z, n0, n1)), C("ns"))
            for a in range(n0, n1, RW // 16):
                b = min(n1, a + RW // 16)
                scan(R("ms" + z, 16 * a, 16 * b), R("rn16", 0, 16 * (b - a)), R("xv" + z, 16 * a, 16 * b), 0.0, A.min, A.max)
            while tiles and done + tiles[0] <= n1:
                b = done + tiles.pop(0)
                d = R(PD[pieces[0] % len(PD)], 0, 8 * (b - done))
                pieces[0] += 1
                group(d, [(to_half("rz3", e_), R("xv" + z, 16 * done + e_, 16 * b, 2)) for e_ in range(2)], (1,) if b - done > 32 else ())
                act(R("ad" + z, 8 * done, 8 * b), d, AF.Abs)
                done = b
                if done % H == 0:
                    j = done // H - 1
                    group(R(BD, 64 * j, 64 * j + 64),
                          [(R("l1", 78 - 64 * h - 2 * p2, 206 - 64 * h - 2 * p2), R("ad" + z, 512 * (2 * j + h) + p2, 512 * (2 * j + h + 1), 8))
                           for h in ((1, 0) if j and VP[k][1][1] == "S" else (0, 1)) for p2 in range(8)], (8,))
            n0 = n1
        r = R("r" + z, 0, H)
        act(r, R(BD, 0, H), AF.Relu, bias=C("nb" + z), scale=8192.0)
        xn = R("xn", H * k, H * k + H)
        for j in range(2):
            group(R(BX, 64 * j, 64 * j + 64), [(to_half("hx", h), R("ms" + z, 1024 * (2 * j + h) + 15, 1024 * (2 * j + h + 1), 16)) for h in range(2)])
        ts(xn, R(BX, 0, H), MAGIC, -MAGIC, A.add, A.add)
        ahead = []
        if not last:
            spread([(R(xb, B + H * h, B + H * h + H, p=p), R("xn", H * k, H * k + H, p=HALF[h])) for h in range(2) for p in HALF], "sx%d" % k)
            ahead.append(len(nodes) - 1)
            lists(s, t + 1, "xn", H * k, 0)
        ab, landed = R("ab", H * k, H * k + H), []

        def names():
            for j in range(2):
                group(R(BP, NP + 64 * j, NP + 64 * j + 64), [(to_half("nl", h), R("lh" + z, 64 * (2 * j + h), 64 * (2 * j + h + 1))) for h in range(2)]
                      + [(ib, R("r" + z, 64 * j, 64 * j + 64))])
            tt(ab, R(BP, NP, NP + H), R("bi", H * t, H * t + H), A.min)
            for k0, k1 in OUT.get(k, ()):
                ts(R("an", H * k0, H * k1), R("ab", H * k0, H * k1), SH, None, A.add)
                for j in range(k0, k1):
                    for h in range(2):
                        c0 = G * (j // 2) + H * h
                        store(T.ya[64 * (j % 2):64 * (j % 2) + 64, c0:c0 + H], R("an", H * j, H * j + H, p=HALF[h]))
        if last:
            for h in range(2):
                store(T.yx[rows, Y + H * h:Y + H * h + H], R("xn", H * k, H * k + H, p=HALF[h]))
        if k == LAST:
            names()
        group(R(BM, 128, 384), [(ib, R("ow", 0, 256)), (r, R("ng2", 0, 256))], (1,))
        if k < LAST:
            act(R("nq" + z, 64, 320), R(BM, 128, 384), AF.Relu)
        else:
            ts(R("nq" + z, 64, 320), R(BM, 128, 384), 0.0, None, A.max)
        group(R(BM, 384, 392), [(ib, R("ich", 0, 8)), (R("nq" + z, 0, 128), R("none8", 0, 8)), (R("nq" + z, 64, 192), R("nbef", 0, 8)),
                                (R("nq" + z, 192, 320), R("g2", 0, 128, 16))])
        copy(R("off" + z, 0, 8), R(BM, 384, 392))
        dst = IND(R("mw", 768 * k, 768 * k + 768), R("off" + z, 0, 8))
        node("V", [lambda: g.vector.tensor_copy(dst[0], xn[0])], xn[1] + dst[1][1:], dst[1][:1], (0.05, 0, 0, H))
        n = node("G", [lambda: send(s, t)], R("mw", 768 * k, 768 * k + CAP)[1], [], (0.3, 0, 0, 0), sem="rl", inc=lanes(rank, t)[2], soft=ahead)
        node("R", [None], [], R("rx", H * k, H * k + H)[1], (0.0, 0, 0, 0), sem="ma%d" % k, preds=[n], lat="m",
             inc=sum(len(lanes((rank - 1 - (FO * t + f) % (N - 1)) % N, t)[f][1]) for f in range(FO)))
        if k < LAST:
            names()
        if not last:
            ts(R("n8" + z, 0, H), xn, th[s], -8192.0, A.is_lt, A.mult)
            for h in range(2):
                group(R("pc", NP + H * h, NP + H * h + H), [(R("rph", H * h, H * h + H), R("n8" + z, 0, H)), (R("rps", H * h, H * h + H), ab)])
            move(KE, R(kt, B, B + NP), R("pc", NP, 2 * NP))
        mail = R(BM, 384, 512)
        if last:
            for j in range(2 * s):
                group(mail, [(R("rp", 0, 128), R("rx", H * (k - 1 + j), H * (k + j)))])
                copy(R("xb%d" % j, B + NP, B + G), mail)
                store(T.yx[64 * j:64 * j + 64, Y + NP:Y + G], R("xb%d" % j, B + NP, B + G, p=LO))
            return
        group(mail, [(R("rp", 0, 128), R("rx", H * k, H * k + H))])
        ts(R("nm" + z, 0, 128), mail, th[s], 8192.0, A.is_lt, A.mult)
        tt(R(kt, B + NP, B + G), mc[t], R("nm" + z, 0, 128), A.subtract)
        copy(R(xb, B + NP, B + G), mail)
        if s:
            group(R(BM, 376, 384), [(R("onesb", 0, 128), R("nq%d" % j, 64, 192, 16)) for j in range(2)])
            node("V", [lambda: g.vector.tensor_reduce(C("cs")[0], T[BM][:, 376:384], AxisListType.X, A.add)],
                 R(BM, 376, 384)[1], C("cs")[1], (0.0, 64, 0, 0))
            ts(C("cia"), C("cs"), -1.0, 2048.0, A.mult, A.add)
            ts(C("cja"), C("cia"), 15, None, A.bitwise_and)
            for j in range(2):
                ts(C("nb%d" % j), C("cja"), -8192.0, C("nt%d" % j), A.mult, A.add)
        store(T.yx[rows, Y:Y + G], R(xb, B, B + G, p=LO))

    for t in range(RO):
        for s in range(2):
            step(s, t)

    if "order" not in STATS:
        STATS["nodes"], STATS["order"] = nodes, schedule(nodes)
    order = loads + [k for k in STATS["order"] if k not in loads]

    count, waited, snap, token, made = {}, {}, {}, {}, []
    known = {q: {} for q in "VSTGYR"}
    for k in order:
        nd = nodes[k]
        q, sem = nd["q"], nd["sem"]
        kn = known[q]
        for j, fn in enumerate(nd["fns"]):
            need, ps = {}, set() if j else set(nd["ps"]) - nd["soft"]
            if nd["early"]:
                ps = nd["early"][j] if j else nd["before"] | nd["early"][0]
            if q == "G":
                if made and (nd["alone"] or nodes[made[-1]]["alone"]):
                    ps = ps | {made[-1]}
                if sem == "sg":
                    made.append(k)
            for p in ps:
                s, n = token[p]
                if q != "R" and kn.get(s, 0) < n:
                    need[s] = max(need.get(s, 0), n)
            for s, n in list(need.items()):
                if any(o != s and snap[(o, m)].get(s, 0) >= n for o, m in need.items()):
                    del need[s]
            for s, n in need.items():
                queues[q].wait_ge(T.sem[s], n)
                waited[s] = max(waited.get(s, 0), n)
                for o, m in snap[(s, n)].items():
                    kn[o] = max(kn.get(o, 0), m)
            count[sem] = count.get(sem, 0) + nd["inc"]
            if fn is not None:
                call = fn()
                if sem != "rl":
                    call.then_inc(T.sem[sem], nd["inc"])
        n = count[sem]
        token[k] = (sem, n)
        snap[(sem, n)] = dict(kn) if q != "R" else {}
        snap[(sem, n)][sem] = n
    for s, n in count.items():
        if waited.get(s, 0) < n:
            (g if s == "rl" else g.sync).wait_ge(T.sem[s], n)
